import numpy as np
import ml_dtypes


def mxq(x, axis, fmt="e4m3"):
    dtype, down = {"e4m3": (ml_dtypes.float8_e4m3fn, 7), "e5m2": (ml_dtypes.float8_e5m2, 14)}[fmt]
    v = np.moveaxis(np.asarray(x, np.float32).astype(ml_dtypes.bfloat16).astype(np.float64), axis, -1)
    blocks = v.reshape(v.shape[:-1] + (-1, 32))
    amax = np.abs(blocks).max(-1, keepdims=True)
    byte = np.maximum(np.where(amax > 0, np.frexp(amax)[1] - 1 + 127, 0) - down, 1)
    scale = np.exp2(byte - 127.0)
    codes = (blocks / scale).astype(np.float32).astype(dtype).astype(np.float64)
    return np.moveaxis((codes * scale).reshape(v.shape), -1, axis)


WIDE = False


def mx_kscale(k):
    if not WIDE:
        return np.ones(k)
    levels = np.array([10, -10, 5, -5, 0])
    if k % 512:
        return np.exp2(np.random.permutation(np.resize(levels, k // 32))).repeat(32)
    a = np.empty((k // 512, 16))
    for p in range(k // 512):
        a[p, :8] = np.random.permutation(np.resize(levels, 8))
        for g in range(8):
            far = levels[np.abs(levels - a[p, g]) >= 10]
            a[p, g + 8] = far[np.random.randint(len(far))]
    return np.exp2(a.ravel()).repeat(32)


def f64(x):
    return np.asarray(x).astype(np.float64)


def striped(idx):
    return np.tile(idx.reshape(-1, 16).T, (8, 1)).astype(np.uint16)


def unstriped(offs):
    return offs[:16].T.reshape(-1).astype(np.int64)


E2M1 = np.array([0.0, 0.5, 1.0, 1.5, 2.0, 3.0, 4.0, 6.0, -0.0, -0.5, -1.0, -1.5, -2.0, -3.0, -4.0, -6.0])


def pack_weight(w, fmt):
    k, n = w.shape
    w = f64(np.asarray(w, np.float32).astype(ml_dtypes.bfloat16)).reshape(k // 32, 32, n)
    amax = np.abs(w).max(1)
    if fmt == "e4m3":
        byte = np.frexp(amax)[1] - 1 + 127 - 7
    else:
        mant, ex = np.frexp(amax / 6.0)
        byte = np.where(mant > 0.5, ex, ex - 1) + 127
    byte = np.clip(np.where(amax > 0, byte, 1), 1, 254)
    scaled = (w * np.exp2(127.0 - byte)[:, None, :]).reshape(k, n).astype(np.float32)
    by_word = np.ascontiguousarray(scaled.reshape(k // 512, 128, 4, n).transpose(0, 1, 3, 2))
    if fmt == "e4m3":
        words = by_word.astype(ml_dtypes.float8_e4m3fn).view(np.uint8)
    else:
        c = by_word.astype(ml_dtypes.float4_e2m1fn).view(np.uint8) & 0xF
        words = (c[..., 0::2] | (c[..., 1::2] << 4)).reshape(k // 512, 128, 2 * n)
    return np.ascontiguousarray(words), np.ascontiguousarray(byte.astype(np.uint8).reshape(k // 512, 16, n))


def unpack_weight(words, scales, fmt):
    g, _, n = scales.shape
    words = np.ascontiguousarray(words).reshape(g, 128, n, -1)
    if fmt == "e4m3":
        vals = words.view(ml_dtypes.float8_e4m3fn).astype(np.float64)
    else:
        nib = np.empty((g, 128, n, 4), np.uint8)
        nib[..., 0::2] = words & 0xF
        nib[..., 1::2] = words >> 4
        vals = E2M1[nib]
    vals = vals * np.repeat(np.exp2(scales.astype(np.float64) - 127.0), 8, axis=1)[..., None]
    return vals.transpose(0, 1, 3, 2).reshape(g * 512, n)


def gelu(v):
    return 0.5 * v * (1.0 + np.tanh(np.sqrt(2.0 / np.pi) * (v + 0.044715 * v**3)))


def striped8(idx):
    return np.concatenate([v.reshape(-1, 16).T for v in idx]).astype(np.uint16)


def unstriped8(offs):
    return np.stack([offs[16 * g:16 * g + 16].T.reshape(-1) for g in range(8)]).astype(np.int64)


def heads(xT, wgt, idx8):
    k = np.arange(xT.shape[0])
    return wgt[k // 4 % 128] * xT[k[:, None], idx8[k % 512 // 64]]


K, D, H, N, T, TU, S = 1024, 512, 1024, 512, 2048, 2048, 1024

def setup_inputs():
    n = np.random.standard_normal
    s = mx_kscale(K)[:, None]
    d = mx_kscale(D)[:, None]
    u = mx_kscale(H)[:, None]
    tab_words, tab_scales = pack_weight(n((D, TU)) * d, "e4m3")
    wg_words, wg_scales = pack_weight(n((D, H)) / np.sqrt(D) / d, "e2m1")
    wt_words, wt_scales = pack_weight(n((H, N)) / np.sqrt(H) / u, "e4m3")
    return {
        "tab_words": tab_words, "tab_scales": tab_scales,
        "offs": striped(np.random.permutation(TU)[:S]),
        "xT": (n((K, T)) * s).astype(np.float32),
        "wgt": np.repeat(np.random.uniform(0.5, 2.0, (8, S)), 16, axis=0).astype(np.float32),
        "offs2": striped8(np.stack([np.random.permutation(T)[:S] for _ in range(8)])),
        "wp": (n((K, H)) / np.sqrt(K) / s * u.T).astype(np.float32),
        "wg_words": wg_words, "wg_scales": wg_scales,
        "bg": (0.5 * n(H)).astype(np.float32),
        "wt_words": wt_words, "wt_scales": wt_scales,
        "bt": (0.5 * n(N)).astype(np.float32),
    }

def reference(tab_words, tab_scales, offs, xT, wgt, offs2, wp, wg_words, wg_scales, bg, wt_words, wt_scales, bt):
    v = unpack_weight(tab_words, tab_scales, "e4m3")[:, unstriped(offs)]
    wg = unpack_weight(wg_words, wg_scales, "e2m1")
    wt = unpack_weight(wt_words, wt_scales, "e4m3")
    xg = heads(f64(xT), f64(wgt), unstriped8(offs2))
    a = mxq(f64(wp), 0, "e4m3").T @ mxq(xg, 0, "e4m3")
    b = (wg.T @ v) + f64(bg)[:, None]
    h = a * (1.0 / (1.0 + np.exp(-b)))
    return (wt.T @ mxq(h, 0, "e4m3")) + f64(bt)[:, None]

@@ -1,0 +1,311 @@
+from contextlib import ExitStack
+
+import concourse.mybir as mybir
+
+K, D, H, N, T, S = 1024, 512, 1024, 512, 2048, 1024
+FLOPS = 2 * S * (K * H + D * H + H * N)
+
+F32 = mybir.dt.float32
+BF16 = mybir.dt.bfloat16
+I32 = mybir.dt.int32
+U32 = mybir.dt.uint32
+U16 = mybir.dt.uint16
+U8 = mybir.dt.uint8
+FP8X4 = mybir.dt.float8_e4m3fn_x4
+FP4X4 = mybir.dt.float4_e2m1fn_x4
+MULT = mybir.AluOpType.mult
+ACT = mybir.ActivationFunctionType
+
+P = 128
+PACK = 4
+KP = P * PACK
+BANK = 512
+JC = 128
+
+
+def tile_list_interest_user_gate_kernel(
+    tc, tab_words, tab_scales, offs, xT, wgt, offs2, wp, wg_words, wg_scales, bg, wt_words, wt_scales, bt, out
+):
+    nc = tc.nc
+    with ExitStack() as ctx:
+        lists = ctx.enter_context(tc.tile_pool(name="lists", bufs=1))
+        keep = ctx.enter_context(tc.tile_pool(name="keep", bufs=1))
+        stream = ctx.enter_context(tc.tile_pool(name="stream", bufs=7))
+        stage = ctx.enter_context(tc.tile_pool(name="stage", bufs=3))
+        psum = ctx.enter_context(tc.psum_pool(name="psum", bufs=4))
+
+        users = lists.tile([P, S // 16], U16, name="users")
+        clicks = lists.tile([P, S // 16], U16, name="clicks")
+
+        tab_w = keep.tile([P, T], U32, name="tab_w", align_bytes=64)
+        tab_s = keep.tile([P, T], U8, name="tab_s", align_bytes=64)
+        v_w = keep.tile([P, S], U32, name="v_w", align_bytes=64)
+        v_s = keep.tile([P, S], U8, name="v_s", align_bytes=64)
+        wg_w_raw = keep.tile([P, 2 * H], U8, name="wg_w_raw", align_bytes=64)
+        wg_s_raw = keep.tile([P, H], U8, name="wg_s_raw", align_bytes=64)
+        wg_w = keep.tile([P, 2 * H], U8, name="wg_w", align_bytes=64)
+        wg_s = keep.tile([P, H], U8, name="wg_s", align_bytes=64)
+        wt_s = keep.tile([P, 2, N], U8, name="wt_s", align_bytes=64)
+        wgt_sb = keep.tile([P, S], F32, name="wgt_sb", align_bytes=64)
+        bg_sb = keep.tile([P, 2, PACK], F32, name="bg_sb", align_bytes=64)
+        bt_sb = keep.tile([P, N // P], F32, name="bt_sb", align_bytes=64)
+        picked = [keep.tile([P, PACK, S], F32, name="picked%d" % a, align_bytes=64) for a in range(2)]
+        gate = [keep.tile([P, PACK, S], F32, name="gate%d" % h, align_bytes=64) for h in range(2)]
+        xg_w = [keep.tile([P, S], U32, name="xg_w%d" % a, align_bytes=64) for a in range(2)]
+        xg_s = [keep.tile([P, S], U8, name="xg_s%d" % a, align_bytes=64) for a in range(2)]
+        wp_w = [keep.tile([P, H], U32, name="wp_w%d" % a, align_bytes=64) for a in range(2)]
+        wp_s = [keep.tile([P, H], U8, name="wp_s%d" % a, align_bytes=64) for a in range(2)]
+        h_w = [keep.tile([P, S], U32, name="h_w%d" % h, align_bytes=64) for h in range(2)]
+        h_s = [keep.tile([P, S], U8, name="h_s%d" % h, align_bytes=64) for h in range(2)]
+
+        def load_scale_rows(plane, rows, quadrants, queue):
+            for q in quadrants:
+                queue.dma_start(out=plane[32 * q : 32 * q + 4].bitcast(I32), in_=rows[4 * q : 4 * q + 4].bitcast(I32))
+
+        planes = {}
+
+        def load_plane(a, t):
+            planes[a, t] = stream.tile([P, T], F32, name="plane", tag="stream", align_bytes=64)
+            rows = xT[KP * a : KP * (a + 1), :].rearrange("(p i) c -> p i c", i=PACK)
+            nc.sync.dma_start(out=planes[a, t][:], in_=rows[:, t, :])
+
+        wp_raw = {}
+
+        def load_wp(h, a):
+            wp_raw[h, a] = stream.tile([P, PACK, KP], F32, name="wp_raw", tag="stream", align_bytes=64)
+            rows = wp[KP * a : KP * (a + 1), KP * h : KP * (h + 1)].rearrange("(p i) c -> p i c", i=PACK)
+            nc.sync.dma_start(out=wp_raw[h, a][:], in_=rows)
+
+        def gather(a, t, lo, hi):
+            nc.vector.tensor_tensor(
+                picked[a][:, t, lo:hi], planes[a, t][:].indirect(clicks[:, lo // 16 : hi // 16]), wgt_sb[:, lo:hi], MULT
+            )
+
+        xg_bf = {}
+
+        def round_xg(a, lo, hi):
+            xg_bf[a, lo] = stage.tile([P, PACK * (hi - lo)], BF16, name="xg_bf", tag="xg_bf", align_bytes=64)
+            nc.scalar.copy(
+                out=xg_bf[a, lo][:].rearrange("p (c i t) -> p c t i", i=4, t=PACK),
+                in_=picked[a][:, :, lo:hi].rearrange("p t (c i) -> p c t i", i=4),
+            )
+
+        def quantize_xg(a, lo, hi):
+            nc.vector.quantize_mx(out=xg_w[a][:, lo:hi].bitcast(FP8X4), scales=xg_s[a][:, lo:hi], in_=xg_bf[a, lo][:])
+
+        wp_bf = {}
+
+        def round_wp(h, a, copy):
+            wp_bf[h, a] = stage.tile([P, PACK * KP], BF16, name="wp_bf", tag="wp_bf", align_bytes=64)
+            copy(
+                out=wp_bf[h, a][:].rearrange("p (t m i) -> p m i t", t=PACK, i=PACK),
+                in_=wp_raw[h, a][:].rearrange("p i (m t) -> p m i t", t=PACK),
+            )
+
+        def quantize_wp(h, a):
+            cols = slice(KP * h, KP * (h + 1))
+            nc.vector.quantize_mx(out=wp_w[a][:, cols].bitcast(FP8X4), scales=wp_s[a][:, cols], in_=wp_bf[h, a][:])
+
+        def make_gate(h, t, lo):
+            acc = psum.tile([P, BANK], F32, name="acc", tag="acc")
+            c0 = KP * h + P * t
+            nc.tensor.matmul_mx(
+                out=acc[:],
+                lhsT=wg_w[:, 2 * c0 : 2 * (c0 + P)].bitcast(FP4X4),
+                lhsT_scale=wg_s[:, c0 : c0 + P],
+                rhs=v_w[:, lo : lo + BANK].bitcast(FP8X4),
+                rhs_scale=v_s[:, lo : lo + BANK],
+                start=True,
+                stop=True,
+            )
+            nc.scalar.activation(
+                out=gate[h][:, t, lo : lo + BANK], in_=acc[:], func=ACT.Sigmoid, bias=bg_sb[:, h, t : t + 1]
+            )
+
+        h_bf = {}
+
+        def make_h(h, lo, hi):
+            h_bf[h, lo] = stage.tile([P, PACK * (hi - lo)], BF16, name="h_bf", tag="h_bf", bufs=4, align_bytes=64)
+            for j0 in range(lo, hi, JC):
+                acc = psum.tile([P, PACK, JC], F32, name="acc", tag="acc")
+                for t in range(PACK):
+                    c0 = KP * h + P * t
+                    for a in range(2):
+                        nc.tensor.matmul_mx(
+                            out=acc[:, t, :],
+                            lhsT=wp_w[a][:, c0 : c0 + P].bitcast(FP8X4),
+                            lhsT_scale=wp_s[a][:, c0 : c0 + P],
+                            rhs=xg_w[a][:, j0 : j0 + JC].bitcast(FP8X4),
+                            rhs_scale=xg_s[a][:, j0 : j0 + JC],
+                            start=(a == 0),
+                            stop=(a == 1),
+                        )
+                nc.vector.tensor_tensor(
+                    h_bf[h, lo][:, PACK * (j0 - lo) : PACK * (j0 - lo + JC)].rearrange("p (c i t) -> p c t i", i=4, t=PACK),
+                    acc[:].rearrange("p t (c i) -> p c t i", i=4),
+                    gate[h][:, :, j0 : j0 + JC].rearrange("p t (c i) -> p c t i", i=4),
+                    MULT,
+                )
+
+        def quantize_h(h, lo, hi):
+            nc.vector.quantize_mx(out=h_w[h][:, lo:hi].bitcast(FP8X4), scales=h_s[h][:, lo:hi], in_=h_bf[h, lo][:])
+
+        tower = {}
+
+        def tower_pass(h, lo, hi):
+            for m in range(N // P):
+                if h == 0:
+                    tower[lo, m] = psum.tile([P, hi - lo], F32, name="tower", tag="tower")
+                nc.tensor.matmul_mx(
+                    out=tower[lo, m][:],
+                    lhsT=wt_w[:, h, P * m : P * (m + 1)].bitcast(FP8X4),
+                    lhsT_scale=wt_s[:, h, P * m : P * (m + 1)],
+                    rhs=h_w[h][:, lo:hi].bitcast(FP8X4),
+                    rhs_scale=h_s[h][:, lo:hi],
+                    start=(h == 0),
+                    stop=(h == 1),
+                )
+
+        out_rows = out.rearrange("(m p) j -> p m j", p=P)
+
+        def tower_bank(lo, hi, m0, m1, on_vector):
+            acc = psum.tile([P, m1 - m0, hi - lo], F32, name="tower", tag="tower")
+            for m in range(m0, m1):
+                for h in range(2):
+                    nc.tensor.matmul_mx(
+                        out=acc[:, m - m0, :],
+                        lhsT=wt_w[:, h, P * m : P * (m + 1)].bitcast(FP8X4),
+                        lhsT_scale=wt_s[:, h, P * m : P * (m + 1)],
+                        rhs=h_w[h][:, lo:hi].bitcast(FP8X4),
+                        rhs_scale=h_s[h][:, lo:hi],
+                        start=(h == 0),
+                        stop=(h == 1),
+                    )
+            res = stage.tile([P, m1 - m0, hi - lo], F32, name="res", tag="res", bufs=6, align_bytes=64)
+            for m in range(m0, m1):
+                if on_vector:
+                    nc.vector.tensor_scalar_add(res[:, m - m0, :], acc[:, m - m0, :], bt_sb[:, m : m + 1])
+                else:
+                    nc.scalar.activation(out=res[:, m - m0, :], in_=acc[:, m - m0, :], func=ACT.Identity, bias=bt_sb[:, m : m + 1])
+            nc.sync.dma_start(out=out_rows[:, m0:m1, lo:hi], in_=res[:])
+
+        def store(lo, hi, on_vector):
+            for m in range(N // P):
+                res = stage.tile([P, hi - lo], F32, name="res", tag="res", bufs=6, align_bytes=64)
+                if m in on_vector:
+                    nc.vector.tensor_scalar_add(res[:], tower[lo, m][:], bt_sb[:, m : m + 1])
+                else:
+                    nc.scalar.activation(out=res[:], in_=tower[lo, m][:], func=ACT.Identity, bias=bt_sb[:, m : m + 1])
+                nc.sync.dma_start(out=out[P * m : P * (m + 1), lo:hi], in_=res[:])
+
+        warm = keep.tile([P, 2], F32, name="warm", align_bytes=64)
+        nc.vector.memset(tab_s[:].bitcast(I32), 0)
+        nc.gpsimd.memset(wg_s_raw[:].bitcast(I32), 0)
+        nc.gpsimd.memset(wt_s[:].bitcast(I32), 0)
+        nc.gpsimd.memset(warm[:, 0:1], 0.0)
+        nc.scalar.activation(out=warm[:, 1:2], in_=warm[:, 0:1], func=ACT.Sigmoid)
+        wt_rows = wt_scales.rearrange("a r n -> r a n")
+        nc.sync.dma_start(users[:], offs)
+        nc.sync.dma_start(out=wg_w_raw[:].bitcast(I32), in_=wg_words[0].bitcast(I32))
+        nc.sync.dma_start(clicks[:], offs2)
+        load_scale_rows(tab_s, tab_scales[0], range(4), nc.sync)
+        nc.sync.dma_start(out=tab_w[:].bitcast(I32), in_=tab_words[0].rearrange("p n t -> p (n t)").bitcast(I32))
+        load_scale_rows(wg_s_raw, wg_scales[0], range(4), nc.sync)
+        nc.sync.dma_start(out=wgt_sb[:], in_=wgt)
+        load_plane(0, 0)
+        nc.sync.dma_start(out=bg_sb[:], in_=bg.rearrange("(h p t) -> p h t", h=2, t=PACK))
+        load_plane(0, 1)
+        load_plane(0, 2)
+        load_scale_rows(wt_s, wt_rows, range(0, 2), nc.sync)
+        load_plane(0, 3)
+        load_scale_rows(wt_s, wt_rows, range(2, 4), nc.sync)
+        load_wp(0, 0)
+        load_plane(1, 0)
+        with nc.allow_non_contiguous_dma(reason="one bias value for each partition"):
+            nc.sync.dma_start(out=bt_sb[:], in_=bt.rearrange("(m p) -> p m", p=P))
+        load_plane(1, 1)
+        load_plane(1, 2)
+        load_wp(0, 1)
+        load_plane(1, 3)
+        load_wp(1, 0)
+        load_wp(1, 1)
+        wt_w = stream.tile([P, 2, N], U32, name="wt_w", tag="stream", align_bytes=64)
+        nc.sync.dma_start(out=wt_w[:].bitcast(I32), in_=wt_words.rearrange("a p n t -> p a (n t)").bitcast(I32))
+        nc.vector.tensor_copy(
+            out=wg_w[:].bitcast(U16).rearrange("p (h t m) -> p h m t", h=2, t=PACK),
+            in_=wg_w_raw[:].bitcast(U16).rearrange("p (h m t) -> p h m t", h=2, t=PACK),
+        )
+        nc.vector.tensor_copy(v_s[:], tab_s[:].indirect(users[:]))
+        nc.vector.tensor_copy(
+            out=wg_s[:].rearrange("p (h t m) -> p h m t", h=2, t=PACK),
+            in_=wg_s_raw[:].rearrange("p (h m t) -> p h m t", h=2, t=PACK),
+        )
+        nc.vector.tensor_copy(v_w[:, 0:512], tab_w[:].indirect(users[:, 0:32]))
+        nc.vector.tensor_copy(v_w[:, 512:1024], tab_w[:].indirect(users[:, 32:64]))
+        for t in range(PACK):
+            make_gate(0, t, 0)
+        for t in range(PACK):
+            make_gate(0, t, 512)
+        gather(0, 0, 0, 512)
+        gather(0, 0, 512, 1024)
+        gather(0, 1, 0, 512)
+        gather(0, 1, 512, 1024)
+        gather(0, 2, 0, 512)
+        gather(0, 2, 512, 1024)
+        gather(0, 3, 0, 512)
+        gather(0, 3, 512, 1024)
+        for t in range(PACK):
+            make_gate(1, t, 0)
+        for t in range(PACK):
+            make_gate(1, t, 512)
+        round_wp(0, 0, nc.scalar.copy)
+        round_xg(0, 0, 512)
+        round_xg(0, 512, 1024)
+        gather(1, 0, 0, 512)
+        gather(1, 0, 512, 1024)
+        quantize_wp(0, 0)
+        gather(1, 1, 0, 512)
+        quantize_xg(0, 0, 512)
+        gather(1, 1, 512, 1024)
+        gather(1, 2, 0, 512)
+        quantize_xg(0, 512, 1024)
+        gather(1, 2, 512, 1024)
+        round_wp(0, 1, nc.scalar.copy)
+        gather(1, 3, 0, 256)
+        gather(1, 3, 256, 512)
+        quantize_wp(0, 1)
+        gather(1, 3, 512, 1024)
+        round_xg(1, 0, 256)
+        round_xg(1, 256, 512)
+        round_wp(1, 0, nc.scalar.copy)
+        round_wp(1, 1, nc.scalar.copy)
+        round_xg(1, 512, 1024)
+        quantize_xg(1, 0, 256)
+        make_h(0, 0, 256)
+        quantize_xg(1, 256, 512)
+        make_h(0, 256, 512)
+        quantize_wp(1, 0)
+        quantize_h(0, 0, 256)
+        quantize_wp(1, 1)
+        quantize_h(0, 256, 512)
+        tower_pass(0, 0, 512)
+        make_h(1, 0, 512)
+        quantize_xg(1, 512, 1024)
+        make_h(0, 512, 768)
+        quantize_h(1, 0, 512)
+        tower_pass(1, 0, 512)
+        store(0, 512, ())
+        make_h(1, 512, 768)
+        quantize_h(0, 512, 768)
+        make_h(0, 768, 1024)
+        quantize_h(1, 512, 768)
+        tower_bank(512, 768, 0, 2, False)
+        tower_bank(512, 768, 2, 4, False)
+        make_h(1, 768, 896)
+        quantize_h(0, 768, 1024)
+        make_h(1, 896, 1024)
+        quantize_h(1, 768, 896)
+        tower_bank(768, 896, 0, 4, False)
+        quantize_h(1, 896, 1024)
+        tower_bank(896, 1024, 0, 2, False)
+        tower_bank(896, 1024, 2, 4, True)

@@ -45,11 +45,12 @@ def tile_list_interest_user_gate_kernel(
         wg_s_raw = keep.tile([P, H], U8, name="wg_s_raw", align_bytes=64)
         wg_w = keep.tile([P, 2 * H], U8, name="wg_w", align_bytes=64)
         wg_s = keep.tile([P, H], U8, name="wg_s", align_bytes=64)
-        wt_s = keep.tile([P, 2, N], U8, name="wt_s", align_bytes=64)
         wgt_sb = keep.tile([P, S], F32, name="wgt_sb", align_bytes=64)
-        bg_sb = keep.tile([P, 2, PACK], F32, name="bg_sb", align_bytes=64)
-        bt_sb = keep.tile([P, N // P], F32, name="bt_sb", align_bytes=64)
-        picked = [keep.tile([P, PACK, S], F32, name="picked%d" % a, align_bytes=64) for a in range(2)]
+        bg_sb = keep.tile([P, 2, 8], F32, name="bg_sb", align_bytes=64)
+        picked = {}
+        for a in range(2):
+            for s in range(2):
+                picked[a, s] = keep.tile([P, PACK, BANK], F32, name="picked", tag="picked%d%d" % (a, s), align_bytes=64)
         gate = [keep.tile([P, PACK, S], F32, name="gate%d" % h, align_bytes=64) for h in range(2)]
         xg_w = [keep.tile([P, S], U32, name="xg_w%d" % a, align_bytes=64) for a in range(2)]
         xg_s = [keep.tile([P, S], U8, name="xg_s%d" % a, align_bytes=64) for a in range(2)]
@@ -78,16 +79,16 @@ def tile_list_interest_user_gate_kernel(
 
         def gather(a, t, lo, hi):
             nc.vector.tensor_tensor(
-                picked[a][:, t, lo:hi], planes[a, t][:].indirect(clicks[:, lo // 16 : hi // 16]), wgt_sb[:, lo:hi], MULT
+                picked[a, lo // BANK][:, t, lo % BANK : lo % BANK + hi - lo], planes[a, t][:].indirect(clicks[:, lo // 16 : hi // 16]), wgt_sb[:, lo:hi], MULT
             )
 
         xg_bf = {}
 
         def round_xg(a, lo, hi):
-            xg_bf[a, lo] = stage.tile([P, PACK * (hi - lo)], BF16, name="xg_bf", tag="xg_bf", align_bytes=64)
+            xg_bf[a, lo] = stage.tile([P, PACK * (hi - lo)], BF16, name="xg_bf", tag="xg_bf", bufs=4, align_bytes=64)
             nc.scalar.copy(
-                out=xg_bf[a, lo][:].rearrange("p (c i t) -> p c t i", i=4, t=PACK),
-                in_=picked[a][:, :, lo:hi].rearrange("p t (c i) -> p c t i", i=4),
+                out=xg_bf[a, lo][:].rearrange("p (c i t) -> p c t i", i=2, t=PACK),
+                in_=picked[a, lo // BANK][:, :, lo % BANK : lo % BANK + hi - lo].rearrange("p t (c i) -> p c t i", i=2),
             )
 
         def quantize_xg(a, lo, hi):
@@ -96,7 +97,11 @@ def tile_list_interest_user_gate_kernel(
         wp_bf = {}
 
         def round_wp(h, a, copy):
-            wp_bf[h, a] = stage.tile([P, PACK * KP], BF16, name="wp_bf", tag="wp_bf", align_bytes=64)
+            if (h, a) == (1, 0):
+                late = keep.tile([P, 2, PACK * KP], BF16, name="wp_bf", tag="picked10", align_bytes=64)
+                wp_bf[1, 0], wp_bf[1, 1] = late[:, 0, :], late[:, 1, :]
+            if h == 0:
+                wp_bf[h, a] = stage.tile([P, PACK * KP], BF16, name="wp_bf", tag="wp_bf", bufs=2, align_bytes=64)
             copy(
                 out=wp_bf[h, a][:].rearrange("p (t m i) -> p m i t", t=PACK, i=PACK),
                 in_=wp_raw[h, a][:].rearrange("p i (m t) -> p m i t", t=PACK),
@@ -141,9 +146,9 @@ def tile_list_interest_user_gate_kernel(
                             stop=(a == 1),
                         )
                 nc.vector.tensor_tensor(
-                    h_bf[h, lo][:, PACK * (j0 - lo) : PACK * (j0 - lo + JC)].rearrange("p (c i t) -> p c t i", i=4, t=PACK),
-                    acc[:].rearrange("p t (c i) -> p c t i", i=4),
-                    gate[h][:, :, j0 : j0 + JC].rearrange("p t (c i) -> p c t i", i=4),
+                    h_bf[h, lo][:, PACK * (j0 - lo) : PACK * (j0 - lo + JC)].rearrange("p (c i t) -> p c t i", i=2, t=PACK),
+                    acc[:].rearrange("p t (c i) -> p c t i", i=2),
+                    gate[h][:, :, j0 : j0 + JC].rearrange("p t (c i) -> p c t i", i=2),
                     MULT,
                 )
 
@@ -201,7 +206,6 @@ def tile_list_interest_user_gate_kernel(
         warm = keep.tile([P, 2], F32, name="warm", align_bytes=64)
         nc.vector.memset(tab_s[:].bitcast(I32), 0)
         nc.gpsimd.memset(wg_s_raw[:].bitcast(I32), 0)
-        nc.gpsimd.memset(wt_s[:].bitcast(I32), 0)
         nc.gpsimd.memset(warm[:, 0:1], 0.0)
         nc.scalar.activation(out=warm[:, 1:2], in_=warm[:, 0:1], func=ACT.Sigmoid)
         wt_rows = wt_scales.rearrange("a r n -> r a n")
@@ -213,32 +217,34 @@ def tile_list_interest_user_gate_kernel(
         load_scale_rows(wg_s_raw, wg_scales[0], range(4), nc.sync)
         nc.sync.dma_start(out=wgt_sb[:], in_=wgt)
         load_plane(0, 0)
-        nc.sync.dma_start(out=bg_sb[:], in_=bg.rearrange("(h p t) -> p h t", h=2, t=PACK))
+        nc.sync.dma_start(out=bg_sb[:, :, 0:PACK], in_=bg.rearrange("(h p t) -> p h t", h=2, t=PACK))
         load_plane(0, 1)
         load_plane(0, 2)
-        load_scale_rows(wt_s, wt_rows, range(0, 2), nc.sync)
         load_plane(0, 3)
-        load_scale_rows(wt_s, wt_rows, range(2, 4), nc.sync)
-        load_wp(0, 0)
         load_plane(1, 0)
-        with nc.allow_non_contiguous_dma(reason="one bias value for each partition"):
-            nc.sync.dma_start(out=bt_sb[:], in_=bt.rearrange("(m p) -> p m", p=P))
         load_plane(1, 1)
         load_plane(1, 2)
-        load_wp(0, 1)
+        load_wp(0, 0)
         load_plane(1, 3)
+        load_wp(0, 1)
         load_wp(1, 0)
         load_wp(1, 1)
+        wt_s = stream.tile([P, 2, N], U8, name="wt_s", tag="stream", align_bytes=64)
+        nc.gpsimd.memset(wt_s[:].bitcast(I32), 0)
+        load_scale_rows(wt_s, wt_rows, range(4), nc.sync)
         wt_w = stream.tile([P, 2, N], U32, name="wt_w", tag="stream", align_bytes=64)
         nc.sync.dma_start(out=wt_w[:].bitcast(I32), in_=wt_words.rearrange("a p n t -> p a (n t)").bitcast(I32))
+        bt_sb = stream.tile([P, N // P], F32, name="bt_sb", tag="stream", align_bytes=64)
+        with nc.allow_non_contiguous_dma(reason="one bias value for each partition"):
+            nc.sync.dma_start(out=bt_sb[:], in_=bt.rearrange("(m p) -> p m", p=P))
         nc.vector.tensor_copy(
-            out=wg_w[:].bitcast(U16).rearrange("p (h t m) -> p h m t", h=2, t=PACK),
-            in_=wg_w_raw[:].bitcast(U16).rearrange("p (h m t) -> p h m t", h=2, t=PACK),
+            out=wg_w[:].bitcast(U16).rearrange("p (h t m) -> p h t m", h=2, t=PACK),
+            in_=wg_w_raw[:].bitcast(U16).rearrange("p (h m t) -> p h t m", h=2, t=PACK),
         )
         nc.vector.tensor_copy(v_s[:], tab_s[:].indirect(users[:]))
         nc.vector.tensor_copy(
-            out=wg_s[:].rearrange("p (h t m) -> p h m t", h=2, t=PACK),
-            in_=wg_s_raw[:].rearrange("p (h m t) -> p h m t", h=2, t=PACK),
+            out=wg_s[:].rearrange("p (h t m) -> p h t m", h=2, t=PACK),
+            in_=wg_s_raw[:].rearrange("p (h m t) -> p h t m", h=2, t=PACK),
         )
         nc.vector.tensor_copy(v_w[:, 0:512], tab_w[:].indirect(users[:, 0:32]))
         nc.vector.tensor_copy(v_w[:, 512:1024], tab_w[:].indirect(users[:, 32:64]))
@@ -258,36 +264,34 @@ def tile_list_interest_user_gate_kernel(
             make_gate(1, t, 0)
         for t in range(PACK):
             make_gate(1, t, 512)
-        round_wp(0, 0, nc.scalar.copy)
         round_xg(0, 0, 512)
         round_xg(0, 512, 1024)
+        round_wp(0, 0, nc.scalar.copy)
         gather(1, 0, 0, 512)
         gather(1, 0, 512, 1024)
-        quantize_wp(0, 0)
-        gather(1, 1, 0, 512)
         quantize_xg(0, 0, 512)
+        gather(1, 1, 0, 512)
         gather(1, 1, 512, 1024)
-        gather(1, 2, 0, 512)
         quantize_xg(0, 512, 1024)
+        gather(1, 2, 0, 512)
         gather(1, 2, 512, 1024)
-        round_wp(0, 1, nc.scalar.copy)
         gather(1, 3, 0, 256)
         gather(1, 3, 256, 512)
-        quantize_wp(0, 1)
-        gather(1, 3, 512, 1024)
+        quantize_wp(0, 0)
         round_xg(1, 0, 256)
         round_xg(1, 256, 512)
+        round_wp(0, 1, nc.vector.tensor_copy)
+        quantize_xg(1, 0, 256)
+        quantize_wp(0, 1)
+        quantize_xg(1, 256, 512)
+        gather(1, 3, 512, 1024)
         round_wp(1, 0, nc.scalar.copy)
         round_wp(1, 1, nc.scalar.copy)
         round_xg(1, 512, 1024)
-        quantize_xg(1, 0, 256)
-        make_h(0, 0, 256)
-        quantize_xg(1, 256, 512)
-        make_h(0, 256, 512)
+        make_h(0, 0, 512)
         quantize_wp(1, 0)
-        quantize_h(0, 0, 256)
+        quantize_h(0, 0, 512)
         quantize_wp(1, 1)
-        quantize_h(0, 256, 512)
         tower_pass(0, 0, 512)
         make_h(1, 0, 512)
         quantize_xg(1, 512, 1024)

@@ -98,7 +98,7 @@ def tile_list_interest_user_gate_kernel(
 
         def round_wp(h, a, copy):
             if (h, a) == (1, 0):
-                late = keep.tile([P, 2, PACK * KP], BF16, name="wp_bf", tag="picked10", align_bytes=64)
+                late = keep.tile([P, 2, PACK * KP], BF16, name="wp_bf", tag="picked11", align_bytes=64)
                 wp_bf[1, 0], wp_bf[1, 1] = late[:, 0, :], late[:, 1, :]
             if h == 0:
                 wp_bf[h, a] = stage.tile([P, PACK * KP], BF16, name="wp_bf", tag="wp_bf", bufs=2, align_bytes=64)
@@ -127,11 +127,25 @@ def tile_list_interest_user_gate_kernel(
                 out=gate[h][:, t, lo : lo + BANK], in_=acc[:], func=ACT.Sigmoid, bias=bg_sb[:, h, t : t + 1]
             )
 
+        def warm_up(passes):
+            scratch = psum.tile([P, BANK], F32, name="tower", tag="tower")
+            for rep in range(passes):
+                nc.tensor.matmul_mx(
+                    out=scratch[:],
+                    lhsT=wp_w[0][:, 0:P].bitcast(FP8X4),
+                    lhsT_scale=wp_s[0][:, 0:P],
+                    rhs=xg_w[0][:, 0:BANK].bitcast(FP8X4),
+                    rhs_scale=xg_s[0][:, 0:BANK],
+                    start=True,
+                    stop=True,
+                )
+
         h_bf = {}
 
-        def make_h(h, lo, hi):
-            h_bf[h, lo] = stage.tile([P, PACK * (hi - lo)], BF16, name="h_bf", tag="h_bf", bufs=4, align_bytes=64)
-            for j0 in range(lo, hi, JC):
+        def make_h(h, lo, hi, first, last):
+            if first == lo:
+                h_bf[h, lo] = stage.tile([P, PACK * (hi - lo)], BF16, name="h_bf", tag="h_bf", bufs=4, align_bytes=64)
+            for j0 in range(first, last, JC):
                 acc = psum.tile([P, PACK, JC], F32, name="acc", tag="acc")
                 for t in range(PACK):
                     c0 = KP * h + P * t
@@ -173,8 +187,8 @@ def tile_list_interest_user_gate_kernel(
 
         out_rows = out.rearrange("(m p) j -> p m j", p=P)
 
-        def tower_bank(lo, hi, m0, m1, on_vector):
-            acc = psum.tile([P, m1 - m0, hi - lo], F32, name="tower", tag="tower")
+        def tower_bank(lo, hi, m0, m1, on_vector, tag):
+            acc = psum.tile([P, m1 - m0, hi - lo], F32, name="tower", tag=tag)
             for m in range(m0, m1):
                 for h in range(2):
                     nc.tensor.matmul_mx(
@@ -277,39 +291,45 @@ def tile_list_interest_user_gate_kernel(
         gather(1, 2, 512, 1024)
         gather(1, 3, 0, 256)
         gather(1, 3, 256, 512)
+        gather(1, 3, 512, 1024)
         quantize_wp(0, 0)
+        warm_up(4)
         round_xg(1, 0, 256)
         round_xg(1, 256, 512)
-        round_wp(0, 1, nc.vector.tensor_copy)
+        round_xg(1, 512, 1024)
         quantize_xg(1, 0, 256)
+        round_wp(0, 1, nc.vector.tensor_copy)
         quantize_wp(0, 1)
         quantize_xg(1, 256, 512)
-        gather(1, 3, 512, 1024)
         round_wp(1, 0, nc.scalar.copy)
         round_wp(1, 1, nc.scalar.copy)
-        round_xg(1, 512, 1024)
-        make_h(0, 0, 512)
-        quantize_wp(1, 0)
-        quantize_h(0, 0, 512)
-        quantize_wp(1, 1)
-        tower_pass(0, 0, 512)
-        make_h(1, 0, 512)
         quantize_xg(1, 512, 1024)
-        make_h(0, 512, 768)
-        quantize_h(1, 0, 512)
-        tower_pass(1, 0, 512)
-        store(0, 512, ())
-        make_h(1, 512, 768)
-        quantize_h(0, 512, 768)
-        make_h(0, 768, 1024)
+        make_h(0, 0, 512, 0, 512)
+        make_h(0, 512, 1024, 512, 768)
+        quantize_h(0, 0, 512)
+        tower_pass(0, 0, 256)
+        quantize_wp(1, 0)
+        quantize_wp(1, 1)
+        make_h(0, 512, 1024, 768, 1024)
+        make_h(1, 0, 256, 0, 256)
+        quantize_h(0, 512, 1024)
+        make_h(1, 256, 512, 256, 384)
+        quantize_h(1, 0, 256)
+        tower_pass(1, 0, 256)
+        store(0, 256, ())
+        make_h(1, 256, 512, 384, 512)
+        make_h(1, 512, 768, 512, 640)
+        quantize_h(1, 256, 512)
+        tower_bank(256, 512, 0, 2, False, "tower")
+        tower_bank(256, 512, 2, 4, False, "tower")
+        make_h(1, 512, 768, 640, 768)
+        make_h(1, 768, 896, 768, 896)
         quantize_h(1, 512, 768)
-        tower_bank(512, 768, 0, 2, False)
-        tower_bank(512, 768, 2, 4, False)
-        make_h(1, 768, 896)
-        quantize_h(0, 768, 1024)
-        make_h(1, 896, 1024)
+        tower_bank(512, 768, 0, 2, False, "tower")
+        tower_bank(512, 768, 2, 4, False, "tower")
+        make_h(1, 896, 1024, 896, 1024)
         quantize_h(1, 768, 896)
-        tower_bank(768, 896, 0, 4, False)
         quantize_h(1, 896, 1024)
-        tower_bank(896, 1024, 0, 2, False)
-        tower_bank(896, 1024, 2, 4, True)
+        tower_bank(768, 896, 0, 4, True, "tower")
+        tower_bank(896, 1024, 0, 2, False, "tower")
+        tower_bank(896, 1024, 2, 4, True, "acc")

@@ -32,7 +32,7 @@ def tile_list_interest_user_gate_kernel(
         keep = ctx.enter_context(tc.tile_pool(name="keep", bufs=1))
         stream = ctx.enter_context(tc.tile_pool(name="stream", bufs=7))
         stage = ctx.enter_context(tc.tile_pool(name="stage", bufs=3))
-        psum = ctx.enter_context(tc.psum_pool(name="psum", bufs=4))
+        psum = ctx.enter_context(tc.psum_pool(name="psum", bufs=1))
 
         users = lists.tile([P, S // 16], U16, name="users")
         clicks = lists.tile([P, S // 16], U16, name="clicks")
@@ -47,10 +47,7 @@ def tile_list_interest_user_gate_kernel(
         wg_s = keep.tile([P, H], U8, name="wg_s", align_bytes=64)
         wgt_sb = keep.tile([P, S], F32, name="wgt_sb", align_bytes=64)
         bg_sb = keep.tile([P, 2, 8], F32, name="bg_sb", align_bytes=64)
-        picked = {}
-        for a in range(2):
-            for s in range(2):
-                picked[a, s] = keep.tile([P, PACK, BANK], F32, name="picked", tag="picked%d%d" % (a, s), align_bytes=64)
+        picked = [keep.tile([P, PACK, S], F32, name="picked%d" % a, align_bytes=64) for a in range(2)]
         gate = [keep.tile([P, PACK, S], F32, name="gate%d" % h, align_bytes=64) for h in range(2)]
         xg_w = [keep.tile([P, S], U32, name="xg_w%d" % a, align_bytes=64) for a in range(2)]
         xg_s = [keep.tile([P, S], U8, name="xg_s%d" % a, align_bytes=64) for a in range(2)]
@@ -79,30 +76,25 @@ def tile_list_interest_user_gate_kernel(
 
         def gather(a, t, lo, hi):
             nc.vector.tensor_tensor(
-                picked[a, lo // BANK][:, t, lo % BANK : lo % BANK + hi - lo], planes[a, t][:].indirect(clicks[:, lo // 16 : hi // 16]), wgt_sb[:, lo:hi], MULT
+                picked[a][:, t, lo:hi], planes[a, t][:].indirect(clicks[:, lo // 16 : hi // 16]), wgt_sb[:, lo:hi], MULT
             )
 
-        xg_bf = {}
+        xg_bf = [keep.tile([P, PACK * S], BF16, name="xg_bf%d" % a, align_bytes=64) for a in range(2)]
 
         def round_xg(a, lo, hi):
-            xg_bf[a, lo] = stage.tile([P, PACK * (hi - lo)], BF16, name="xg_bf", tag="xg_bf", bufs=4, align_bytes=64)
             nc.scalar.copy(
-                out=xg_bf[a, lo][:].rearrange("p (c i t) -> p c t i", i=2, t=PACK),
-                in_=picked[a, lo // BANK][:, :, lo % BANK : lo % BANK + hi - lo].rearrange("p t (c i) -> p c t i", i=2),
+                out=xg_bf[a][:, PACK * lo : PACK * hi].rearrange("p (c i t) -> p c t i", i=2, t=PACK),
+                in_=picked[a][:, :, lo:hi].rearrange("p t (c i) -> p c t i", i=2),
             )
 
         def quantize_xg(a, lo, hi):
-            nc.vector.quantize_mx(out=xg_w[a][:, lo:hi].bitcast(FP8X4), scales=xg_s[a][:, lo:hi], in_=xg_bf[a, lo][:])
+            nc.vector.quantize_mx(out=xg_w[a][:, lo:hi].bitcast(FP8X4), scales=xg_s[a][:, lo:hi], in_=xg_bf[a][:, PACK * lo : PACK * hi])
 
         wp_bf = {}
 
-        def round_wp(h, a, copy):
-            if (h, a) == (1, 0):
-                late = keep.tile([P, 2, PACK * KP], BF16, name="wp_bf", tag="picked11", align_bytes=64)
-                wp_bf[1, 0], wp_bf[1, 1] = late[:, 0, :], late[:, 1, :]
-            if h == 0:
-                wp_bf[h, a] = stage.tile([P, PACK * KP], BF16, name="wp_bf", tag="wp_bf", bufs=2, align_bytes=64)
-            copy(
+        def round_wp(h, a):
+            wp_bf[h, a] = stage.tile([P, PACK * KP], BF16, name="wp_bf", tag="wp_bf", bufs=2, align_bytes=64)
+            nc.scalar.copy(
                 out=wp_bf[h, a][:].rearrange("p (t m i) -> p m i t", t=PACK, i=PACK),
                 in_=wp_raw[h, a][:].rearrange("p i (m t) -> p m i t", t=PACK),
             )
@@ -111,11 +103,18 @@ def tile_list_interest_user_gate_kernel(
             cols = slice(KP * h, KP * (h + 1))
             nc.vector.quantize_mx(out=wp_w[a][:, cols].bitcast(FP8X4), scales=wp_s[a][:, cols], in_=wp_bf[h, a][:])
 
+        def order_wg_scales(h):
+            cols = slice(KP * h, KP * (h + 1))
+            nc.vector.tensor_copy(
+                out=wg_s[:, cols].rearrange("p (t m) -> p t m", t=PACK),
+                in_=wg_s_raw[:, cols].rearrange("p (m t) -> p t m", t=PACK),
+            )
+
         def make_gate(h, t, lo):
-            acc = psum.tile([P, BANK], F32, name="acc", tag="acc")
+            pre = psum.tile([P, BANK], F32, name="pre", tag="bank%d" % (t + PACK * (lo // BANK)))
             c0 = KP * h + P * t
             nc.tensor.matmul_mx(
-                out=acc[:],
+                out=pre[:],
                 lhsT=wg_w[:, 2 * c0 : 2 * (c0 + P)].bitcast(FP4X4),
                 lhsT_scale=wg_s[:, c0 : c0 + P],
                 rhs=v_w[:, lo : lo + BANK].bitcast(FP8X4),
@@ -124,44 +123,37 @@ def tile_list_interest_user_gate_kernel(
                 stop=True,
             )
             nc.scalar.activation(
-                out=gate[h][:, t, lo : lo + BANK], in_=acc[:], func=ACT.Sigmoid, bias=bg_sb[:, h, t : t + 1]
+                out=gate[h][:, t, lo : lo + BANK], in_=pre[:], func=ACT.Sigmoid, bias=bg_sb[:, h, t : t + 1]
             )
 
-        def warm_up(passes):
-            scratch = psum.tile([P, BANK], F32, name="tower", tag="tower")
-            for rep in range(passes):
-                nc.tensor.matmul_mx(
-                    out=scratch[:],
-                    lhsT=wp_w[0][:, 0:P].bitcast(FP8X4),
-                    lhsT_scale=wp_s[0][:, 0:P],
-                    rhs=xg_w[0][:, 0:BANK].bitcast(FP8X4),
-                    rhs_scale=xg_s[0][:, 0:BANK],
-                    start=True,
-                    stop=True,
-                )
-
         h_bf = {}
+
+        acc = {}
+
+        def project(h, a, first, last, bank):
+            for j0 in range(first, last, JC):
+                if a == 0:
+                    acc[h, j0] = psum.tile([P, PACK, JC], F32, name="acc", tag="bank%d" % (bank + (j0 - first) // JC))
+                for t in range(PACK):
+                    c0 = KP * h + P * t
+                    nc.tensor.matmul_mx(
+                        out=acc[h, j0][:, t, :],
+                        lhsT=wp_w[a][:, c0 : c0 + P].bitcast(FP8X4),
+                        lhsT_scale=wp_s[a][:, c0 : c0 + P],
+                        rhs=xg_w[a][:, j0 : j0 + JC].bitcast(FP8X4),
+                        rhs_scale=xg_s[a][:, j0 : j0 + JC],
+                        start=(a == 0 and t == 0),
+                        stop=(a == 1 and t == PACK - 1),
+                    )
 
         def make_h(h, lo, hi, first, last):
             if first == lo:
                 h_bf[h, lo] = stage.tile([P, PACK * (hi - lo)], BF16, name="h_bf", tag="h_bf", bufs=4, align_bytes=64)
             for j0 in range(first, last, JC):
-                acc = psum.tile([P, PACK, JC], F32, name="acc", tag="acc")
-                for t in range(PACK):
-                    c0 = KP * h + P * t
-                    for a in range(2):
-                        nc.tensor.matmul_mx(
-                            out=acc[:, t, :],
-                            lhsT=wp_w[a][:, c0 : c0 + P].bitcast(FP8X4),
-                            lhsT_scale=wp_s[a][:, c0 : c0 + P],
-                            rhs=xg_w[a][:, j0 : j0 + JC].bitcast(FP8X4),
-                            rhs_scale=xg_s[a][:, j0 : j0 + JC],
-                            start=(a == 0),
-                            stop=(a == 1),
-                        )
+                project(h, 1, j0, j0 + JC, None)
                 nc.vector.tensor_tensor(
                     h_bf[h, lo][:, PACK * (j0 - lo) : PACK * (j0 - lo + JC)].rearrange("p (c i t) -> p c t i", i=2, t=PACK),
-                    acc[:].rearrange("p t (c i) -> p c t i", i=2),
+                    acc[h, j0][:].rearrange("p t (c i) -> p c t i", i=2),
                     gate[h][:, :, j0 : j0 + JC].rearrange("p t (c i) -> p c t i", i=2),
                     MULT,
                 )
@@ -169,53 +161,38 @@ def tile_list_interest_user_gate_kernel(
         def quantize_h(h, lo, hi):
             nc.vector.quantize_mx(out=h_w[h][:, lo:hi].bitcast(FP8X4), scales=h_s[h][:, lo:hi], in_=h_bf[h, lo][:])
 
+        out_rows = out.rearrange("(m p) j -> p m j", p=P)
+
         tower = {}
 
-        def tower_pass(h, lo, hi):
-            for m in range(N // P):
-                if h == 0:
-                    tower[lo, m] = psum.tile([P, hi - lo], F32, name="tower", tag="tower")
+        def tower_pass(h, lo, hi, m0, m1, bank):
+            if h == 0:
+                tower[lo, m0] = psum.tile([P, m1 - m0, hi - lo], F32, name="tower", tag="bank%d" % bank)
+            for m in range(m0, m1):
                 nc.tensor.matmul_mx(
-                    out=tower[lo, m][:],
+                    out=tower[lo, m0][:, m - m0, :],
                     lhsT=wt_w[:, h, P * m : P * (m + 1)].bitcast(FP8X4),
                     lhsT_scale=wt_s[:, h, P * m : P * (m + 1)],
                     rhs=h_w[h][:, lo:hi].bitcast(FP8X4),
                     rhs_scale=h_s[h][:, lo:hi],
-                    start=(h == 0),
-                    stop=(h == 1),
+                    start=(h == 0 and m == m0),
+                    stop=(h == 1 and m == m1 - 1),
                 )
 
-        out_rows = out.rearrange("(m p) j -> p m j", p=P)
-
-        def tower_bank(lo, hi, m0, m1, on_vector, tag):
-            acc = psum.tile([P, m1 - m0, hi - lo], F32, name="tower", tag=tag)
-            for m in range(m0, m1):
-                for h in range(2):
-                    nc.tensor.matmul_mx(
-                        out=acc[:, m - m0, :],
-                        lhsT=wt_w[:, h, P * m : P * (m + 1)].bitcast(FP8X4),
-                        lhsT_scale=wt_s[:, h, P * m : P * (m + 1)],
-                        rhs=h_w[h][:, lo:hi].bitcast(FP8X4),
-                        rhs_scale=h_s[h][:, lo:hi],
-                        start=(h == 0),
-                        stop=(h == 1),
-                    )
+        def store(lo, hi, m0, m1, on_vector):
             res = stage.tile([P, m1 - m0, hi - lo], F32, name="res", tag="res", bufs=6, align_bytes=64)
             for m in range(m0, m1):
                 if on_vector:
-                    nc.vector.tensor_scalar_add(res[:, m - m0, :], acc[:, m - m0, :], bt_sb[:, m : m + 1])
+                    nc.vector.tensor_scalar_add(res[:, m - m0, :], tower[lo, m0][:, m - m0, :], bt_sb[:, m : m + 1])
                 else:
-                    nc.scalar.activation(out=res[:, m - m0, :], in_=acc[:, m - m0, :], func=ACT.Identity, bias=bt_sb[:, m : m + 1])
+                    nc.scalar.activation(
+                        out=res[:, m - m0, :], in_=tower[lo, m0][:, m - m0, :], func=ACT.Identity, bias=bt_sb[:, m : m + 1]
+                    )
             nc.sync.dma_start(out=out_rows[:, m0:m1, lo:hi], in_=res[:])
 
-        def store(lo, hi, on_vector):
-            for m in range(N // P):
-                res = stage.tile([P, hi - lo], F32, name="res", tag="res", bufs=6, align_bytes=64)
-                if m in on_vector:
-                    nc.vector.tensor_scalar_add(res[:], tower[lo, m][:], bt_sb[:, m : m + 1])
-                else:
-                    nc.scalar.activation(out=res[:], in_=tower[lo, m][:], func=ACT.Identity, bias=bt_sb[:, m : m + 1])
-                nc.sync.dma_start(out=out[P * m : P * (m + 1), lo:hi], in_=res[:])
+        def finish(lo, hi, m0, m1, on_vector):
+            tower_pass(1, lo, hi, m0, m1, None)
+            store(lo, hi, m0, m1, on_vector)
 
         warm = keep.tile([P, 2], F32, name="warm", align_bytes=64)
         nc.vector.memset(tab_s[:].bitcast(I32), 0)
@@ -230,17 +207,17 @@ def tile_list_interest_user_gate_kernel(
         nc.sync.dma_start(out=tab_w[:].bitcast(I32), in_=tab_words[0].rearrange("p n t -> p (n t)").bitcast(I32))
         load_scale_rows(wg_s_raw, wg_scales[0], range(4), nc.sync)
         nc.sync.dma_start(out=wgt_sb[:], in_=wgt)
-        load_plane(0, 0)
         nc.sync.dma_start(out=bg_sb[:, :, 0:PACK], in_=bg.rearrange("(h p t) -> p h t", h=2, t=PACK))
+        load_plane(0, 0)
         load_plane(0, 1)
         load_plane(0, 2)
         load_plane(0, 3)
         load_plane(1, 0)
         load_plane(1, 1)
-        load_plane(1, 2)
         load_wp(0, 0)
-        load_plane(1, 3)
+        load_plane(1, 2)
         load_wp(0, 1)
+        load_plane(1, 3)
         load_wp(1, 0)
         load_wp(1, 1)
         wt_s = stream.tile([P, 2, N], U8, name="wt_s", tag="stream", align_bytes=64)
@@ -256,80 +233,82 @@ def tile_list_interest_user_gate_kernel(
             in_=wg_w_raw[:].bitcast(U16).rearrange("p (h m t) -> p h t m", h=2, t=PACK),
         )
         nc.vector.tensor_copy(v_s[:], tab_s[:].indirect(users[:]))
-        nc.vector.tensor_copy(
-            out=wg_s[:].rearrange("p (h t m) -> p h t m", h=2, t=PACK),
-            in_=wg_s_raw[:].rearrange("p (h m t) -> p h t m", h=2, t=PACK),
-        )
         nc.vector.tensor_copy(v_w[:, 0:512], tab_w[:].indirect(users[:, 0:32]))
+        order_wg_scales(0)
         nc.vector.tensor_copy(v_w[:, 512:1024], tab_w[:].indirect(users[:, 32:64]))
+        order_wg_scales(1)
+        for h in range(2):
+            for lo in range(0, S, BANK):
+                for t in range(PACK):
+                    make_gate(h, t, lo)
         for t in range(PACK):
-            make_gate(0, t, 0)
-        for t in range(PACK):
-            make_gate(0, t, 512)
-        gather(0, 0, 0, 512)
-        gather(0, 0, 512, 1024)
-        gather(0, 1, 0, 512)
-        gather(0, 1, 512, 1024)
-        gather(0, 2, 0, 512)
-        gather(0, 2, 512, 1024)
-        gather(0, 3, 0, 512)
-        gather(0, 3, 512, 1024)
-        for t in range(PACK):
-            make_gate(1, t, 0)
-        for t in range(PACK):
-            make_gate(1, t, 512)
+            gather(0, t, 0, S)
         round_xg(0, 0, 512)
         round_xg(0, 512, 1024)
-        round_wp(0, 0, nc.scalar.copy)
-        gather(1, 0, 0, 512)
-        gather(1, 0, 512, 1024)
-        quantize_xg(0, 0, 512)
-        gather(1, 1, 0, 512)
-        gather(1, 1, 512, 1024)
-        quantize_xg(0, 512, 1024)
-        gather(1, 2, 0, 512)
-        gather(1, 2, 512, 1024)
-        gather(1, 3, 0, 256)
-        gather(1, 3, 256, 512)
-        gather(1, 3, 512, 1024)
+        round_wp(0, 0)
+        round_wp(0, 1)
+        gather(1, 0, 0, S)
+        gather(1, 1, 0, S)
+        quantize_xg(0, 0, S)
         quantize_wp(0, 0)
-        warm_up(4)
-        round_xg(1, 0, 256)
-        round_xg(1, 256, 512)
-        round_xg(1, 512, 1024)
-        quantize_xg(1, 0, 256)
-        round_wp(0, 1, nc.vector.tensor_copy)
+        project(0, 0, 0, S, 0)
+        gather(1, 2, 0, S)
+        gather(1, 3, 0, 256)
         quantize_wp(0, 1)
+        gather(1, 3, 256, 512)
+        gather(1, 3, 512, 768)
+        round_xg(1, 0, 256)
+        quantize_xg(1, 0, 256)
+        gather(1, 3, 768, 1024)
+        round_xg(1, 256, 512)
+        round_xg(1, 512, 768)
+        round_wp(1, 0)
+        round_wp(1, 1)
+        round_xg(1, 768, 1024)
         quantize_xg(1, 256, 512)
-        round_wp(1, 0, nc.scalar.copy)
-        round_wp(1, 1, nc.scalar.copy)
-        quantize_xg(1, 512, 1024)
-        make_h(0, 0, 512, 0, 512)
-        make_h(0, 512, 1024, 512, 768)
-        quantize_h(0, 0, 512)
-        tower_pass(0, 0, 256)
+        make_h(0, 0, 512, 0, 256)
+        quantize_xg(1, 512, 768)
+        make_h(0, 0, 512, 256, 512)
         quantize_wp(1, 0)
+        project(1, 0, 0, 512, 0)
+        make_h(0, 512, 768, 512, 640)
+        quantize_h(0, 0, 512)
+        make_h(0, 512, 768, 640, 768)
+        tower_pass(0, 0, 256, 0, 2, 4)
+        tower_pass(0, 0, 256, 2, 4, 5)
         quantize_wp(1, 1)
-        make_h(0, 512, 1024, 768, 1024)
+        quantize_h(0, 512, 768)
+        quantize_xg(1, 768, 1024)
         make_h(1, 0, 256, 0, 256)
-        quantize_h(0, 512, 1024)
+        project(1, 0, 512, 768, 0)
         make_h(1, 256, 512, 256, 384)
         quantize_h(1, 0, 256)
-        tower_pass(1, 0, 256)
-        store(0, 256, ())
+        finish(0, 256, 0, 2, False)
+        finish(0, 256, 2, 4, False)
         make_h(1, 256, 512, 384, 512)
+        tower_pass(0, 256, 512, 0, 2, 2)
+        tower_pass(0, 256, 512, 2, 4, 3)
         make_h(1, 512, 768, 512, 640)
         quantize_h(1, 256, 512)
-        tower_bank(256, 512, 0, 2, False, "tower")
-        tower_bank(256, 512, 2, 4, False, "tower")
+        finish(256, 512, 0, 2, False)
+        finish(256, 512, 2, 4, False)
+        project(1, 0, 768, 1024, 4)
         make_h(1, 512, 768, 640, 768)
-        make_h(1, 768, 896, 768, 896)
+        tower_pass(0, 512, 768, 0, 2, 0)
+        tower_pass(0, 512, 768, 2, 4, 1)
+        make_h(0, 768, 1024, 768, 896)
         quantize_h(1, 512, 768)
-        tower_bank(512, 768, 0, 2, False, "tower")
-        tower_bank(512, 768, 2, 4, False, "tower")
-        make_h(1, 896, 1024, 896, 1024)
+        finish(512, 768, 0, 2, False)
+        finish(512, 768, 2, 4, False)
+        make_h(0, 768, 1024, 896, 1024)
+        make_h(1, 768, 896, 768, 896)
+        quantize_h(0, 768, 1024)
+        tower_pass(0, 768, 896, 0, 4, 6)
+        tower_pass(0, 896, 1024, 0, 2, 7)
+        tower_pass(0, 896, 1024, 2, 4, 2)
         quantize_h(1, 768, 896)
+        finish(768, 896, 0, 4, False)
+        make_h(1, 896, 1024, 896, 1024)
         quantize_h(1, 896, 1024)
-        tower_bank(768, 896, 0, 4, True, "tower")
-        tower_bank(896, 1024, 0, 2, False, "tower")
-        tower_bank(896, 1024, 2, 4, True, "acc")
+        finish(896, 1024, 0, 2, True)
+        finish(896, 1024, 2, 4, False)

@@ -1,6 +1,7 @@
 from contextlib import ExitStack
 
 import concourse.mybir as mybir
+from concourse.masks import make_identity
 
 K, D, H, N, T, S = 1024, 512, 1024, 512, 2048, 1024
 FLOPS = 2 * S * (K * H + D * H + H * N)
@@ -46,6 +47,8 @@ def tile_list_interest_user_gate_kernel(
         wg_w = keep.tile([P, 2 * H], U8, name="wg_w", align_bytes=64)
         wg_s = keep.tile([P, H], U8, name="wg_s", align_bytes=64)
         wgt_sb = keep.tile([P, S], F32, name="wgt_sb", align_bytes=64)
+        wgt_raw = keep.tile([P, P], F32, name="wgt_raw", align_bytes=64)
+        ident = keep.tile([P, P], F32, name="ident", align_bytes=64)
         bg_sb = keep.tile([P, 2, 8], F32, name="bg_sb", align_bytes=64)
         picked = [keep.tile([P, PACK, S], F32, name="picked%d" % a, align_bytes=64) for a in range(2)]
         gate = [keep.tile([P, PACK, S], F32, name="gate%d" % h, align_bytes=64) for h in range(2)]
@@ -69,10 +72,10 @@ def tile_list_interest_user_gate_kernel(
 
         wp_raw = {}
 
-        def load_wp(h, a):
-            wp_raw[h, a] = stream.tile([P, PACK, KP], F32, name="wp_raw", tag="stream", align_bytes=64)
-            rows = wp[KP * a : KP * (a + 1), KP * h : KP * (h + 1)].rearrange("(p i) c -> p i c", i=PACK)
-            nc.sync.dma_start(out=wp_raw[h, a][:], in_=rows)
+        def load_wp(h, a, lo=0, hi=KP):
+            wp_raw[h, a, lo] = stream.tile([P, PACK, hi - lo], F32, name="wp_raw", tag="stream", align_bytes=64)
+            rows = wp[KP * a : KP * (a + 1), KP * h + lo : KP * h + hi].rearrange("(p i) c -> p i c", i=PACK)
+            nc.sync.dma_start(out=wp_raw[h, a, lo][:], in_=rows)
 
         def gather(a, t, lo, hi):
             nc.vector.tensor_tensor(
@@ -92,11 +95,12 @@ def tile_list_interest_user_gate_kernel(
 
         wp_bf = {}
 
-        def round_wp(h, a):
-            wp_bf[h, a] = stage.tile([P, PACK * KP], BF16, name="wp_bf", tag="wp_bf", bufs=2, align_bytes=64)
+        def round_wp(h, a, lo=0, hi=KP):
+            if lo == 0:
+                wp_bf[h, a] = stage.tile([P, PACK * KP], BF16, name="wp_bf", tag="wp_bf", bufs=2, align_bytes=64)
             nc.scalar.copy(
-                out=wp_bf[h, a][:].rearrange("p (t m i) -> p m i t", t=PACK, i=PACK),
-                in_=wp_raw[h, a][:].rearrange("p i (m t) -> p m i t", t=PACK),
+                out=wp_bf[h, a][:].rearrange("p (t m i) -> p m i t", t=PACK, i=PACK)[:, lo // PACK : hi // PACK],
+                in_=wp_raw[h, a, lo][:].rearrange("p i (m t) -> p m i t", t=PACK),
             )
 
         def quantize_wp(h, a):
@@ -199,14 +203,15 @@ def tile_list_interest_user_gate_kernel(
         nc.gpsimd.memset(wg_s_raw[:].bitcast(I32), 0)
         nc.gpsimd.memset(warm[:, 0:1], 0.0)
         nc.scalar.activation(out=warm[:, 1:2], in_=warm[:, 0:1], func=ACT.Sigmoid)
+        make_identity(nc, ident[:])
         wt_rows = wt_scales.rearrange("a r n -> r a n")
         nc.sync.dma_start(users[:], offs)
         nc.sync.dma_start(out=wg_w_raw[:].bitcast(I32), in_=wg_words[0].bitcast(I32))
-        nc.sync.dma_start(clicks[:], offs2)
+        nc.sync.dma_start(out=wgt_raw[:], in_=wgt.rearrange("(g q) (b c) -> g (q b) c", q=16, c=P)[:, 0:16, :])
         load_scale_rows(tab_s, tab_scales[0], range(4), nc.sync)
         nc.sync.dma_start(out=tab_w[:].bitcast(I32), in_=tab_words[0].rearrange("p n t -> p (n t)").bitcast(I32))
         load_scale_rows(wg_s_raw, wg_scales[0], range(4), nc.sync)
-        nc.sync.dma_start(out=wgt_sb[:], in_=wgt)
+        nc.sync.dma_start(clicks[:], offs2)
         nc.sync.dma_start(out=bg_sb[:, :, 0:PACK], in_=bg.rearrange("(h p t) -> p h t", h=2, t=PACK))
         load_plane(0, 0)
         load_plane(0, 1)
@@ -214,11 +219,12 @@ def tile_list_interest_user_gate_kernel(
         load_plane(0, 3)
         load_plane(1, 0)
         load_plane(1, 1)
-        load_wp(0, 0)
         load_plane(1, 2)
+        load_wp(0, 0)
         load_wp(0, 1)
+        load_wp(1, 0, 0, 256)
         load_plane(1, 3)
-        load_wp(1, 0)
+        load_wp(1, 0, 256, 512)
         load_wp(1, 1)
         wt_s = stream.tile([P, 2, N], U8, name="wt_s", tag="stream", align_bytes=64)
         nc.gpsimd.memset(wt_s[:].bitcast(I32), 0)
@@ -228,6 +234,21 @@ def tile_list_interest_user_gate_kernel(
         bt_sb = stream.tile([P, N // P], F32, name="bt_sb", tag="stream", align_bytes=64)
         with nc.allow_non_contiguous_dma(reason="one bias value for each partition"):
             nc.sync.dma_start(out=bt_sb[:], in_=bt.rearrange("(m p) -> p m", p=P))
+        turned = psum.tile([P, P], F32, name="turned", tag="bank0")
+        nc.tensor.transpose(turned[:], wgt_raw[:], ident[:])
+        for half in range(2):
+            spread = stage.tile([P, PACK, P], F32, name="spread", tag="res", bufs=6, align_bytes=64)
+            nc.scalar.copy(
+                out=spread[:].rearrange("p b (g u r) -> p b g u r", g=8, r=2),
+                in_=turned[:]
+                .rearrange("p (g r b) -> p b g r", g=8, r=2)[:, PACK * half : PACK * (half + 1)]
+                .unsqueeze(3)
+                .broadcast_to([P, PACK, 8, 8, 2]),
+            )
+            back = psum.tile([P, PACK, P], F32, name="back", tag="bank%d" % (1 + half))
+            for b in range(PACK):
+                nc.tensor.transpose(back[:, b, :], spread[:, b, :], ident[:])
+            nc.scalar.copy(out=wgt_sb[:, BANK * half : BANK * (half + 1)], in_=back[:].rearrange("p b c -> p (b c)"))
         nc.vector.tensor_copy(
             out=wg_w[:].bitcast(U16).rearrange("p (h t m) -> p h t m", h=2, t=PACK),
             in_=wg_w_raw[:].bitcast(U16).rearrange("p (h m t) -> p h t m", h=2, t=PACK),
@@ -247,12 +268,13 @@ def tile_list_interest_user_gate_kernel(
         round_xg(0, 512, 1024)
         round_wp(0, 0)
         round_wp(0, 1)
+        round_wp(1, 0, 0, 256)
         gather(1, 0, 0, S)
         gather(1, 1, 0, S)
+        gather(1, 2, 0, S)
         quantize_xg(0, 0, S)
         quantize_wp(0, 0)
         project(0, 0, 0, S, 0)
-        gather(1, 2, 0, S)
         gather(1, 3, 0, 256)
         quantize_wp(0, 1)
         gather(1, 3, 256, 512)
@@ -261,54 +283,56 @@ def tile_list_interest_user_gate_kernel(
         quantize_xg(1, 0, 256)
         gather(1, 3, 768, 1024)
         round_xg(1, 256, 512)
-        round_xg(1, 512, 768)
-        round_wp(1, 0)
+        round_wp(1, 0, 256, 512)
         round_wp(1, 1)
+        round_xg(1, 512, 768)
         round_xg(1, 768, 1024)
         quantize_xg(1, 256, 512)
-        make_h(0, 0, 512, 0, 256)
-        quantize_xg(1, 512, 768)
-        make_h(0, 0, 512, 256, 512)
+        make_h(0, 0, 512, 0, 384)
         quantize_wp(1, 0)
-        project(1, 0, 0, 512, 0)
-        make_h(0, 512, 768, 512, 640)
-        quantize_h(0, 0, 512)
-        make_h(0, 512, 768, 640, 768)
-        tower_pass(0, 0, 256, 0, 2, 4)
-        tower_pass(0, 0, 256, 2, 4, 5)
+        project(1, 0, 0, 256, 0)
+        make_h(0, 0, 512, 384, 512)
+        project(1, 0, 256, 512, 2)
         quantize_wp(1, 1)
-        quantize_h(0, 512, 768)
-        quantize_xg(1, 768, 1024)
+        quantize_h(0, 0, 512)
+        quantize_xg(1, 512, 768)
         make_h(1, 0, 256, 0, 256)
-        project(1, 0, 512, 768, 0)
-        make_h(1, 256, 512, 256, 384)
+        tower_pass(0, 0, 256, 0, 2, 0)
+        tower_pass(0, 0, 256, 2, 4, 1)
+        make_h(0, 512, 768, 512, 640)
         quantize_h(1, 0, 256)
         finish(0, 256, 0, 2, False)
         finish(0, 256, 2, 4, False)
+        make_h(0, 512, 768, 640, 768)
+        project(1, 0, 512, 768, 4)
+        make_h(1, 256, 512, 256, 384)
+        quantize_h(0, 512, 768)
         make_h(1, 256, 512, 384, 512)
         tower_pass(0, 256, 512, 0, 2, 2)
         tower_pass(0, 256, 512, 2, 4, 3)
+        quantize_xg(1, 768, 1024)
         make_h(1, 512, 768, 512, 640)
         quantize_h(1, 256, 512)
         finish(256, 512, 0, 2, False)
         finish(256, 512, 2, 4, False)
-        project(1, 0, 768, 1024, 4)
+        project(1, 0, 768, 1024, 0)
         make_h(1, 512, 768, 640, 768)
-        tower_pass(0, 512, 768, 0, 2, 0)
-        tower_pass(0, 512, 768, 2, 4, 1)
-        make_h(0, 768, 1024, 768, 896)
+        tower_pass(0, 512, 768, 0, 2, 4)
+        tower_pass(0, 512, 768, 2, 4, 5)
+        make_h(0, 768, 896, 768, 896)
         quantize_h(1, 512, 768)
         finish(512, 768, 0, 2, False)
         finish(512, 768, 2, 4, False)
-        make_h(0, 768, 1024, 896, 1024)
         make_h(1, 768, 896, 768, 896)
-        quantize_h(0, 768, 1024)
+        quantize_h(0, 768, 896)
         tower_pass(0, 768, 896, 0, 4, 6)
-        tower_pass(0, 896, 1024, 0, 2, 7)
-        tower_pass(0, 896, 1024, 2, 4, 2)
+        make_h(0, 896, 1024, 896, 1024)
         quantize_h(1, 768, 896)
         finish(768, 896, 0, 4, False)
         make_h(1, 896, 1024, 896, 1024)
+        quantize_h(0, 896, 1024)
+        tower_pass(0, 896, 1024, 0, 2, 7)
+        tower_pass(0, 896, 1024, 2, 4, 2)
         quantize_h(1, 896, 1024)
         finish(896, 1024, 0, 2, True)
         finish(896, 1024, 2, 4, False)

@@ -38,26 +38,26 @@ def tile_list_interest_user_gate_kernel(
         users = lists.tile([P, S // 16], U16, name="users")
         clicks = lists.tile([P, S // 16], U16, name="clicks")
 
-        tab_w = keep.tile([P, T], U32, name="tab_w", align_bytes=64)
-        tab_s = keep.tile([P, T], U8, name="tab_s", align_bytes=64)
-        v_w = keep.tile([P, S], U32, name="v_w", align_bytes=64)
-        v_s = keep.tile([P, S], U8, name="v_s", align_bytes=64)
-        wg_w_raw = keep.tile([P, 2 * H], U8, name="wg_w_raw", align_bytes=64)
-        wg_s_raw = keep.tile([P, H], U8, name="wg_s_raw", align_bytes=64)
-        wg_w = keep.tile([P, 2 * H], U8, name="wg_w", align_bytes=64)
-        wg_s = keep.tile([P, H], U8, name="wg_s", align_bytes=64)
-        wgt_sb = keep.tile([P, S], F32, name="wgt_sb", align_bytes=64)
-        wgt_raw = keep.tile([P, P], F32, name="wgt_raw", align_bytes=64)
-        ident = keep.tile([P, P], F32, name="ident", align_bytes=64)
-        bg_sb = keep.tile([P, 2, 8], F32, name="bg_sb", align_bytes=64)
-        picked = [keep.tile([P, PACK, S], F32, name="picked%d" % a, align_bytes=64) for a in range(2)]
-        gate = [keep.tile([P, PACK, S], F32, name="gate%d" % h, align_bytes=64) for h in range(2)]
-        xg_w = [keep.tile([P, S], U32, name="xg_w%d" % a, align_bytes=64) for a in range(2)]
-        xg_s = [keep.tile([P, S], U8, name="xg_s%d" % a, align_bytes=64) for a in range(2)]
-        wp_w = [keep.tile([P, H], U32, name="wp_w%d" % a, align_bytes=64) for a in range(2)]
-        wp_s = [keep.tile([P, H], U8, name="wp_s%d" % a, align_bytes=64) for a in range(2)]
-        h_w = [keep.tile([P, S], U32, name="h_w%d" % h, align_bytes=64) for h in range(2)]
-        h_s = [keep.tile([P, S], U8, name="h_s%d" % h, align_bytes=64) for h in range(2)]
+        tab_w = keep.tile([P, T], U32, name="tab_w", align_bytes=256)
+        tab_s = keep.tile([P, T], U8, name="tab_s", align_bytes=256)
+        v_w = keep.tile([P, S], U32, name="v_w", align_bytes=256)
+        v_s = keep.tile([P, S], U8, name="v_s", align_bytes=256)
+        wg_w_raw = keep.tile([P, 2 * H], U8, name="wg_w_raw", align_bytes=256)
+        wg_s_raw = keep.tile([P, H], U8, name="wg_s_raw", align_bytes=256)
+        wg_w = keep.tile([P, 2 * H], U8, name="wg_w", align_bytes=256)
+        wg_s = keep.tile([P, H], U8, name="wg_s", align_bytes=256)
+        wgt_sb = keep.tile([P, S], F32, name="wgt_sb", align_bytes=256)
+        wgt_raw = keep.tile([P, P], F32, name="wgt_raw", align_bytes=256)
+        ident = keep.tile([P, P], F32, name="ident", align_bytes=256)
+        bg_sb = keep.tile([P, 2, 8], F32, name="bg_sb", align_bytes=256)
+        picked = [keep.tile([P, PACK, S], F32, name="picked%d" % a, align_bytes=256) for a in range(2)]
+        gate = [keep.tile([P, PACK, S], F32, name="gate%d" % h, align_bytes=256) for h in range(2)]
+        xg_w = [keep.tile([P, S], U32, name="xg_w%d" % a, align_bytes=256) for a in range(2)]
+        xg_s = [keep.tile([P, S], U8, name="xg_s%d" % a, align_bytes=256) for a in range(2)]
+        wp_w = [keep.tile([P, H], U32, name="wp_w%d" % a, align_bytes=256) for a in range(2)]
+        wp_s = [keep.tile([P, H], U8, name="wp_s%d" % a, align_bytes=256) for a in range(2)]
+        h_w = [keep.tile([P, S], U32, name="h_w%d" % h, align_bytes=256) for h in range(2)]
+        h_s = [keep.tile([P, S], U8, name="h_s%d" % h, align_bytes=256) for h in range(2)]
 
         def load_scale_rows(plane, rows, quadrants, queue):
             for q in quadrants:
@@ -66,14 +66,14 @@ def tile_list_interest_user_gate_kernel(
         planes = {}
 
         def load_plane(a, t):
-            planes[a, t] = stream.tile([P, T], F32, name="plane", tag="stream", align_bytes=64)
+            planes[a, t] = stream.tile([P, T], F32, name="plane", tag="stream", align_bytes=256)
             rows = xT[KP * a : KP * (a + 1), :].rearrange("(p i) c -> p i c", i=PACK)
             nc.sync.dma_start(out=planes[a, t][:], in_=rows[:, t, :])
 
         wp_raw = {}
 
         def load_wp(h, a, lo=0, hi=KP):
-            wp_raw[h, a, lo] = stream.tile([P, PACK, hi - lo], F32, name="wp_raw", tag="stream", align_bytes=64)
+            wp_raw[h, a, lo] = stream.tile([P, PACK, hi - lo], F32, name="wp_raw", tag="stream", align_bytes=256)
             rows = wp[KP * a : KP * (a + 1), KP * h + lo : KP * h + hi].rearrange("(p i) c -> p i c", i=PACK)
             nc.sync.dma_start(out=wp_raw[h, a, lo][:], in_=rows)
 
@@ -82,7 +82,7 @@ def tile_list_interest_user_gate_kernel(
                 picked[a][:, t, lo:hi], planes[a, t][:].indirect(clicks[:, lo // 16 : hi // 16]), wgt_sb[:, lo:hi], MULT
             )
 
-        xg_bf = [keep.tile([P, PACK * S], BF16, name="xg_bf%d" % a, align_bytes=64) for a in range(2)]
+        xg_bf = [keep.tile([P, PACK * S], BF16, name="xg_bf%d" % a, align_bytes=256) for a in range(2)]
 
         def round_xg(a, lo, hi):
             nc.scalar.copy(
@@ -97,7 +97,7 @@ def tile_list_interest_user_gate_kernel(
 
         def round_wp(h, a, lo=0, hi=KP):
             if lo == 0:
-                wp_bf[h, a] = stage.tile([P, PACK * KP], BF16, name="wp_bf", tag="wp_bf", bufs=2, align_bytes=64)
+                wp_bf[h, a] = stage.tile([P, PACK * KP], BF16, name="wp_bf", tag="wp_bf", bufs=2, align_bytes=256)
             nc.scalar.copy(
                 out=wp_bf[h, a][:].rearrange("p (t m i) -> p m i t", t=PACK, i=PACK)[:, lo // PACK : hi // PACK],
                 in_=wp_raw[h, a, lo][:].rearrange("p i (m t) -> p m i t", t=PACK),
@@ -152,7 +152,7 @@ def tile_list_interest_user_gate_kernel(
 
         def make_h(h, lo, hi, first, last):
             if first == lo:
-                h_bf[h, lo] = stage.tile([P, PACK * (hi - lo)], BF16, name="h_bf", tag="h_bf", bufs=4, align_bytes=64)
+                h_bf[h, lo] = stage.tile([P, PACK * (hi - lo)], BF16, name="h_bf", tag="h_bf", bufs=4, align_bytes=256)
             for j0 in range(first, last, JC):
                 project(h, 1, j0, j0 + JC, None)
                 nc.vector.tensor_tensor(
@@ -184,7 +184,7 @@ def tile_list_interest_user_gate_kernel(
                 )
 
         def store(lo, hi, m0, m1, on_vector):
-            res = stage.tile([P, m1 - m0, hi - lo], F32, name="res", tag="res", bufs=6, align_bytes=64)
+            res = stage.tile([P, m1 - m0, hi - lo], F32, name="res", tag="res", bufs=6, align_bytes=256)
             for m in range(m0, m1):
                 if on_vector:
                     nc.vector.tensor_scalar_add(res[:, m - m0, :], tower[lo, m0][:, m - m0, :], bt_sb[:, m : m + 1])
@@ -198,7 +198,7 @@ def tile_list_interest_user_gate_kernel(
             tower_pass(1, lo, hi, m0, m1, None)
             store(lo, hi, m0, m1, on_vector)
 
-        warm = keep.tile([P, 2], F32, name="warm", align_bytes=64)
+        warm = keep.tile([P, 2], F32, name="warm", align_bytes=256)
         nc.vector.memset(tab_s[:].bitcast(I32), 0)
         nc.gpsimd.memset(wg_s_raw[:].bitcast(I32), 0)
         nc.gpsimd.memset(warm[:, 0:1], 0.0)
@@ -226,18 +226,18 @@ def tile_list_interest_user_gate_kernel(
         load_plane(1, 3)
         load_wp(1, 0, 256, 512)
         load_wp(1, 1)
-        wt_s = stream.tile([P, 2, N], U8, name="wt_s", tag="stream", align_bytes=64)
+        wt_s = stream.tile([P, 2, N], U8, name="wt_s", tag="stream", align_bytes=256)
         nc.gpsimd.memset(wt_s[:].bitcast(I32), 0)
         load_scale_rows(wt_s, wt_rows, range(4), nc.sync)
-        wt_w = stream.tile([P, 2, N], U32, name="wt_w", tag="stream", align_bytes=64)
+        wt_w = stream.tile([P, 2, N], U32, name="wt_w", tag="stream", align_bytes=256)
         nc.sync.dma_start(out=wt_w[:].bitcast(I32), in_=wt_words.rearrange("a p n t -> p a (n t)").bitcast(I32))
-        bt_sb = stream.tile([P, N // P], F32, name="bt_sb", tag="stream", align_bytes=64)
+        bt_sb = stream.tile([P, N // P], F32, name="bt_sb", tag="stream", align_bytes=256)
         with nc.allow_non_contiguous_dma(reason="one bias value for each partition"):
             nc.sync.dma_start(out=bt_sb[:], in_=bt.rearrange("(m p) -> p m", p=P))
         turned = psum.tile([P, P], F32, name="turned", tag="bank0")
         nc.tensor.transpose(turned[:], wgt_raw[:], ident[:])
         for half in range(2):
-            spread = stage.tile([P, PACK, P], F32, name="spread", tag="res", bufs=6, align_bytes=64)
+            spread = stage.tile([P, PACK, P], F32, name="spread", tag="res", bufs=6, align_bytes=256)
             nc.scalar.copy(
                 out=spread[:].rearrange("p b (g u r) -> p b g u r", g=8, r=2),
                 in_=turned[:]

@@ -31,33 +31,32 @@ def tile_list_interest_user_gate_kernel(
     with ExitStack() as ctx:
         lists = ctx.enter_context(tc.tile_pool(name="lists", bufs=1))
         keep = ctx.enter_context(tc.tile_pool(name="keep", bufs=1))
-        stream = ctx.enter_context(tc.tile_pool(name="stream", bufs=7))
         stage = ctx.enter_context(tc.tile_pool(name="stage", bufs=3))
         psum = ctx.enter_context(tc.psum_pool(name="psum", bufs=1))
 
         users = lists.tile([P, S // 16], U16, name="users")
         clicks = lists.tile([P, S // 16], U16, name="clicks")
 
-        tab_w = keep.tile([P, T], U32, name="tab_w", align_bytes=256)
-        tab_s = keep.tile([P, T], U8, name="tab_s", align_bytes=256)
-        v_w = keep.tile([P, S], U32, name="v_w", align_bytes=256)
-        v_s = keep.tile([P, S], U8, name="v_s", align_bytes=256)
-        wg_w_raw = keep.tile([P, 2 * H], U8, name="wg_w_raw", align_bytes=256)
-        wg_s_raw = keep.tile([P, H], U8, name="wg_s_raw", align_bytes=256)
-        wg_w = keep.tile([P, 2 * H], U8, name="wg_w", align_bytes=256)
-        wg_s = keep.tile([P, H], U8, name="wg_s", align_bytes=256)
-        wgt_sb = keep.tile([P, S], F32, name="wgt_sb", align_bytes=256)
-        wgt_raw = keep.tile([P, P], F32, name="wgt_raw", align_bytes=256)
-        ident = keep.tile([P, P], F32, name="ident", align_bytes=256)
-        bg_sb = keep.tile([P, 2, 8], F32, name="bg_sb", align_bytes=256)
-        picked = [keep.tile([P, PACK, S], F32, name="picked%d" % a, align_bytes=256) for a in range(2)]
-        gate = [keep.tile([P, PACK, S], F32, name="gate%d" % h, align_bytes=256) for h in range(2)]
-        xg_w = [keep.tile([P, S], U32, name="xg_w%d" % a, align_bytes=256) for a in range(2)]
-        xg_s = [keep.tile([P, S], U8, name="xg_s%d" % a, align_bytes=256) for a in range(2)]
-        wp_w = [keep.tile([P, H], U32, name="wp_w%d" % a, align_bytes=256) for a in range(2)]
-        wp_s = [keep.tile([P, H], U8, name="wp_s%d" % a, align_bytes=256) for a in range(2)]
-        h_w = [keep.tile([P, S], U32, name="h_w%d" % h, align_bytes=256) for h in range(2)]
-        h_s = [keep.tile([P, S], U8, name="h_s%d" % h, align_bytes=256) for h in range(2)]
+        tab_w = keep.tile([P, T], U32, name="tab_w", align_bytes=64)
+        tab_s = keep.tile([P, T], U8, name="tab_s", align_bytes=64)
+        v_w = {0: keep.tile([P, BANK], U32, name="v_w0", align_bytes=64)}
+        v_s = keep.tile([P, S], U8, name="v_s", align_bytes=64)
+        wg_w_raw = keep.tile([P, 2 * H], U8, name="wg_w_raw", align_bytes=64)
+        wg_s_raw = keep.tile([P, H], U8, name="wg_s_raw", align_bytes=64)
+        wg_w = keep.tile([P, 2 * H], U8, name="wg_w", align_bytes=64)
+        wg_s = keep.tile([P, H], U8, name="wg_s", align_bytes=64)
+        wgt_sb = keep.tile([P, S], F32, name="wgt_sb", align_bytes=64)
+        wgt_raw = keep.tile([P, P], F32, name="wgt_raw", align_bytes=64)
+        ident = keep.tile([P, P], F32, name="ident", align_bytes=64)
+        bg_sb = keep.tile([P, 2, 8], F32, name="bg_sb", align_bytes=64)
+        picked = [keep.tile([P, PACK, S], F32, name="picked%d" % a, align_bytes=64) for a in range(2)]
+        gate = {(h, lo): keep.tile([P, PACK, BANK], F32, name="gate%d_%d" % (h, lo), align_bytes=64) for h in range(2) for lo in (0, BANK)}
+        xg_w = {}
+        xg_s = [keep.tile([P, S], U8, name="xg_s%d" % a, align_bytes=64) for a in range(2)]
+        wp_w = {}
+        wp_s = [keep.tile([P, H], U8, name="wp_s%d" % a, align_bytes=64) for a in range(2)]
+        h_w = [keep.tile([P, S], U32, name="h_w%d" % h, align_bytes=64) for h in range(2)]
+        h_s = [keep.tile([P, S], U8, name="h_s%d" % h, align_bytes=64) for h in range(2)]
 
         def load_scale_rows(plane, rows, quadrants, queue):
             for q in quadrants:
@@ -65,15 +64,15 @@ def tile_list_interest_user_gate_kernel(
 
         planes = {}
 
-        def load_plane(a, t):
-            planes[a, t] = stream.tile([P, T], F32, name="plane", tag="stream", align_bytes=256)
+        def load_plane(a, t, slot):
+            planes[a, t] = keep.tile([P, T], F32, name="plane", tag="slot%d" % slot, align_bytes=64)
             rows = xT[KP * a : KP * (a + 1), :].rearrange("(p i) c -> p i c", i=PACK)
             nc.sync.dma_start(out=planes[a, t][:], in_=rows[:, t, :])
 
         wp_raw = {}
 
-        def load_wp(h, a, lo=0, hi=KP):
-            wp_raw[h, a, lo] = stream.tile([P, PACK, hi - lo], F32, name="wp_raw", tag="stream", align_bytes=256)
+        def load_wp(h, a, slot, lo=0, hi=KP):
+            wp_raw[h, a, lo] = keep.tile([P, PACK, hi - lo], F32, name="wp_raw", tag="slot%d" % slot, align_bytes=64)
             rows = wp[KP * a : KP * (a + 1), KP * h + lo : KP * h + hi].rearrange("(p i) c -> p i c", i=PACK)
             nc.sync.dma_start(out=wp_raw[h, a, lo][:], in_=rows)
 
@@ -82,30 +81,40 @@ def tile_list_interest_user_gate_kernel(
                 picked[a][:, t, lo:hi], planes[a, t][:].indirect(clicks[:, lo // 16 : hi // 16]), wgt_sb[:, lo:hi], MULT
             )
 
-        xg_bf = [keep.tile([P, PACK * S], BF16, name="xg_bf%d" % a, align_bytes=256) for a in range(2)]
+        xg_bf = {}
 
-        def round_xg(a, lo, hi):
-            nc.scalar.copy(
-                out=xg_bf[a][:, PACK * lo : PACK * hi].rearrange("p (c i t) -> p c t i", i=2, t=PACK),
+        def round_xg(a, lo, hi, copy=nc.scalar.copy, tag=None):
+            xg_bf[a, lo] = keep.tile([P, PACK * (hi - lo)], BF16, name="xg_bf", tag=tag or "xg_bf%d_%d" % (a, lo), align_bytes=64)
+            copy(
+                out=xg_bf[a, lo][:].rearrange("p (c i t) -> p c t i", i=2, t=PACK),
                 in_=picked[a][:, :, lo:hi].rearrange("p t (c i) -> p c t i", i=2),
             )
 
-        def quantize_xg(a, lo, hi):
-            nc.vector.quantize_mx(out=xg_w[a][:, lo:hi].bitcast(FP8X4), scales=xg_s[a][:, lo:hi], in_=xg_bf[a][:, PACK * lo : PACK * hi])
+        def quantize_xg(a, lo, hi, tag=None):
+            codes = tag
+            if codes is None:
+                codes = keep.tile([P, hi - lo], U32, name="xg_w", tag="xg_w%d_%d" % (a, lo), align_bytes=64)[:]
+            for j0 in range(lo, hi, JC):
+                xg_w[a, j0] = codes[:, j0 - lo : j0 - lo + JC]
+            nc.vector.quantize_mx(out=codes.bitcast(FP8X4), scales=xg_s[a][:, lo:hi], in_=xg_bf[a, lo][:])
 
         wp_bf = {}
 
-        def round_wp(h, a, lo=0, hi=KP):
+        def round_wp(h, a, tag, lo=0, hi=KP, copy=nc.scalar.copy):
             if lo == 0:
-                wp_bf[h, a] = stage.tile([P, PACK * KP], BF16, name="wp_bf", tag="wp_bf", bufs=2, align_bytes=256)
-            nc.scalar.copy(
+                wp_bf[h, a] = keep.tile([P, PACK * KP], BF16, name="wp_bf", tag=tag, align_bytes=64)
+            copy(
                 out=wp_bf[h, a][:].rearrange("p (t m i) -> p m i t", t=PACK, i=PACK)[:, lo // PACK : hi // PACK],
                 in_=wp_raw[h, a, lo][:].rearrange("p i (m t) -> p m i t", t=PACK),
             )
 
-        def quantize_wp(h, a):
+        def quantize_wp(h, a, tag=None):
             cols = slice(KP * h, KP * (h + 1))
-            nc.vector.quantize_mx(out=wp_w[a][:, cols].bitcast(FP8X4), scales=wp_s[a][:, cols], in_=wp_bf[h, a][:])
+            if tag is None:
+                wp_w[h, a] = keep.tile([P, KP], U32, name="wp_w", tag="wp_w%d%d" % (h, a), align_bytes=64)[:]
+            else:
+                wp_w[h, a] = tag
+            nc.vector.quantize_mx(out=wp_w[h, a].bitcast(FP8X4), scales=wp_s[a][:, cols], in_=wp_bf[h, a][:])
 
         def order_wg_scales(h):
             cols = slice(KP * h, KP * (h + 1))
@@ -115,19 +124,19 @@ def tile_list_interest_user_gate_kernel(
             )
 
         def make_gate(h, t, lo):
-            pre = psum.tile([P, BANK], F32, name="pre", tag="bank%d" % (t + PACK * (lo // BANK)))
+            pre = psum.tile([P, BANK], F32, name="pre", tag="bank%d" % (t + PACK * h))
             c0 = KP * h + P * t
             nc.tensor.matmul_mx(
                 out=pre[:],
                 lhsT=wg_w[:, 2 * c0 : 2 * (c0 + P)].bitcast(FP4X4),
                 lhsT_scale=wg_s[:, c0 : c0 + P],
-                rhs=v_w[:, lo : lo + BANK].bitcast(FP8X4),
+                rhs=v_w[lo][:].bitcast(FP8X4),
                 rhs_scale=v_s[:, lo : lo + BANK],
                 start=True,
                 stop=True,
             )
             nc.scalar.activation(
-                out=gate[h][:, t, lo : lo + BANK], in_=pre[:], func=ACT.Sigmoid, bias=bg_sb[:, h, t : t + 1]
+                out=gate[h, lo][:, t, :], in_=pre[:], func=ACT.Sigmoid, bias=bg_sb[:, h, t : t + 1]
             )
 
         h_bf = {}
@@ -142,23 +151,22 @@ def tile_list_interest_user_gate_kernel(
                     c0 = KP * h + P * t
                     nc.tensor.matmul_mx(
                         out=acc[h, j0][:, t, :],
-                        lhsT=wp_w[a][:, c0 : c0 + P].bitcast(FP8X4),
+                        lhsT=wp_w[h, a][:, P * t : P * (t + 1)].bitcast(FP8X4),
                         lhsT_scale=wp_s[a][:, c0 : c0 + P],
-                        rhs=xg_w[a][:, j0 : j0 + JC].bitcast(FP8X4),
+                        rhs=xg_w[a, j0].bitcast(FP8X4),
                         rhs_scale=xg_s[a][:, j0 : j0 + JC],
                         start=(a == 0 and t == 0),
                         stop=(a == 1 and t == PACK - 1),
                     )
 
-        def make_h(h, lo, hi, first, last):
+        def multiply(h, lo, hi, first, last):
             if first == lo:
-                h_bf[h, lo] = stage.tile([P, PACK * (hi - lo)], BF16, name="h_bf", tag="h_bf", bufs=4, align_bytes=256)
+                h_bf[h, lo] = stage.tile([P, PACK * (hi - lo)], BF16, name="h_bf", tag="h_bf", bufs=4, align_bytes=64)
             for j0 in range(first, last, JC):
-                project(h, 1, j0, j0 + JC, None)
                 nc.vector.tensor_tensor(
                     h_bf[h, lo][:, PACK * (j0 - lo) : PACK * (j0 - lo + JC)].rearrange("p (c i t) -> p c t i", i=2, t=PACK),
                     acc[h, j0][:].rearrange("p t (c i) -> p c t i", i=2),
-                    gate[h][:, :, j0 : j0 + JC].rearrange("p t (c i) -> p c t i", i=2),
+                    gate[h, j0 // BANK * BANK][:, :, j0 % BANK : j0 % BANK + JC].rearrange("p t (c i) -> p c t i", i=2),
                     MULT,
                 )
 
@@ -184,7 +192,7 @@ def tile_list_interest_user_gate_kernel(
                 )
 
         def store(lo, hi, m0, m1, on_vector):
-            res = stage.tile([P, m1 - m0, hi - lo], F32, name="res", tag="res", bufs=6, align_bytes=256)
+            res = stage.tile([P, m1 - m0, hi - lo], F32, name="res", tag="res", bufs=8, align_bytes=64)
             for m in range(m0, m1):
                 if on_vector:
                     nc.vector.tensor_scalar_add(res[:, m - m0, :], tower[lo, m0][:, m - m0, :], bt_sb[:, m : m + 1])
@@ -198,7 +206,7 @@ def tile_list_interest_user_gate_kernel(
             tower_pass(1, lo, hi, m0, m1, None)
             store(lo, hi, m0, m1, on_vector)
 
-        warm = keep.tile([P, 2], F32, name="warm", align_bytes=256)
+        warm = keep.tile([P, 2], F32, name="warm", align_bytes=64)
         nc.vector.memset(tab_s[:].bitcast(I32), 0)
         nc.gpsimd.memset(wg_s_raw[:].bitcast(I32), 0)
         nc.gpsimd.memset(warm[:, 0:1], 0.0)
@@ -213,31 +221,31 @@ def tile_list_interest_user_gate_kernel(
         load_scale_rows(wg_s_raw, wg_scales[0], range(4), nc.sync)
         nc.sync.dma_start(clicks[:], offs2)
         nc.sync.dma_start(out=bg_sb[:, :, 0:PACK], in_=bg.rearrange("(h p t) -> p h t", h=2, t=PACK))
-        load_plane(0, 0)
-        load_plane(0, 1)
-        load_plane(0, 2)
-        load_plane(0, 3)
-        load_plane(1, 0)
-        load_plane(1, 1)
-        load_plane(1, 2)
-        load_wp(0, 0)
-        load_wp(0, 1)
-        load_wp(1, 0, 0, 256)
-        load_plane(1, 3)
-        load_wp(1, 0, 256, 512)
-        load_wp(1, 1)
-        wt_s = stream.tile([P, 2, N], U8, name="wt_s", tag="stream", align_bytes=256)
+        load_plane(0, 0, 0)
+        load_plane(0, 1, 1)
+        load_plane(0, 2, 2)
+        load_plane(0, 3, 3)
+        load_plane(1, 0, 4)
+        load_plane(1, 1, 5)
+        load_plane(1, 2, 6)
+        load_wp(0, 0, 0)
+        load_wp(0, 1, 1)
+        load_wp(1, 0, 2, 0, 256)
+        load_plane(1, 3, 3)
+        load_wp(1, 0, 4, 256, 512)
+        load_wp(1, 1, 5)
+        wt_s = keep.tile([P, 2, N], U8, name="wt_s", tag="slot6", align_bytes=64)
         nc.gpsimd.memset(wt_s[:].bitcast(I32), 0)
         load_scale_rows(wt_s, wt_rows, range(4), nc.sync)
-        wt_w = stream.tile([P, 2, N], U32, name="wt_w", tag="stream", align_bytes=256)
+        wt_w = keep.tile([P, 2, N], U32, name="wt_w", tag="slot0", align_bytes=64)
         nc.sync.dma_start(out=wt_w[:].bitcast(I32), in_=wt_words.rearrange("a p n t -> p a (n t)").bitcast(I32))
-        bt_sb = stream.tile([P, N // P], F32, name="bt_sb", tag="stream", align_bytes=256)
+        bt_sb = keep.tile([P, N // P], F32, name="bt_sb", tag="slot1", align_bytes=64)
         with nc.allow_non_contiguous_dma(reason="one bias value for each partition"):
             nc.sync.dma_start(out=bt_sb[:], in_=bt.rearrange("(m p) -> p m", p=P))
         turned = psum.tile([P, P], F32, name="turned", tag="bank0")
         nc.tensor.transpose(turned[:], wgt_raw[:], ident[:])
         for half in range(2):
-            spread = stage.tile([P, PACK, P], F32, name="spread", tag="res", bufs=6, align_bytes=256)
+            spread = stage.tile([P, PACK, P], F32, name="spread", tag="res", bufs=8, align_bytes=64)
             nc.scalar.copy(
                 out=spread[:].rearrange("p b (g u r) -> p b g u r", g=8, r=2),
                 in_=turned[:]
@@ -254,82 +262,101 @@ def tile_list_interest_user_gate_kernel(
             in_=wg_w_raw[:].bitcast(U16).rearrange("p (h m t) -> p h t m", h=2, t=PACK),
         )
         nc.vector.tensor_copy(v_s[:], tab_s[:].indirect(users[:]))
-        nc.vector.tensor_copy(v_w[:, 0:512], tab_w[:].indirect(users[:, 0:32]))
+        nc.vector.tensor_copy(v_w[0][:], tab_w[:].indirect(users[:, 0:32]))
         order_wg_scales(0)
-        nc.vector.tensor_copy(v_w[:, 512:1024], tab_w[:].indirect(users[:, 32:64]))
         order_wg_scales(1)
-        for h in range(2):
-            for lo in range(0, S, BANK):
+        v_w[BANK] = keep.tile([P, BANK], U32, name="v_w1", tag="wg_s_raw", align_bytes=64)
+        nc.vector.tensor_copy(v_w[BANK][:], tab_w[:].indirect(users[:, 32:64]))
+        for lo in range(0, S, BANK):
+            for h in range(2):
                 for t in range(PACK):
                     make_gate(h, t, lo)
-        for t in range(PACK):
+        for t in range(PACK - 1):
             gather(0, t, 0, S)
+        gather(0, 3, 0, 512)
+        gather(0, 3, 512, 1024)
         round_xg(0, 0, 512)
         round_xg(0, 512, 1024)
-        round_wp(0, 0)
-        round_wp(0, 1)
-        round_wp(1, 0, 0, 256)
+        round_wp(0, 0, "wp_a")
+        round_wp(0, 1, "picked0")
+        round_wp(1, 0, "tab_w", 0, 256)
         gather(1, 0, 0, S)
+        quantize_xg(0, 0, 512)
         gather(1, 1, 0, S)
+        quantize_xg(0, 512, 1024)
         gather(1, 2, 0, S)
-        quantize_xg(0, 0, S)
         quantize_wp(0, 0)
         project(0, 0, 0, S, 0)
-        gather(1, 3, 0, 256)
         quantize_wp(0, 1)
+        gather(1, 3, 0, 256)
         gather(1, 3, 256, 512)
         gather(1, 3, 512, 768)
-        round_xg(1, 0, 256)
-        quantize_xg(1, 0, 256)
         gather(1, 3, 768, 1024)
+        round_xg(1, 0, 256)
         round_xg(1, 256, 512)
-        round_wp(1, 0, 256, 512)
-        round_wp(1, 1)
+        round_wp(1, 0, None, 256, 512)
+        round_wp(1, 1, "wp_a")
         round_xg(1, 512, 768)
         round_xg(1, 768, 1024)
+        quantize_xg(1, 0, 256)
+        project(0, 1, 0, 256, None)
         quantize_xg(1, 256, 512)
-        make_h(0, 0, 512, 0, 384)
+        project(0, 1, 256, 512, None)
+        multiply(0, 0, 512, 0, 256)
         quantize_wp(1, 0)
         project(1, 0, 0, 256, 0)
-        make_h(0, 0, 512, 384, 512)
+        multiply(0, 0, 512, 256, 512)
         project(1, 0, 256, 512, 2)
         quantize_wp(1, 1)
+        project(1, 1, 0, 256, None)
         quantize_h(0, 0, 512)
         quantize_xg(1, 512, 768)
-        make_h(1, 0, 256, 0, 256)
+        multiply(1, 0, 256, 0, 256)
         tower_pass(0, 0, 256, 0, 2, 0)
         tower_pass(0, 0, 256, 2, 4, 1)
-        make_h(0, 512, 768, 512, 640)
+        project(0, 1, 512, 640, None)
+        multiply(0, 512, 768, 512, 640)
         quantize_h(1, 0, 256)
         finish(0, 256, 0, 2, False)
         finish(0, 256, 2, 4, False)
-        make_h(0, 512, 768, 640, 768)
+        project(0, 1, 640, 768, None)
+        multiply(0, 512, 768, 640, 768)
         project(1, 0, 512, 768, 4)
-        make_h(1, 256, 512, 256, 384)
+        project(1, 1, 256, 384, None)
+        multiply(1, 256, 512, 256, 384)
         quantize_h(0, 512, 768)
-        make_h(1, 256, 512, 384, 512)
+        project(1, 1, 384, 512, None)
+        multiply(1, 256, 512, 384, 512)
         tower_pass(0, 256, 512, 0, 2, 2)
         tower_pass(0, 256, 512, 2, 4, 3)
         quantize_xg(1, 768, 1024)
-        make_h(1, 512, 768, 512, 640)
+        project(1, 1, 512, 640, None)
+        multiply(1, 512, 768, 512, 640)
         quantize_h(1, 256, 512)
         finish(256, 512, 0, 2, False)
         finish(256, 512, 2, 4, False)
         project(1, 0, 768, 1024, 0)
-        make_h(1, 512, 768, 640, 768)
+        project(1, 1, 640, 768, None)
+        multiply(1, 512, 768, 640, 768)
         tower_pass(0, 512, 768, 0, 2, 4)
         tower_pass(0, 512, 768, 2, 4, 5)
-        make_h(0, 768, 896, 768, 896)
+        project(0, 1, 768, 896, None)
+        multiply(0, 768, 896, 768, 896)
         quantize_h(1, 512, 768)
         finish(512, 768, 0, 2, False)
         finish(512, 768, 2, 4, False)
-        make_h(1, 768, 896, 768, 896)
+        project(1, 1, 768, 896, None)
+        multiply(1, 768, 896, 768, 896)
         quantize_h(0, 768, 896)
-        tower_pass(0, 768, 896, 0, 4, 6)
-        make_h(0, 896, 1024, 896, 1024)
+        tower_pass(0, 768, 896, 0, 2, 6)
+        tower_pass(0, 768, 896, 2, 4, 3)
+        project(0, 1, 896, 1024, None)
+        multiply(0, 896, 1024, 896, 1024)
         quantize_h(1, 768, 896)
-        finish(768, 896, 0, 4, False)
-        make_h(1, 896, 1024, 896, 1024)
+        finish(768, 896, 0, 2, False)
+        finish(768, 896, 2, 4, False)
+        project(1, 1, 896, 1024, None)
+        multiply(1, 896, 1024, 896, 1024)
         quantize_h(0, 896, 1024)
         tower_pass(0, 896, 1024, 0, 2, 7)
         tower_pass(0, 896, 1024, 2, 4, 2)

@@ -15,6 +15,7 @@ U8 = mybir.dt.uint8
 FP8X4 = mybir.dt.float8_e4m3fn_x4
 FP4X4 = mybir.dt.float4_e2m1fn_x4
 MULT = mybir.AluOpType.mult
+ADD = mybir.AluOpType.add
 ACT = mybir.ActivationFunctionType
 
 P = 128
@@ -37,26 +38,29 @@ def tile_list_interest_user_gate_kernel(
         users = lists.tile([P, S // 16], U16, name="users")
         clicks = lists.tile([P, S // 16], U16, name="clicks")
 
-        tab_w = keep.tile([P, T], U32, name="tab_w", align_bytes=64)
-        tab_s = keep.tile([P, T], U8, name="tab_s", align_bytes=64)
-        v_w = {0: keep.tile([P, BANK], U32, name="v_w0", align_bytes=64)}
-        v_s = keep.tile([P, S], U8, name="v_s", align_bytes=64)
-        wg_w_raw = keep.tile([P, 2 * H], U8, name="wg_w_raw", align_bytes=64)
-        wg_s_raw = keep.tile([P, H], U8, name="wg_s_raw", align_bytes=64)
-        wg_w = keep.tile([P, 2 * H], U8, name="wg_w", align_bytes=64)
-        wg_s = keep.tile([P, H], U8, name="wg_s", align_bytes=64)
-        wgt_sb = keep.tile([P, S], F32, name="wgt_sb", align_bytes=64)
-        wgt_raw = keep.tile([P, P], F32, name="wgt_raw", align_bytes=64)
-        ident = keep.tile([P, P], F32, name="ident", align_bytes=64)
-        bg_sb = keep.tile([P, 2, 8], F32, name="bg_sb", align_bytes=64)
-        picked = [keep.tile([P, PACK, S], F32, name="picked%d" % a, align_bytes=64) for a in range(2)]
-        gate = {(h, lo): keep.tile([P, PACK, BANK], F32, name="gate%d_%d" % (h, lo), align_bytes=64) for h in range(2) for lo in (0, BANK)}
+        tab_w = keep.tile([P, T], U32, name="tab_w", align_bytes=256)
+        tab_s = keep.tile([P, T], U8, name="tab_s", align_bytes=256)
+        v_w = keep.tile([P, S], U32, name="v_w", align_bytes=256)
+        v_s = keep.tile([P, S], U8, name="v_s", align_bytes=256)
+        wg_w_raw = keep.tile([P, 2 * H], U8, name="wg_w_raw", align_bytes=256)
+        wg_s_raw = keep.tile([P, H], U8, name="wg_s_raw", align_bytes=256)
+        wg_w = keep.tile([P, 2 * H], U8, name="wg_w", align_bytes=256)
+        wg_s = keep.tile([P, H], U8, name="wg_s", align_bytes=256)
+        wgt_sb = keep.tile([P, S], F32, name="wgt_sb", align_bytes=256)
+        wgt_last = keep.tile([P, BANK], F32, name="wgt_last", tag="wp_w01", align_bytes=256)
+        wgt_mid = keep.tile([P, BANK], F32, name="wgt_mid", tag="xg_w0_0", align_bytes=256)
+        wgt_raw = keep.tile([P, P], F32, name="wgt_raw", align_bytes=256)
+        ident = keep.tile([P, P], F32, name="ident", align_bytes=256)
+        bg_sb = keep.tile([P, 2, 8], F32, name="bg_sb", align_bytes=256)
+        picked = [keep.tile([P, PACK, S], F32, name="picked%d" % a, align_bytes=256) for a in range(2)]
+        gate = {(h, lo): keep.tile([P, PACK, BANK], F32, name="gate%d_%d" % (h, lo), align_bytes=256) for h in range(2) for lo in (0, BANK)}
         xg_w = {}
-        xg_s = [keep.tile([P, S], U8, name="xg_s%d" % a, align_bytes=64) for a in range(2)]
+        xg_codes = {}
+        xg_s = [keep.tile([P, S], U8, name="xg_s%d" % a, align_bytes=256) for a in range(2)]
         wp_w = {}
-        wp_s = [keep.tile([P, H], U8, name="wp_s%d" % a, align_bytes=64) for a in range(2)]
-        h_w = [keep.tile([P, S], U32, name="h_w%d" % h, align_bytes=64) for h in range(2)]
-        h_s = [keep.tile([P, S], U8, name="h_s%d" % h, align_bytes=64) for h in range(2)]
+        wp_s = [keep.tile([P, H], U8, name="wp_s%d" % a, align_bytes=256) for a in range(2)]
+        h_w = [keep.tile([P, S], U32, name="h_w%d" % h, align_bytes=256) for h in range(2)]
+        h_s = [keep.tile([P, S], U8, name="h_s%d" % h, align_bytes=256) for h in range(2)]
 
         def load_scale_rows(plane, rows, quadrants, queue):
             for q in quadrants:
@@ -65,35 +69,39 @@ def tile_list_interest_user_gate_kernel(
         planes = {}
 
         def load_plane(a, t, slot):
-            planes[a, t] = keep.tile([P, T], F32, name="plane", tag="slot%d" % slot, align_bytes=64)
+            planes[a, t] = keep.tile([P, T], F32, name="plane", tag="slot%d" % slot, align_bytes=256)
             rows = xT[KP * a : KP * (a + 1), :].rearrange("(p i) c -> p i c", i=PACK)
             nc.sync.dma_start(out=planes[a, t][:], in_=rows[:, t, :])
 
         wp_raw = {}
 
         def load_wp(h, a, slot, lo=0, hi=KP):
-            wp_raw[h, a, lo] = keep.tile([P, PACK, hi - lo], F32, name="wp_raw", tag="slot%d" % slot, align_bytes=64)
+            wp_raw[h, a, lo] = keep.tile([P, PACK, hi - lo], F32, name="wp_raw", tag="slot%d" % slot, align_bytes=256)
             rows = wp[KP * a : KP * (a + 1), KP * h + lo : KP * h + hi].rearrange("(p i) c -> p i c", i=PACK)
             nc.sync.dma_start(out=wp_raw[h, a, lo][:], in_=rows)
 
-        def gather(a, t, lo, hi):
+        def gather(a, t, lo, hi, weights=wgt_sb):
             nc.vector.tensor_tensor(
-                picked[a][:, t, lo:hi], planes[a, t][:].indirect(clicks[:, lo // 16 : hi // 16]), wgt_sb[:, lo:hi], MULT
+                picked[a][:, t, lo:hi], planes[a, t][:].indirect(clicks[:, lo // 16 : hi // 16]), weights[:, lo:hi], MULT
             )
 
         xg_bf = {}
 
-        def round_xg(a, lo, hi, copy=nc.scalar.copy, tag=None):
-            xg_bf[a, lo] = keep.tile([P, PACK * (hi - lo)], BF16, name="xg_bf", tag=tag or "xg_bf%d_%d" % (a, lo), align_bytes=64)
+        def round_xg(a, lo, hi, copy=nc.scalar.copy, tag=None, run=2):
+            xg_bf[a, lo] = keep.tile([P, PACK * (hi - lo)], BF16, name="xg_bf", tag=tag or "xg_bf%d_%d" % (a, lo), align_bytes=256)
             copy(
-                out=xg_bf[a, lo][:].rearrange("p (c i t) -> p c t i", i=2, t=PACK),
-                in_=picked[a][:, :, lo:hi].rearrange("p t (c i) -> p c t i", i=2),
+                out=xg_bf[a, lo][:].rearrange("p (c i t) -> p c t i", i=run, t=PACK),
+                in_=picked[a][:, :, lo:hi].rearrange("p t (c i) -> p c t i", i=run),
             )
+
+        def on_gpsimd(out, in_):
+            nc.gpsimd.tensor_scalar(out, in_, 1.0, 0.0, MULT, ADD)
 
         def quantize_xg(a, lo, hi, tag=None):
             codes = tag
             if codes is None:
-                codes = keep.tile([P, hi - lo], U32, name="xg_w", tag="xg_w%d_%d" % (a, lo), align_bytes=64)[:]
+                codes = keep.tile([P, hi - lo], U32, name="xg_w", tag="xg_w%d_%d" % (a, lo), align_bytes=256)[:]
+            xg_codes[a, lo] = codes
             for j0 in range(lo, hi, JC):
                 xg_w[a, j0] = codes[:, j0 - lo : j0 - lo + JC]
             nc.vector.quantize_mx(out=codes.bitcast(FP8X4), scales=xg_s[a][:, lo:hi], in_=xg_bf[a, lo][:])
@@ -102,18 +110,16 @@ def tile_list_interest_user_gate_kernel(
 
         def round_wp(h, a, tag, lo=0, hi=KP, copy=nc.scalar.copy):
             if lo == 0:
-                wp_bf[h, a] = keep.tile([P, PACK * KP], BF16, name="wp_bf", tag=tag, align_bytes=64)
+                wp_bf[h, a] = keep.tile([P, PACK * KP], BF16, name="wp_bf", tag=tag, align_bytes=256)
             copy(
                 out=wp_bf[h, a][:].rearrange("p (t m i) -> p m i t", t=PACK, i=PACK)[:, lo // PACK : hi // PACK],
                 in_=wp_raw[h, a, lo][:].rearrange("p i (m t) -> p m i t", t=PACK),
             )
 
-        def quantize_wp(h, a, tag=None):
+        def quantize_wp(h, a):
             cols = slice(KP * h, KP * (h + 1))
-            if tag is None:
-                wp_w[h, a] = keep.tile([P, KP], U32, name="wp_w", tag="wp_w%d%d" % (h, a), align_bytes=64)[:]
-            else:
-                wp_w[h, a] = tag
+            codes = keep.tile([P, KP], U32, name="wp_w", tag="wp_w%d%d" % (h, a), align_bytes=256)
+            wp_w[h, a] = codes[:]
             nc.vector.quantize_mx(out=wp_w[h, a].bitcast(FP8X4), scales=wp_s[a][:, cols], in_=wp_bf[h, a][:])
 
         def order_wg_scales(h):
@@ -130,7 +136,7 @@ def tile_list_interest_user_gate_kernel(
                 out=pre[:],
                 lhsT=wg_w[:, 2 * c0 : 2 * (c0 + P)].bitcast(FP4X4),
                 lhsT_scale=wg_s[:, c0 : c0 + P],
-                rhs=v_w[lo][:].bitcast(FP8X4),
+                rhs=v_w[:, lo : lo + BANK].bitcast(FP8X4),
                 rhs_scale=v_s[:, lo : lo + BANK],
                 start=True,
                 stop=True,
@@ -138,6 +144,19 @@ def tile_list_interest_user_gate_kernel(
             nc.scalar.activation(
                 out=gate[h, lo][:, t, :], in_=pre[:], func=ACT.Sigmoid, bias=bg_sb[:, h, t : t + 1]
             )
+
+        def warm_up(bank, passes, lo):
+            idle = psum.tile([P, BANK], F32, name="idle", tag="bank%d" % bank)
+            for k in range(passes):
+                nc.tensor.matmul_mx(
+                    out=idle[:],
+                    lhsT=xg_w[0, 0].bitcast(FP8X4),
+                    lhsT_scale=xg_s[0][:, 0:P],
+                    rhs=xg_codes[0, 0][:, lo : lo + BANK].bitcast(FP8X4),
+                    rhs_scale=xg_s[0][:, lo : lo + BANK],
+                    start=True,
+                    stop=True,
+                )
 
         h_bf = {}
 
@@ -161,7 +180,7 @@ def tile_list_interest_user_gate_kernel(
 
         def multiply(h, lo, hi, first, last):
             if first == lo:
-                h_bf[h, lo] = stage.tile([P, PACK * (hi - lo)], BF16, name="h_bf", tag="h_bf", bufs=4, align_bytes=64)
+                h_bf[h, lo] = stage.tile([P, PACK * (hi - lo)], BF16, name="h_bf", tag="h_bf", bufs=4, align_bytes=256)
             for j0 in range(first, last, JC):
                 nc.vector.tensor_tensor(
                     h_bf[h, lo][:, PACK * (j0 - lo) : PACK * (j0 - lo + JC)].rearrange("p (c i t) -> p c t i", i=2, t=PACK),
@@ -192,7 +211,7 @@ def tile_list_interest_user_gate_kernel(
                 )
 
         def store(lo, hi, m0, m1, on_vector):
-            res = stage.tile([P, m1 - m0, hi - lo], F32, name="res", tag="res", bufs=8, align_bytes=64)
+            res = stage.tile([P, m1 - m0, hi - lo], F32, name="res", tag="res", bufs=8, align_bytes=256)
             for m in range(m0, m1):
                 if on_vector:
                     nc.vector.tensor_scalar_add(res[:, m - m0, :], tower[lo, m0][:, m - m0, :], bt_sb[:, m : m + 1])
@@ -206,7 +225,7 @@ def tile_list_interest_user_gate_kernel(
             tower_pass(1, lo, hi, m0, m1, None)
             store(lo, hi, m0, m1, on_vector)
 
-        warm = keep.tile([P, 2], F32, name="warm", align_bytes=64)
+        warm = keep.tile([P, 2], F32, name="warm", align_bytes=256)
         nc.vector.memset(tab_s[:].bitcast(I32), 0)
         nc.gpsimd.memset(wg_s_raw[:].bitcast(I32), 0)
         nc.gpsimd.memset(warm[:, 0:1], 0.0)
@@ -230,22 +249,21 @@ def tile_list_interest_user_gate_kernel(
         load_plane(1, 2, 6)
         load_wp(0, 0, 0)
         load_wp(0, 1, 1)
-        load_wp(1, 0, 2, 0, 256)
-        load_plane(1, 3, 3)
-        load_wp(1, 0, 4, 256, 512)
-        load_wp(1, 1, 5)
-        wt_s = keep.tile([P, 2, N], U8, name="wt_s", tag="slot6", align_bytes=64)
+        load_plane(1, 3, 2)
+        load_wp(1, 0, 3)
+        load_wp(1, 1, 4)
+        wt_s = keep.tile([P, 2, N], U8, name="wt_s", tag="slot5", align_bytes=256)
         nc.gpsimd.memset(wt_s[:].bitcast(I32), 0)
         load_scale_rows(wt_s, wt_rows, range(4), nc.sync)
-        wt_w = keep.tile([P, 2, N], U32, name="wt_w", tag="slot0", align_bytes=64)
+        wt_w = keep.tile([P, 2, N], U32, name="wt_w", tag="slot6", align_bytes=256)
         nc.sync.dma_start(out=wt_w[:].bitcast(I32), in_=wt_words.rearrange("a p n t -> p a (n t)").bitcast(I32))
-        bt_sb = keep.tile([P, N // P], F32, name="bt_sb", tag="slot1", align_bytes=64)
+        bt_sb = keep.tile([P, N // P], F32, name="bt_sb", tag="slot0", align_bytes=256)
         with nc.allow_non_contiguous_dma(reason="one bias value for each partition"):
             nc.sync.dma_start(out=bt_sb[:], in_=bt.rearrange("(m p) -> p m", p=P))
         turned = psum.tile([P, P], F32, name="turned", tag="bank0")
         nc.tensor.transpose(turned[:], wgt_raw[:], ident[:])
         for half in range(2):
-            spread = stage.tile([P, PACK, P], F32, name="spread", tag="res", bufs=8, align_bytes=64)
+            spread = stage.tile([P, PACK, P], F32, name="spread", tag="res", bufs=8, align_bytes=256)
             nc.scalar.copy(
                 out=spread[:].rearrange("p b (g u r) -> p b g u r", g=8, r=2),
                 in_=turned[:]
@@ -257,105 +275,102 @@ def tile_list_interest_user_gate_kernel(
             for b in range(PACK):
                 nc.tensor.transpose(back[:, b, :], spread[:, b, :], ident[:])
             nc.scalar.copy(out=wgt_sb[:, BANK * half : BANK * (half + 1)], in_=back[:].rearrange("p b c -> p (b c)"))
+            if half == 0:
+                nc.scalar.copy(out=wgt_mid[:], in_=back[:].rearrange("p b c -> p (b c)"))
+                nc.scalar.copy(out=wgt_last[:], in_=back[:].rearrange("p b c -> p (b c)"))
         nc.vector.tensor_copy(
             out=wg_w[:].bitcast(U16).rearrange("p (h t m) -> p h t m", h=2, t=PACK),
             in_=wg_w_raw[:].bitcast(U16).rearrange("p (h m t) -> p h t m", h=2, t=PACK),
         )
         nc.vector.tensor_copy(v_s[:], tab_s[:].indirect(users[:]))
-        nc.vector.tensor_copy(v_w[0][:], tab_w[:].indirect(users[:, 0:32]))
+        nc.vector.tensor_copy(v_w[:], tab_w[:].indirect(users[:]))
         order_wg_scales(0)
         order_wg_scales(1)
-        v_w[BANK] = keep.tile([P, BANK], U32, name="v_w1", tag="wg_s_raw", align_bytes=64)
-        nc.vector.tensor_copy(v_w[BANK][:], tab_w[:].indirect(users[:, 32:64]))
         for lo in range(0, S, BANK):
             for h in range(2):
                 for t in range(PACK):
                     make_gate(h, t, lo)
-        for t in range(PACK - 1):
+        for t in range(PACK):
             gather(0, t, 0, S)
-        gather(0, 3, 0, 512)
-        gather(0, 3, 512, 1024)
-        round_xg(0, 0, 512)
-        round_xg(0, 512, 1024)
+        round_xg(0, 0, S)
         round_wp(0, 0, "wp_a")
         round_wp(0, 1, "picked0")
-        round_wp(1, 0, "tab_w", 0, 256)
         gather(1, 0, 0, S)
-        quantize_xg(0, 0, 512)
         gather(1, 1, 0, S)
-        quantize_xg(0, 512, 1024)
-        gather(1, 2, 0, S)
+        gather(1, 2, 0, 512, wgt_mid)
+        gather(1, 2, 512, 1024)
+        quantize_xg(0, 0, S)
         quantize_wp(0, 0)
         project(0, 0, 0, S, 0)
+        gather(1, 3, 0, 256, wgt_last)
+        gather(1, 3, 256, 512, wgt_last)
+        gather(1, 3, 512, 1024)
         quantize_wp(0, 1)
-        gather(1, 3, 0, 256)
-        gather(1, 3, 256, 512)
-        gather(1, 3, 512, 768)
-        gather(1, 3, 768, 1024)
         round_xg(1, 0, 256)
         round_xg(1, 256, 512)
-        round_wp(1, 0, None, 256, 512)
+        round_wp(1, 0, "tab_w")
         round_wp(1, 1, "wp_a")
-        round_xg(1, 512, 768)
-        round_xg(1, 768, 1024)
+        round_xg(1, 768, 1024, tag="slot4")
         quantize_xg(1, 0, 256)
         project(0, 1, 0, 256, None)
         quantize_xg(1, 256, 512)
         project(0, 1, 256, 512, None)
+        round_xg(1, 512, 768, on_gpsimd, tag="xg_bf1_256", run=1)
         multiply(0, 0, 512, 0, 256)
+        warm_up(1, 2, 0)
+        quantize_xg(1, 512, 768)
+        project(0, 1, 512, 768, None)
         quantize_wp(1, 0)
         project(1, 0, 0, 256, 0)
         multiply(0, 0, 512, 256, 512)
         project(1, 0, 256, 512, 2)
+        multiply(0, 512, 768, 512, 640)
+        quantize_h(0, 0, 512)
         quantize_wp(1, 1)
         project(1, 1, 0, 256, None)
-        quantize_h(0, 0, 512)
-        quantize_xg(1, 512, 768)
-        multiply(1, 0, 256, 0, 256)
-        tower_pass(0, 0, 256, 0, 2, 0)
-        tower_pass(0, 0, 256, 2, 4, 1)
-        project(0, 1, 512, 640, None)
-        multiply(0, 512, 768, 512, 640)
+        multiply(0, 512, 768, 640, 768)
+        tower_pass(0, 0, 256, 0, 2, 4)
+        tower_pass(0, 0, 256, 2, 4, 5)
+        project(1, 1, 256, 512, None)
+        quantize_h(0, 512, 768)
+        multiply(1, 0, 256, 0, 128)
+        multiply(1, 0, 256, 128, 256)
+        project(1, 0, 512, 640, 0)
+        project(1, 1, 512, 640, None)
+        quantize_xg(1, 768, 1024)
+        multiply(1, 256, 512, 256, 384)
         quantize_h(1, 0, 256)
         finish(0, 256, 0, 2, False)
         finish(0, 256, 2, 4, False)
-        project(0, 1, 640, 768, None)
-        multiply(0, 512, 768, 640, 768)
-        project(1, 0, 512, 768, 4)
-        project(1, 1, 256, 384, None)
-        multiply(1, 256, 512, 256, 384)
-        quantize_h(0, 512, 768)
-        project(1, 1, 384, 512, None)
+        project(1, 0, 640, 768, 1)
+        project(1, 1, 640, 768, None)
         multiply(1, 256, 512, 384, 512)
         tower_pass(0, 256, 512, 0, 2, 2)
         tower_pass(0, 256, 512, 2, 4, 3)
-        quantize_xg(1, 768, 1024)
-        project(1, 1, 512, 640, None)
         multiply(1, 512, 768, 512, 640)
         quantize_h(1, 256, 512)
         finish(256, 512, 0, 2, False)
         finish(256, 512, 2, 4, False)
-        project(1, 0, 768, 1024, 0)
-        project(1, 1, 640, 768, None)
+        project(0, 1, 768, 1024, None)
         multiply(1, 512, 768, 640, 768)
         tower_pass(0, 512, 768, 0, 2, 4)
         tower_pass(0, 512, 768, 2, 4, 5)
-        project(0, 1, 768, 896, None)
         multiply(0, 768, 896, 768, 896)
         quantize_h(1, 512, 768)
         finish(512, 768, 0, 2, False)
         finish(512, 768, 2, 4, False)
+        project(1, 0, 768, 896, 0)
         project(1, 1, 768, 896, None)
+        project(1, 0, 896, 1024, 1)
+        project(1, 1, 896, 1024, None)
         multiply(1, 768, 896, 768, 896)
         quantize_h(0, 768, 896)
         tower_pass(0, 768, 896, 0, 2, 6)
         tower_pass(0, 768, 896, 2, 4, 3)
-        project(0, 1, 896, 1024, None)
         multiply(0, 896, 1024, 896, 1024)
         quantize_h(1, 768, 896)
         finish(768, 896, 0, 2, False)
         finish(768, 896, 2, 4, False)
-        project(1, 1, 896, 1024, None)
         multiply(1, 896, 1024, 896, 1024)
         quantize_h(0, 896, 1024)
         tower_pass(0, 896, 1024, 0, 2, 7)

@@ -47,15 +47,12 @@ def tile_list_interest_user_gate_kernel(
         wg_w = keep.tile([P, 2 * H], U8, name="wg_w", align_bytes=256)
         wg_s = keep.tile([P, H], U8, name="wg_s", align_bytes=256)
         wgt_sb = keep.tile([P, S], F32, name="wgt_sb", align_bytes=256)
-        wgt_last = keep.tile([P, BANK], F32, name="wgt_last", tag="wp_w01", align_bytes=256)
-        wgt_mid = keep.tile([P, BANK], F32, name="wgt_mid", tag="xg_w0_0", align_bytes=256)
         wgt_raw = keep.tile([P, P], F32, name="wgt_raw", align_bytes=256)
         ident = keep.tile([P, P], F32, name="ident", align_bytes=256)
         bg_sb = keep.tile([P, 2, 8], F32, name="bg_sb", align_bytes=256)
         picked = [keep.tile([P, PACK, S], F32, name="picked%d" % a, align_bytes=256) for a in range(2)]
         gate = {(h, lo): keep.tile([P, PACK, BANK], F32, name="gate%d_%d" % (h, lo), align_bytes=256) for h in range(2) for lo in (0, BANK)}
         xg_w = {}
-        xg_codes = {}
         xg_s = [keep.tile([P, S], U8, name="xg_s%d" % a, align_bytes=256) for a in range(2)]
         wp_w = {}
         wp_s = [keep.tile([P, H], U8, name="wp_s%d" % a, align_bytes=256) for a in range(2)]
@@ -80,9 +77,9 @@ def tile_list_interest_user_gate_kernel(
             rows = wp[KP * a : KP * (a + 1), KP * h + lo : KP * h + hi].rearrange("(p i) c -> p i c", i=PACK)
             nc.sync.dma_start(out=wp_raw[h, a, lo][:], in_=rows)
 
-        def gather(a, t, lo, hi, weights=wgt_sb):
+        def gather(a, t, lo, hi):
             nc.vector.tensor_tensor(
-                picked[a][:, t, lo:hi], planes[a, t][:].indirect(clicks[:, lo // 16 : hi // 16]), weights[:, lo:hi], MULT
+                picked[a][:, t, lo:hi], planes[a, t][:].indirect(clicks[:, lo // 16 : hi // 16]), wgt_sb[:, lo:hi], MULT
             )
 
         xg_bf = {}
@@ -98,10 +95,7 @@ def tile_list_interest_user_gate_kernel(
             nc.gpsimd.tensor_scalar(out, in_, 1.0, 0.0, MULT, ADD)
 
         def quantize_xg(a, lo, hi, tag=None):
-            codes = tag
-            if codes is None:
-                codes = keep.tile([P, hi - lo], U32, name="xg_w", tag="xg_w%d_%d" % (a, lo), align_bytes=256)[:]
-            xg_codes[a, lo] = codes
+            codes = keep.tile([P, hi - lo], U32, name="xg_w", tag=tag or "xg_w%d_%d" % (a, lo), align_bytes=256)[:]
             for j0 in range(lo, hi, JC):
                 xg_w[a, j0] = codes[:, j0 - lo : j0 - lo + JC]
             nc.vector.quantize_mx(out=codes.bitcast(FP8X4), scales=xg_s[a][:, lo:hi], in_=xg_bf[a, lo][:])
@@ -124,7 +118,7 @@ def tile_list_interest_user_gate_kernel(
 
         def order_wg_scales(h):
             cols = slice(KP * h, KP * (h + 1))
-            nc.vector.tensor_copy(
+            nc.gpsimd.tensor_copy(
                 out=wg_s[:, cols].rearrange("p (t m) -> p t m", t=PACK),
                 in_=wg_s_raw[:, cols].rearrange("p (m t) -> p t m", t=PACK),
             )
@@ -144,19 +138,6 @@ def tile_list_interest_user_gate_kernel(
             nc.scalar.activation(
                 out=gate[h, lo][:, t, :], in_=pre[:], func=ACT.Sigmoid, bias=bg_sb[:, h, t : t + 1]
             )
-
-        def warm_up(bank, passes, lo):
-            idle = psum.tile([P, BANK], F32, name="idle", tag="bank%d" % bank)
-            for k in range(passes):
-                nc.tensor.matmul_mx(
-                    out=idle[:],
-                    lhsT=xg_w[0, 0].bitcast(FP8X4),
-                    lhsT_scale=xg_s[0][:, 0:P],
-                    rhs=xg_codes[0, 0][:, lo : lo + BANK].bitcast(FP8X4),
-                    rhs_scale=xg_s[0][:, lo : lo + BANK],
-                    start=True,
-                    stop=True,
-                )
 
         h_bf = {}
 
@@ -248,16 +229,17 @@ def tile_list_interest_user_gate_kernel(
         load_plane(1, 1, 5)
         load_plane(1, 2, 6)
         load_wp(0, 0, 0)
-        load_wp(0, 1, 1)
+        load_wp(0, 1, 1, 0, 256)
         load_plane(1, 3, 2)
-        load_wp(1, 0, 3)
-        load_wp(1, 1, 4)
-        wt_s = keep.tile([P, 2, N], U8, name="wt_s", tag="slot5", align_bytes=256)
+        load_wp(0, 1, 3, 256, 512)
+        load_wp(1, 0, 4)
+        load_wp(1, 1, 5)
+        wt_s = keep.tile([P, 2, N], U8, name="wt_s", tag="slot6", align_bytes=256)
         nc.gpsimd.memset(wt_s[:].bitcast(I32), 0)
         load_scale_rows(wt_s, wt_rows, range(4), nc.sync)
-        wt_w = keep.tile([P, 2, N], U32, name="wt_w", tag="slot6", align_bytes=256)
+        wt_w = keep.tile([P, 2, N], U32, name="wt_w", tag="slot0", align_bytes=256)
         nc.sync.dma_start(out=wt_w[:].bitcast(I32), in_=wt_words.rearrange("a p n t -> p a (n t)").bitcast(I32))
-        bt_sb = keep.tile([P, N // P], F32, name="bt_sb", tag="slot0", align_bytes=256)
+        bt_sb = keep.tile([P, N // P], F32, name="bt_sb", tag="slot1", align_bytes=256)
         with nc.allow_non_contiguous_dma(reason="one bias value for each partition"):
             nc.sync.dma_start(out=bt_sb[:], in_=bt.rearrange("(m p) -> p m", p=P))
         turned = psum.tile([P, P], F32, name="turned", tag="bank0")
@@ -275,15 +257,13 @@ def tile_list_interest_user_gate_kernel(
             for b in range(PACK):
                 nc.tensor.transpose(back[:, b, :], spread[:, b, :], ident[:])
             nc.scalar.copy(out=wgt_sb[:, BANK * half : BANK * (half + 1)], in_=back[:].rearrange("p b c -> p (b c)"))
-            if half == 0:
-                nc.scalar.copy(out=wgt_mid[:], in_=back[:].rearrange("p b c -> p (b c)"))
-                nc.scalar.copy(out=wgt_last[:], in_=back[:].rearrange("p b c -> p (b c)"))
         nc.vector.tensor_copy(
             out=wg_w[:].bitcast(U16).rearrange("p (h t m) -> p h t m", h=2, t=PACK),
             in_=wg_w_raw[:].bitcast(U16).rearrange("p (h m t) -> p h t m", h=2, t=PACK),
         )
         nc.vector.tensor_copy(v_s[:], tab_s[:].indirect(users[:]))
-        nc.vector.tensor_copy(v_w[:], tab_w[:].indirect(users[:]))
+        nc.vector.tensor_copy(v_w[:, 0:512], tab_w[:].indirect(users[:, 0:32]))
+        nc.vector.tensor_copy(v_w[:, 512:1024], tab_w[:].indirect(users[:, 32:64]))
         order_wg_scales(0)
         order_wg_scales(1)
         for lo in range(0, S, BANK):
@@ -292,32 +272,34 @@ def tile_list_interest_user_gate_kernel(
                     make_gate(h, t, lo)
         for t in range(PACK):
             gather(0, t, 0, S)
-        round_xg(0, 0, S)
+        round_xg(0, 0, 512)
+        round_xg(0, 512, 1024)
         round_wp(0, 0, "wp_a")
-        round_wp(0, 1, "picked0")
+        round_wp(0, 1, "picked0", 0, 256)
         gather(1, 0, 0, S)
         gather(1, 1, 0, S)
-        gather(1, 2, 0, 512, wgt_mid)
-        gather(1, 2, 512, 1024)
-        quantize_xg(0, 0, S)
+        quantize_xg(0, 0, 512)
+        gather(1, 2, 0, S)
         quantize_wp(0, 0)
-        project(0, 0, 0, S, 0)
-        gather(1, 3, 0, 256, wgt_last)
-        gather(1, 3, 256, 512, wgt_last)
+        project(0, 0, 0, 512, 0)
+        gather(1, 3, 0, 256)
+        gather(1, 3, 256, 512)
         gather(1, 3, 512, 1024)
-        quantize_wp(0, 1)
         round_xg(1, 0, 256)
+        round_wp(0, 1, None, 256, 512)
         round_xg(1, 256, 512)
         round_wp(1, 0, "tab_w")
         round_wp(1, 1, "wp_a")
-        round_xg(1, 768, 1024, tag="slot4")
+        round_xg(1, 768, 1024, tag="slot5")
         quantize_xg(1, 0, 256)
+        quantize_wp(0, 1)
         project(0, 1, 0, 256, None)
+        quantize_xg(0, 512, 1024, "picked0")
         quantize_xg(1, 256, 512)
         project(0, 1, 256, 512, None)
+        project(0, 0, 512, 1024, 4)
         round_xg(1, 512, 768, on_gpsimd, tag="xg_bf1_256", run=1)
         multiply(0, 0, 512, 0, 256)
-        warm_up(1, 2, 0)
         quantize_xg(1, 512, 768)
         project(0, 1, 512, 768, None)
         quantize_wp(1, 0)
@@ -355,7 +337,7 @@ def tile_list_interest_user_gate_kernel(
         multiply(1, 512, 768, 640, 768)
         tower_pass(0, 512, 768, 0, 2, 4)
         tower_pass(0, 512, 768, 2, 4, 5)
-        multiply(0, 768, 896, 768, 896)
+        multiply(0, 768, 1024, 768, 896)
         quantize_h(1, 512, 768)
         finish(512, 768, 0, 2, False)
         finish(512, 768, 2, 4, False)
@@ -363,16 +345,15 @@ def tile_list_interest_user_gate_kernel(
         project(1, 1, 768, 896, None)
         project(1, 0, 896, 1024, 1)
         project(1, 1, 896, 1024, None)
+        multiply(0, 768, 1024, 896, 1024)
         multiply(1, 768, 896, 768, 896)
-        quantize_h(0, 768, 896)
+        quantize_h(0, 768, 1024)
         tower_pass(0, 768, 896, 0, 2, 6)
         tower_pass(0, 768, 896, 2, 4, 3)
-        multiply(0, 896, 1024, 896, 1024)
+        multiply(1, 896, 1024, 896, 1024)
         quantize_h(1, 768, 896)
         finish(768, 896, 0, 2, False)
         finish(768, 896, 2, 4, False)
-        multiply(1, 896, 1024, 896, 1024)
-        quantize_h(0, 896, 1024)
         tower_pass(0, 896, 1024, 0, 2, 7)
         tower_pass(0, 896, 1024, 2, 4, 2)
         quantize_h(1, 896, 1024)

@@ -159,8 +159,10 @@ def tile_list_interest_user_gate_kernel(
                         stop=(a == 1 and t == PACK - 1),
                     )
 
-        def multiply(h, lo, hi, first, last):
-            if first == lo:
+        def multiply(h, lo, hi, first, last, tag=None):
+            if tag is not None:
+                h_bf[h, lo] = keep.tile([P, PACK * (hi - lo)], BF16, name="h_held", tag=tag, align_bytes=256)
+            elif first == lo:
                 h_bf[h, lo] = stage.tile([P, PACK * (hi - lo)], BF16, name="h_bf", tag="h_bf", bufs=4, align_bytes=256)
             for j0 in range(first, last, JC):
                 nc.vector.tensor_tensor(
@@ -299,52 +301,48 @@ def tile_list_interest_user_gate_kernel(
         project(0, 1, 256, 512, None)
         project(0, 0, 512, 1024, 4)
         round_xg(1, 512, 768, on_gpsimd, tag="xg_bf1_256", run=1)
-        multiply(0, 0, 512, 0, 256)
+        multiply(0, 0, 512, 0, 512)
+        quantize_wp(1, 0)
         quantize_xg(1, 512, 768)
         project(0, 1, 512, 768, None)
-        quantize_wp(1, 0)
-        project(1, 0, 0, 256, 0)
-        multiply(0, 0, 512, 256, 512)
-        project(1, 0, 256, 512, 2)
-        multiply(0, 512, 768, 512, 640)
+        project(1, 0, 0, 512, 0)
         quantize_h(0, 0, 512)
         quantize_wp(1, 1)
-        project(1, 1, 0, 256, None)
-        multiply(0, 512, 768, 640, 768)
-        tower_pass(0, 0, 256, 0, 2, 4)
-        tower_pass(0, 0, 256, 2, 4, 5)
-        project(1, 1, 256, 512, None)
-        quantize_h(0, 512, 768)
-        multiply(1, 0, 256, 0, 128)
-        multiply(1, 0, 256, 128, 256)
-        project(1, 0, 512, 640, 0)
+        project(1, 1, 0, 512, None)
+        multiply(0, 512, 768, 512, 640, "wp_a")
+        multiply(1, 0, 256, 0, 256)
+        project(1, 0, 512, 640, 4)
         project(1, 1, 512, 640, None)
-        quantize_xg(1, 768, 1024)
-        multiply(1, 256, 512, 256, 384)
+        tower_pass(0, 0, 256, 0, 2, 0)
+        tower_pass(0, 0, 256, 2, 4, 1)
+        multiply(0, 512, 768, 640, 768)
         quantize_h(1, 0, 256)
         finish(0, 256, 0, 2, False)
         finish(0, 256, 2, 4, False)
-        project(1, 0, 640, 768, 1)
+        project(1, 0, 640, 768, 5)
         project(1, 1, 640, 768, None)
+        multiply(1, 256, 512, 256, 384)
+        quantize_xg(1, 768, 1024)
+        quantize_h(0, 512, 768)
         multiply(1, 256, 512, 384, 512)
         tower_pass(0, 256, 512, 0, 2, 2)
         tower_pass(0, 256, 512, 2, 4, 3)
+        project(0, 1, 768, 1024, None)
         multiply(1, 512, 768, 512, 640)
         quantize_h(1, 256, 512)
         finish(256, 512, 0, 2, False)
         finish(256, 512, 2, 4, False)
-        project(0, 1, 768, 1024, None)
+        project(1, 0, 768, 896, 0)
+        project(1, 1, 768, 896, None)
         multiply(1, 512, 768, 640, 768)
+        project(1, 0, 896, 1024, 1)
+        project(1, 1, 896, 1024, None)
         tower_pass(0, 512, 768, 0, 2, 4)
         tower_pass(0, 512, 768, 2, 4, 5)
         multiply(0, 768, 1024, 768, 896)
         quantize_h(1, 512, 768)
         finish(512, 768, 0, 2, False)
         finish(512, 768, 2, 4, False)
-        project(1, 0, 768, 896, 0)
-        project(1, 1, 768, 896, None)
-        project(1, 0, 896, 1024, 1)
-        project(1, 1, 896, 1024, None)
         multiply(0, 768, 1024, 896, 1024)
         multiply(1, 768, 896, 768, 896)
         quantize_h(0, 768, 1024)

@@ -208,11 +208,8 @@ def tile_list_interest_user_gate_kernel(
             tower_pass(1, lo, hi, m0, m1, None)
             store(lo, hi, m0, m1, on_vector)
 
-        warm = keep.tile([P, 2], F32, name="warm", align_bytes=256)
         nc.vector.memset(tab_s[:].bitcast(I32), 0)
         nc.gpsimd.memset(wg_s_raw[:].bitcast(I32), 0)
-        nc.gpsimd.memset(warm[:, 0:1], 0.0)
-        nc.scalar.activation(out=warm[:, 1:2], in_=warm[:, 0:1], func=ACT.Sigmoid)
         make_identity(nc, ident[:])
         wt_rows = wt_scales.rearrange("a r n -> r a n")
         nc.sync.dma_start(users[:], offs)

@@ -228,8 +228,8 @@ def tile_list_interest_user_gate_kernel(
         load_plane(1, 1, 5)
         load_plane(1, 2, 6)
         load_wp(0, 0, 0)
-        load_wp(0, 1, 1, 0, 256)
         load_plane(1, 3, 2)
+        load_wp(0, 1, 1, 0, 256)
         load_wp(0, 1, 3, 256, 512)
         load_wp(1, 0, 4)
         load_wp(1, 1, 5)
@@ -274,68 +274,68 @@ def tile_list_interest_user_gate_kernel(
         round_xg(0, 0, 512)
         round_xg(0, 512, 1024)
         round_wp(0, 0, "wp_a")
-        round_wp(0, 1, "picked0", 0, 256)
         gather(1, 0, 0, S)
         gather(1, 1, 0, S)
         quantize_xg(0, 0, 512)
+        quantize_xg(0, 512, 1024)
         gather(1, 2, 0, S)
         quantize_wp(0, 0)
         project(0, 0, 0, 512, 0)
         gather(1, 3, 0, 256)
         gather(1, 3, 256, 512)
+        round_xg(1, 0, 256, nc.vector.tensor_copy, run=4)
         gather(1, 3, 512, 1024)
-        round_xg(1, 0, 256)
+        round_wp(0, 1, "picked0", 0, 256)
         round_wp(0, 1, None, 256, 512)
-        round_xg(1, 256, 512)
+        round_xg(1, 256, 512, tag="slot3")
         round_wp(1, 0, "tab_w")
         round_wp(1, 1, "wp_a")
         round_xg(1, 768, 1024, tag="slot5")
         quantize_xg(1, 0, 256)
         quantize_wp(0, 1)
         project(0, 1, 0, 256, None)
-        quantize_xg(0, 512, 1024, "picked0")
         quantize_xg(1, 256, 512)
         project(0, 1, 256, 512, None)
-        project(0, 0, 512, 1024, 4)
-        round_xg(1, 512, 768, on_gpsimd, tag="xg_bf1_256", run=1)
-        multiply(0, 0, 512, 0, 512)
+        round_xg(1, 512, 768, on_gpsimd, tag="picked0", run=1)
+        multiply(0, 0, 512, 0, 512, "slot3")
+        project(0, 0, 512, 1024, 0)
         quantize_wp(1, 0)
         quantize_xg(1, 512, 768)
         project(0, 1, 512, 768, None)
-        project(1, 0, 0, 512, 0)
+        project(1, 0, 0, 512, 4)
         quantize_h(0, 0, 512)
         quantize_wp(1, 1)
         project(1, 1, 0, 512, None)
         multiply(0, 512, 768, 512, 640, "wp_a")
         multiply(1, 0, 256, 0, 256)
-        project(1, 0, 512, 640, 4)
+        project(1, 0, 512, 640, 0)
         project(1, 1, 512, 640, None)
-        tower_pass(0, 0, 256, 0, 2, 0)
-        tower_pass(0, 0, 256, 2, 4, 1)
+        tower_pass(0, 0, 256, 0, 2, 4)
+        tower_pass(0, 0, 256, 2, 4, 5)
         multiply(0, 512, 768, 640, 768)
         quantize_h(1, 0, 256)
         finish(0, 256, 0, 2, False)
         finish(0, 256, 2, 4, False)
-        project(1, 0, 640, 768, 5)
+        project(1, 0, 640, 768, 1)
         project(1, 1, 640, 768, None)
         multiply(1, 256, 512, 256, 384)
         quantize_xg(1, 768, 1024)
         quantize_h(0, 512, 768)
         multiply(1, 256, 512, 384, 512)
-        tower_pass(0, 256, 512, 0, 2, 2)
-        tower_pass(0, 256, 512, 2, 4, 3)
+        tower_pass(0, 256, 512, 0, 2, 6)
+        tower_pass(0, 256, 512, 2, 4, 7)
         project(0, 1, 768, 1024, None)
         multiply(1, 512, 768, 512, 640)
         quantize_h(1, 256, 512)
         finish(256, 512, 0, 2, False)
         finish(256, 512, 2, 4, False)
-        project(1, 0, 768, 896, 0)
+        project(1, 0, 768, 896, 4)
         project(1, 1, 768, 896, None)
         multiply(1, 512, 768, 640, 768)
-        project(1, 0, 896, 1024, 1)
+        project(1, 0, 896, 1024, 5)
         project(1, 1, 896, 1024, None)
-        tower_pass(0, 512, 768, 0, 2, 4)
-        tower_pass(0, 512, 768, 2, 4, 5)
+        tower_pass(0, 512, 768, 0, 2, 0)
+        tower_pass(0, 512, 768, 2, 4, 1)
         multiply(0, 768, 1024, 768, 896)
         quantize_h(1, 512, 768)
         finish(512, 768, 0, 2, False)
@@ -343,14 +343,14 @@ def tile_list_interest_user_gate_kernel(
         multiply(0, 768, 1024, 896, 1024)
         multiply(1, 768, 896, 768, 896)
         quantize_h(0, 768, 1024)
-        tower_pass(0, 768, 896, 0, 2, 6)
-        tower_pass(0, 768, 896, 2, 4, 3)
+        tower_pass(0, 768, 896, 0, 2, 2)
+        tower_pass(0, 768, 896, 2, 4, 7)
         multiply(1, 896, 1024, 896, 1024)
         quantize_h(1, 768, 896)
         finish(768, 896, 0, 2, False)
         finish(768, 896, 2, 4, False)
-        tower_pass(0, 896, 1024, 0, 2, 7)
-        tower_pass(0, 896, 1024, 2, 4, 2)
+        tower_pass(0, 896, 1024, 0, 2, 3)
+        tower_pass(0, 896, 1024, 2, 4, 6)
         quantize_h(1, 896, 1024)
         finish(896, 1024, 0, 2, True)
         finish(896, 1024, 2, 4, False)

@@ -56,7 +56,7 @@ def tile_list_interest_user_gate_kernel(
         xg_s = [keep.tile([P, S], U8, name="xg_s%d" % a, align_bytes=256) for a in range(2)]
         wp_w = {}
         wp_s = [keep.tile([P, H], U8, name="wp_s%d" % a, align_bytes=256) for a in range(2)]
-        h_w = [keep.tile([P, S], U32, name="h_w%d" % h, align_bytes=256) for h in range(2)]
+        h_w = {}
         h_s = [keep.tile([P, S], U8, name="h_s%d" % h, align_bytes=256) for h in range(2)]
 
         def load_scale_rows(plane, rows, quadrants, queue):
@@ -84,10 +84,12 @@ def tile_list_interest_user_gate_kernel(
 
         xg_bf = {}
 
-        def round_xg(a, lo, hi, copy=nc.scalar.copy, tag=None, run=2):
-            xg_bf[a, lo] = keep.tile([P, PACK * (hi - lo)], BF16, name="xg_bf", tag=tag or "xg_bf%d_%d" % (a, lo), align_bytes=256)
+        def round_xg(a, lo, hi, copy=nc.scalar.copy, tag=None, run=2, into=None):
+            if into is None:
+                into = keep.tile([P, PACK * (hi - lo)], BF16, name="xg_bf", tag=tag or "xg_bf%d_%d" % (a, lo), align_bytes=256)[:]
+            xg_bf[a, lo] = into
             copy(
-                out=xg_bf[a, lo][:].rearrange("p (c i t) -> p c t i", i=run, t=PACK),
+                out=xg_bf[a, lo].rearrange("p (c i t) -> p c t i", i=run, t=PACK),
                 in_=picked[a][:, :, lo:hi].rearrange("p t (c i) -> p c t i", i=run),
             )
 
@@ -98,7 +100,7 @@ def tile_list_interest_user_gate_kernel(
             codes = keep.tile([P, hi - lo], U32, name="xg_w", tag=tag or "xg_w%d_%d" % (a, lo), align_bytes=256)[:]
             for j0 in range(lo, hi, JC):
                 xg_w[a, j0] = codes[:, j0 - lo : j0 - lo + JC]
-            nc.vector.quantize_mx(out=codes.bitcast(FP8X4), scales=xg_s[a][:, lo:hi], in_=xg_bf[a, lo][:])
+            nc.vector.quantize_mx(out=codes.bitcast(FP8X4), scales=xg_s[a][:, lo:hi], in_=xg_bf[a, lo])
 
         wp_bf = {}
 
@@ -159,8 +161,10 @@ def tile_list_interest_user_gate_kernel(
                         stop=(a == 1 and t == PACK - 1),
                     )
 
-        def multiply(h, lo, hi, first, last, tag=None):
-            if tag is not None:
+        def multiply(h, lo, hi, first, last, tag=None, made=False):
+            if made:
+                pass
+            elif tag is not None:
                 h_bf[h, lo] = keep.tile([P, PACK * (hi - lo)], BF16, name="h_held", tag=tag, align_bytes=256)
             elif first == lo:
                 h_bf[h, lo] = stage.tile([P, PACK * (hi - lo)], BF16, name="h_bf", tag="h_bf", bufs=4, align_bytes=256)
@@ -172,8 +176,26 @@ def tile_list_interest_user_gate_kernel(
                     MULT,
                 )
 
+        def multiply_on_gpsimd(h, lo, j0, sums, tag=None):
+            if tag is not None:
+                h_bf[h, lo] = keep.tile([P, PACK * JC], BF16, name="h_held", tag=tag, align_bytes=256)
+            nc.scalar.copy(out=sums.rearrange("p (c t) -> p c t", t=PACK), in_=acc[h, j0][:].rearrange("p t c -> p c t"))
+            nc.gpsimd.tensor_tensor(
+                h_bf[h, lo][:, PACK * (j0 - lo) : PACK * (j0 - lo + JC)].rearrange("p (c t) -> p c t", t=PACK),
+                sums.rearrange("p (c t) -> p c t", t=PACK),
+                gate[h, j0 // BANK * BANK][:, :, j0 % BANK : j0 % BANK + JC].rearrange("p t c -> p c t"),
+                MULT,
+            )
+
+        def h_codes(h, lo, hi, tag=None):
+            codes = keep.tile([P, hi - lo], U32, name="h_w", tag=tag or "h_w%d_%d" % (h, lo), align_bytes=256)
+            for j0 in range(lo, hi, JC):
+                h_w[h, j0] = codes[:, j0 - lo :]
+
         def quantize_h(h, lo, hi):
-            nc.vector.quantize_mx(out=h_w[h][:, lo:hi].bitcast(FP8X4), scales=h_s[h][:, lo:hi], in_=h_bf[h, lo][:])
+            if (h, lo) not in h_w:
+                h_codes(h, lo, hi)
+            nc.vector.quantize_mx(out=h_w[h, lo][:, 0 : hi - lo].bitcast(FP8X4), scales=h_s[h][:, lo:hi], in_=h_bf[h, lo][:, 0 : PACK * (hi - lo)])
 
         out_rows = out.rearrange("(m p) j -> p m j", p=P)
 
@@ -187,7 +209,7 @@ def tile_list_interest_user_gate_kernel(
                     out=tower[lo, m0][:, m - m0, :],
                     lhsT=wt_w[:, h, P * m : P * (m + 1)].bitcast(FP8X4),
                     lhsT_scale=wt_s[:, h, P * m : P * (m + 1)],
-                    rhs=h_w[h][:, lo:hi].bitcast(FP8X4),
+                    rhs=h_w[h, lo][:, 0 : hi - lo].bitcast(FP8X4),
                     rhs_scale=h_s[h][:, lo:hi],
                     start=(h == 0 and m == m0),
                     stop=(h == 1 and m == m1 - 1),
@@ -290,57 +312,68 @@ def tile_list_interest_user_gate_kernel(
         round_xg(1, 256, 512, tag="slot3")
         round_wp(1, 0, "tab_w")
         round_wp(1, 1, "wp_a")
-        round_xg(1, 768, 1024, tag="slot5")
         quantize_xg(1, 0, 256)
         quantize_wp(0, 1)
         project(0, 1, 0, 256, None)
         quantize_xg(1, 256, 512)
         project(0, 1, 256, 512, None)
-        round_xg(1, 512, 768, on_gpsimd, tag="picked0", run=1)
-        multiply(0, 0, 512, 0, 512, "slot3")
+        shared = keep.tile([P, 6 * BANK], BF16, name="shared", tag="slot3", align_bytes=256)
+        h_bf[0, 0] = shared[:, 0 : 4 * BANK]
+        round_xg(1, 512, 768, on_gpsimd, run=1, into=shared[:, 4 * BANK : 6 * BANK])
+        multiply(0, 0, 512, 0, 512, made=True)
         project(0, 0, 512, 1024, 0)
         quantize_wp(1, 0)
         quantize_xg(1, 512, 768)
         project(0, 1, 512, 768, None)
         project(1, 0, 0, 512, 4)
-        quantize_h(0, 0, 512)
         quantize_wp(1, 1)
+        h_codes(0, 0, 512, "wp_a")
+        quantize_h(0, 0, 512)
+        late = keep.tile([P, 3 * BANK], F32, name="late", tag="slot5", align_bytes=256)
+        multiply_on_gpsimd(0, 512, 512, late[:, 0:BANK], "slot3")
         project(1, 1, 0, 512, None)
-        multiply(0, 512, 768, 512, 640, "wp_a")
-        multiply(1, 0, 256, 0, 256)
+        multiply(1, 0, 256, 0, 256, "slot4")
+        multiply(1, 256, 512, 256, 384)
         project(1, 0, 512, 640, 0)
         project(1, 1, 512, 640, None)
+        nc.scalar.copy(out=late[:, BANK : 2 * BANK].rearrange("p (c t) -> p c t", t=PACK), in_=acc[0, 640][:].rearrange("p t c -> p c t"))
+        round_xg(1, 768, 1024, into=late[:, 2 * BANK : 3 * BANK].bitcast(BF16))
+        project(1, 0, 640, 768, 1)
+        project(1, 1, 640, 768, None)
         tower_pass(0, 0, 256, 0, 2, 4)
         tower_pass(0, 0, 256, 2, 4, 5)
-        multiply(0, 512, 768, 640, 768)
+        quantize_xg(1, 768, 1024)
         quantize_h(1, 0, 256)
         finish(0, 256, 0, 2, False)
         finish(0, 256, 2, 4, False)
-        project(1, 0, 640, 768, 1)
-        project(1, 1, 640, 768, None)
-        multiply(1, 256, 512, 256, 384)
-        quantize_xg(1, 768, 1024)
-        quantize_h(0, 512, 768)
+        h_bf[0, 640] = keep.tile([P, PACK * JC], BF16, name="h_held", tag="slot4", align_bytes=256)
+        nc.gpsimd.tensor_tensor(
+            h_bf[0, 640][:].rearrange("p (c t) -> p c t", t=PACK),
+            late[:, BANK : 2 * BANK].rearrange("p (c t) -> p c t", t=PACK),
+            gate[0, BANK][:, :, JC : 2 * JC].rearrange("p t c -> p c t"),
+            MULT,
+        )
         multiply(1, 256, 512, 384, 512)
+        multiply(1, 512, 768, 512, 768)
+        project(0, 1, 768, 1024, None)
         tower_pass(0, 256, 512, 0, 2, 6)
         tower_pass(0, 256, 512, 2, 4, 7)
-        project(0, 1, 768, 1024, None)
-        multiply(1, 512, 768, 512, 640)
+        project(1, 0, 768, 896, 0)
+        project(1, 1, 768, 896, None)
         quantize_h(1, 256, 512)
         finish(256, 512, 0, 2, False)
         finish(256, 512, 2, 4, False)
-        project(1, 0, 768, 896, 4)
-        project(1, 1, 768, 896, None)
-        multiply(1, 512, 768, 640, 768)
-        project(1, 0, 896, 1024, 5)
+        project(1, 0, 896, 1024, 1)
         project(1, 1, 896, 1024, None)
-        tower_pass(0, 512, 768, 0, 2, 0)
-        tower_pass(0, 512, 768, 2, 4, 1)
-        multiply(0, 768, 1024, 768, 896)
+        h_codes(0, 512, 768)
+        quantize_h(0, 512, 640)
+        quantize_h(0, 640, 768)
         quantize_h(1, 512, 768)
+        tower_pass(0, 512, 768, 0, 2, 4)
+        tower_pass(0, 512, 768, 2, 4, 5)
         finish(512, 768, 0, 2, False)
         finish(512, 768, 2, 4, False)
-        multiply(0, 768, 1024, 896, 1024)
+        multiply(0, 768, 1024, 768, 1024)
         multiply(1, 768, 896, 768, 896)
         quantize_h(0, 768, 1024)
         tower_pass(0, 768, 896, 0, 2, 2)

@@ -73,9 +73,9 @@ def tile_list_interest_user_gate_kernel(
         wp_raw = {}
 
         def load_wp(h, a, slot, lo=0, hi=KP):
-            wp_raw[h, a, lo] = keep.tile([P, PACK, hi - lo], F32, name="wp_raw", tag="slot%d" % slot, align_bytes=256)
+            wp_raw[h, a, lo] = keep.tile([P, PACK, hi - lo], F32, name="wp_raw", tag="slot%d" % slot, align_bytes=256)[:]
             rows = wp[KP * a : KP * (a + 1), KP * h + lo : KP * h + hi].rearrange("(p i) c -> p i c", i=PACK)
-            nc.sync.dma_start(out=wp_raw[h, a, lo][:], in_=rows)
+            nc.sync.dma_start(out=wp_raw[h, a, lo], in_=rows)
 
         def gather(a, t, lo, hi):
             nc.vector.tensor_tensor(
@@ -84,13 +84,13 @@ def tile_list_interest_user_gate_kernel(
 
         xg_bf = {}
 
-        def round_xg(a, lo, hi, copy=nc.scalar.copy, tag=None, run=2, into=None):
+        def round_xg(a, lo, hi, copy=nc.scalar.copy, tag=None, run=2, into=None, t0=0, t1=PACK):
             if into is None:
                 into = keep.tile([P, PACK * (hi - lo)], BF16, name="xg_bf", tag=tag or "xg_bf%d_%d" % (a, lo), align_bytes=256)[:]
             xg_bf[a, lo] = into
             copy(
-                out=xg_bf[a, lo].rearrange("p (c i t) -> p c t i", i=run, t=PACK),
-                in_=picked[a][:, :, lo:hi].rearrange("p t (c i) -> p c t i", i=run),
+                out=xg_bf[a, lo].rearrange("p (c i t) -> p c t i", i=run, t=PACK)[:, :, t0:t1],
+                in_=picked[a][:, t0:t1, lo:hi].rearrange("p t (c i) -> p c t i", i=run),
             )
 
         def on_gpsimd(out, in_):
@@ -109,7 +109,7 @@ def tile_list_interest_user_gate_kernel(
                 wp_bf[h, a] = keep.tile([P, PACK * KP], BF16, name="wp_bf", tag=tag, align_bytes=256)
             copy(
                 out=wp_bf[h, a][:].rearrange("p (t m i) -> p m i t", t=PACK, i=PACK)[:, lo // PACK : hi // PACK],
-                in_=wp_raw[h, a, lo][:].rearrange("p i (m t) -> p m i t", t=PACK),
+                in_=wp_raw[h, a, lo].rearrange("p i (m t) -> p m i t", t=PACK),
             )
 
         def quantize_wp(h, a):
@@ -226,6 +226,18 @@ def tile_list_interest_user_gate_kernel(
                     )
             nc.sync.dma_start(out=out_rows[:, m0:m1, lo:hi], in_=res[:])
 
+        def finish_last(lo, hi, banks):
+            for m in range(PACK):
+                tower_pass(0, lo, hi, m, m + 1, banks[m])
+            quantize_h(1, lo, hi)
+            for m0 in (0, 2):
+                res = stage.tile([P, 2, hi - lo], F32, name="res", tag="res", bufs=8, align_bytes=256)
+                tower_pass(1, lo, hi, m0, m0 + 1, None)
+                tower_pass(1, lo, hi, m0 + 1, m0 + 2, None)
+                nc.vector.tensor_scalar_add(res[:, 0, :], tower[lo, m0][:, 0, :], bt_sb[:, m0 : m0 + 1])
+                nc.scalar.activation(out=res[:, 1, :], in_=tower[lo, m0 + 1][:, 0, :], func=ACT.Identity, bias=bt_sb[:, m0 + 1 : m0 + 2])
+                nc.sync.dma_start(out=out_rows[:, m0 : m0 + 2, lo:hi], in_=res[:])
+
         def finish(lo, hi, m0, m1, on_vector):
             tower_pass(1, lo, hi, m0, m1, None)
             store(lo, hi, m0, m1, on_vector)
@@ -250,11 +262,13 @@ def tile_list_interest_user_gate_kernel(
         load_plane(1, 1, 5)
         load_plane(1, 2, 6)
         load_wp(0, 0, 0)
-        load_plane(1, 3, 2)
         load_wp(0, 1, 1, 0, 256)
+        load_plane(1, 3, 2)
         load_wp(0, 1, 3, 256, 512)
         load_wp(1, 0, 4)
         load_wp(1, 1, 5)
+        wp_raw[1, 1, 320] = wp_raw[1, 1, 0][:, :, 320:512]
+        wp_raw[1, 1, 0] = wp_raw[1, 1, 0][:, :, 0:320]
         wt_s = keep.tile([P, 2, N], U8, name="wt_s", tag="slot6", align_bytes=256)
         nc.gpsimd.memset(wt_s[:].bitcast(I32), 0)
         load_scale_rows(wt_s, wt_rows, range(4), nc.sync)
@@ -291,41 +305,42 @@ def tile_list_interest_user_gate_kernel(
             for h in range(2):
                 for t in range(PACK):
                     make_gate(h, t, lo)
-        for t in range(PACK):
+        for t in range(PACK - 1):
             gather(0, t, 0, S)
+        gather(0, 3, 0, 512)
+        gather(0, 3, 512, 1024)
         round_xg(0, 0, 512)
         round_xg(0, 512, 1024)
         round_wp(0, 0, "wp_a")
+        round_wp(0, 1, "picked0", 0, 256)
         gather(1, 0, 0, S)
         gather(1, 1, 0, S)
         quantize_xg(0, 0, 512)
-        quantize_xg(0, 512, 1024)
         gather(1, 2, 0, S)
         quantize_wp(0, 0)
         project(0, 0, 0, 512, 0)
         gather(1, 3, 0, 256)
         gather(1, 3, 256, 512)
-        round_xg(1, 0, 256, nc.vector.tensor_copy, run=4)
         gather(1, 3, 512, 1024)
-        round_wp(0, 1, "picked0", 0, 256)
+        round_xg(1, 0, 256)
         round_wp(0, 1, None, 256, 512)
-        round_xg(1, 256, 512, tag="slot3")
+        round_xg(1, 256, 512)
         round_wp(1, 0, "tab_w")
-        round_wp(1, 1, "wp_a")
+        round_wp(1, 1, "wp_a", 0, 320)
         quantize_xg(1, 0, 256)
         quantize_wp(0, 1)
         project(0, 1, 0, 256, None)
+        quantize_xg(0, 512, 1024, "picked0")
         quantize_xg(1, 256, 512)
         project(0, 1, 256, 512, None)
-        shared = keep.tile([P, 6 * BANK], BF16, name="shared", tag="slot3", align_bytes=256)
-        h_bf[0, 0] = shared[:, 0 : 4 * BANK]
-        round_xg(1, 512, 768, on_gpsimd, run=1, into=shared[:, 4 * BANK : 6 * BANK])
-        multiply(0, 0, 512, 0, 512, made=True)
-        project(0, 0, 512, 1024, 0)
+        project(0, 0, 512, 1024, 4)
+        round_xg(1, 512, 768, on_gpsimd, tag="xg_bf1_256", run=1)
+        multiply(0, 0, 512, 0, 512, "slot3")
         quantize_wp(1, 0)
         quantize_xg(1, 512, 768)
+        round_wp(1, 1, None, 320, 512, nc.vector.tensor_copy)
         project(0, 1, 512, 768, None)
-        project(1, 0, 0, 512, 4)
+        project(1, 0, 0, 512, 0)
         quantize_wp(1, 1)
         h_codes(0, 0, 512, "wp_a")
         quantize_h(0, 0, 512)
@@ -334,14 +349,14 @@ def tile_list_interest_user_gate_kernel(
         project(1, 1, 0, 512, None)
         multiply(1, 0, 256, 0, 256, "slot4")
         multiply(1, 256, 512, 256, 384)
-        project(1, 0, 512, 640, 0)
+        project(1, 0, 512, 640, 4)
         project(1, 1, 512, 640, None)
         nc.scalar.copy(out=late[:, BANK : 2 * BANK].rearrange("p (c t) -> p c t", t=PACK), in_=acc[0, 640][:].rearrange("p t c -> p c t"))
         round_xg(1, 768, 1024, into=late[:, 2 * BANK : 3 * BANK].bitcast(BF16))
-        project(1, 0, 640, 768, 1)
+        project(1, 0, 640, 768, 5)
         project(1, 1, 640, 768, None)
-        tower_pass(0, 0, 256, 0, 2, 4)
-        tower_pass(0, 0, 256, 2, 4, 5)
+        tower_pass(0, 0, 256, 0, 2, 0)
+        tower_pass(0, 0, 256, 2, 4, 1)
         quantize_xg(1, 768, 1024)
         quantize_h(1, 0, 256)
         finish(0, 256, 0, 2, False)
@@ -356,34 +371,30 @@ def tile_list_interest_user_gate_kernel(
         multiply(1, 256, 512, 384, 512)
         multiply(1, 512, 768, 512, 768)
         project(0, 1, 768, 1024, None)
-        tower_pass(0, 256, 512, 0, 2, 6)
-        tower_pass(0, 256, 512, 2, 4, 7)
-        project(1, 0, 768, 896, 0)
+        tower_pass(0, 256, 512, 0, 2, 2)
+        tower_pass(0, 256, 512, 2, 4, 3)
+        project(1, 0, 768, 896, 4)
         project(1, 1, 768, 896, None)
         quantize_h(1, 256, 512)
         finish(256, 512, 0, 2, False)
         finish(256, 512, 2, 4, False)
-        project(1, 0, 896, 1024, 1)
-        project(1, 1, 896, 1024, None)
         h_codes(0, 512, 768)
         quantize_h(0, 512, 640)
         quantize_h(0, 640, 768)
         quantize_h(1, 512, 768)
-        tower_pass(0, 512, 768, 0, 2, 4)
-        tower_pass(0, 512, 768, 2, 4, 5)
+        tower_pass(0, 512, 768, 0, 2, 0)
+        tower_pass(0, 512, 768, 2, 4, 1)
         finish(512, 768, 0, 2, False)
         finish(512, 768, 2, 4, False)
         multiply(0, 768, 1024, 768, 1024)
+        project(1, 0, 896, 1024, 6)
+        project(1, 1, 896, 1024, None)
         multiply(1, 768, 896, 768, 896)
         quantize_h(0, 768, 1024)
-        tower_pass(0, 768, 896, 0, 2, 2)
-        tower_pass(0, 768, 896, 2, 4, 7)
+        tower_pass(0, 768, 896, 0, 2, 5)
+        tower_pass(0, 768, 896, 2, 4, 3)
         multiply(1, 896, 1024, 896, 1024)
         quantize_h(1, 768, 896)
         finish(768, 896, 0, 2, False)
         finish(768, 896, 2, 4, False)
-        tower_pass(0, 896, 1024, 0, 2, 3)
-        tower_pass(0, 896, 1024, 2, 4, 6)
-        quantize_h(1, 896, 1024)
-        finish(896, 1024, 0, 2, True)
-        finish(896, 1024, 2, 4, False)
+        finish_last(896, 1024, (7, 2, 0, 1))

@@ -267,8 +267,6 @@ def tile_list_interest_user_gate_kernel(
         load_wp(0, 1, 3, 256, 512)
         load_wp(1, 0, 4)
         load_wp(1, 1, 5)
-        wp_raw[1, 1, 320] = wp_raw[1, 1, 0][:, :, 320:512]
-        wp_raw[1, 1, 0] = wp_raw[1, 1, 0][:, :, 0:320]
         wt_s = keep.tile([P, 2, N], U8, name="wt_s", tag="slot6", align_bytes=256)
         nc.gpsimd.memset(wt_s[:].bitcast(I32), 0)
         load_scale_rows(wt_s, wt_rows, range(4), nc.sync)
@@ -326,7 +324,7 @@ def tile_list_interest_user_gate_kernel(
         round_wp(0, 1, None, 256, 512)
         round_xg(1, 256, 512)
         round_wp(1, 0, "tab_w")
-        round_wp(1, 1, "wp_a", 0, 320)
+        round_wp(1, 1, "wp_a")
         quantize_xg(1, 0, 256)
         quantize_wp(0, 1)
         project(0, 1, 0, 256, None)
@@ -338,7 +336,6 @@ def tile_list_interest_user_gate_kernel(
         multiply(0, 0, 512, 0, 512, "slot3")
         quantize_wp(1, 0)
         quantize_xg(1, 512, 768)
-        round_wp(1, 1, None, 320, 512, nc.vector.tensor_copy)
         project(0, 1, 512, 768, None)
         project(1, 0, 0, 512, 0)
         quantize_wp(1, 1)

@@ -176,16 +176,29 @@ def tile_list_interest_user_gate_kernel(
                     MULT,
                 )
 
+        def copy_sums(h, j0, sums):
+            nc.scalar.copy(out=sums.rearrange("p (c t) -> p c t", t=PACK), in_=acc[h, j0][:].rearrange("p t c -> p c t"))
+
         def multiply_on_gpsimd(h, lo, j0, sums, tag=None):
             if tag is not None:
                 h_bf[h, lo] = keep.tile([P, PACK * JC], BF16, name="h_held", tag=tag, align_bytes=256)
-            nc.scalar.copy(out=sums.rearrange("p (c t) -> p c t", t=PACK), in_=acc[h, j0][:].rearrange("p t c -> p c t"))
             nc.gpsimd.tensor_tensor(
                 h_bf[h, lo][:, PACK * (j0 - lo) : PACK * (j0 - lo + JC)].rearrange("p (c t) -> p c t", t=PACK),
                 sums.rearrange("p (c t) -> p c t", t=PACK),
-                gate[h, j0 // BANK * BANK][:, :, j0 % BANK : j0 % BANK + JC].rearrange("p t c -> p c t"),
+                woven_gate[j0].rearrange("p (c t) -> p c t", t=PACK),
                 MULT,
             )
+
+        woven_gate = {}
+
+        def weave_gate(tag):
+            woven = keep.tile([P, 2 * BANK], F32, name="woven", tag=tag, align_bytes=256)
+            nc.scalar.copy(
+                out=woven[:].rearrange("p (c i t) -> p c t i", i=2, t=PACK),
+                in_=gate[0, BANK][:, :, 0 : 2 * JC].rearrange("p t (c i) -> p c t i", i=2),
+            )
+            woven_gate[512] = woven[:, 0:BANK]
+            woven_gate[640] = woven[:, BANK : 2 * BANK]
 
         def h_codes(h, lo, hi, tag=None):
             codes = keep.tile([P, hi - lo], U32, name="h_w", tag=tag or "h_w%d_%d" % (h, lo), align_bytes=256)
@@ -309,11 +322,12 @@ def tile_list_interest_user_gate_kernel(
         gather(0, 3, 512, 1024)
         round_xg(0, 0, 512)
         round_xg(0, 512, 1024)
-        round_wp(0, 0, "wp_a")
-        round_wp(0, 1, "picked0", 0, 256)
         gather(1, 0, 0, S)
         gather(1, 1, 0, S)
         quantize_xg(0, 0, 512)
+        weave_gate("xg_bf0_0")
+        round_wp(0, 0, "wp_a")
+        round_wp(0, 1, "picked0", 0, 256)
         gather(1, 2, 0, S)
         quantize_wp(0, 0)
         project(0, 0, 0, 512, 0)
@@ -331,46 +345,41 @@ def tile_list_interest_user_gate_kernel(
         quantize_xg(0, 512, 1024, "picked0")
         quantize_xg(1, 256, 512)
         project(0, 1, 256, 512, None)
-        project(0, 0, 512, 1024, 4)
         round_xg(1, 512, 768, on_gpsimd, tag="xg_bf1_256", run=1)
         multiply(0, 0, 512, 0, 512, "slot3")
+        project(0, 0, 512, 1024, 0)
         quantize_wp(1, 0)
         quantize_xg(1, 512, 768)
         project(0, 1, 512, 768, None)
-        project(1, 0, 0, 512, 0)
+        project(1, 0, 0, 512, 4)
         quantize_wp(1, 1)
         h_codes(0, 0, 512, "wp_a")
         quantize_h(0, 0, 512)
         late = keep.tile([P, 3 * BANK], F32, name="late", tag="slot5", align_bytes=256)
+        copy_sums(0, 512, late[:, 0:BANK])
         multiply_on_gpsimd(0, 512, 512, late[:, 0:BANK], "slot3")
         project(1, 1, 0, 512, None)
         multiply(1, 0, 256, 0, 256, "slot4")
         multiply(1, 256, 512, 256, 384)
-        project(1, 0, 512, 640, 4)
+        project(1, 0, 512, 640, 0)
         project(1, 1, 512, 640, None)
-        nc.scalar.copy(out=late[:, BANK : 2 * BANK].rearrange("p (c t) -> p c t", t=PACK), in_=acc[0, 640][:].rearrange("p t c -> p c t"))
+        copy_sums(0, 640, late[:, BANK : 2 * BANK])
         round_xg(1, 768, 1024, into=late[:, 2 * BANK : 3 * BANK].bitcast(BF16))
-        project(1, 0, 640, 768, 5)
+        project(1, 0, 640, 768, 1)
         project(1, 1, 640, 768, None)
-        tower_pass(0, 0, 256, 0, 2, 0)
-        tower_pass(0, 0, 256, 2, 4, 1)
+        tower_pass(0, 0, 256, 0, 2, 4)
+        tower_pass(0, 0, 256, 2, 4, 5)
         quantize_xg(1, 768, 1024)
         quantize_h(1, 0, 256)
         finish(0, 256, 0, 2, False)
         finish(0, 256, 2, 4, False)
-        h_bf[0, 640] = keep.tile([P, PACK * JC], BF16, name="h_held", tag="slot4", align_bytes=256)
-        nc.gpsimd.tensor_tensor(
-            h_bf[0, 640][:].rearrange("p (c t) -> p c t", t=PACK),
-            late[:, BANK : 2 * BANK].rearrange("p (c t) -> p c t", t=PACK),
-            gate[0, BANK][:, :, JC : 2 * JC].rearrange("p t c -> p c t"),
-            MULT,
-        )
+        multiply_on_gpsimd(0, 640, 640, late[:, BANK : 2 * BANK], "slot4")
         multiply(1, 256, 512, 384, 512)
         multiply(1, 512, 768, 512, 768)
         project(0, 1, 768, 1024, None)
-        tower_pass(0, 256, 512, 0, 2, 2)
-        tower_pass(0, 256, 512, 2, 4, 3)
-        project(1, 0, 768, 896, 4)
+        tower_pass(0, 256, 512, 0, 2, 6)
+        tower_pass(0, 256, 512, 2, 4, 7)
+        project(1, 0, 768, 896, 0)
         project(1, 1, 768, 896, None)
         quantize_h(1, 256, 512)
         finish(256, 512, 0, 2, False)
@@ -379,19 +388,19 @@ def tile_list_interest_user_gate_kernel(
         quantize_h(0, 512, 640)
         quantize_h(0, 640, 768)
         quantize_h(1, 512, 768)
-        tower_pass(0, 512, 768, 0, 2, 0)
-        tower_pass(0, 512, 768, 2, 4, 1)
+        tower_pass(0, 512, 768, 0, 2, 4)
+        tower_pass(0, 512, 768, 2, 4, 5)
         finish(512, 768, 0, 2, False)
         finish(512, 768, 2, 4, False)
         multiply(0, 768, 1024, 768, 1024)
-        project(1, 0, 896, 1024, 6)
+        project(1, 0, 896, 1024, 2)
         project(1, 1, 896, 1024, None)
         multiply(1, 768, 896, 768, 896)
         quantize_h(0, 768, 1024)
-        tower_pass(0, 768, 896, 0, 2, 5)
-        tower_pass(0, 768, 896, 2, 4, 3)
+        tower_pass(0, 768, 896, 0, 2, 1)
+        tower_pass(0, 768, 896, 2, 4, 7)
         multiply(1, 896, 1024, 896, 1024)
         quantize_h(1, 768, 896)
         finish(768, 896, 0, 2, False)
         finish(768, 896, 2, 4, False)
-        finish_last(896, 1024, (7, 2, 0, 1))
+        finish_last(896, 1024, (3, 6, 4, 5))

@@ -22,7 +22,16 @@ P = 128
 PACK = 4
 KP = P * PACK
 BANK = 512
-JC = 128
+BLOCK = 128
+LIST_ROWS = 16
+HEADS = 8
+ALIGN = 256
+H_TILES = 4
+RESULT_TILES = 8
+
+WP_AHEAD = 256
+WP_LAST_ON_SCALAR = 384
+XG_ON_GPSIMD = 192
 
 
 def tile_list_interest_user_gate_kernel(
@@ -32,102 +41,98 @@ def tile_list_interest_user_gate_kernel(
     with ExitStack() as ctx:
         lists = ctx.enter_context(tc.tile_pool(name="lists", bufs=1))
         keep = ctx.enter_context(tc.tile_pool(name="keep", bufs=1))
-        stage = ctx.enter_context(tc.tile_pool(name="stage", bufs=3))
+        stage = ctx.enter_context(tc.tile_pool(name="stage", bufs=1))
         psum = ctx.enter_context(tc.psum_pool(name="psum", bufs=1))
 
-        users = lists.tile([P, S // 16], U16, name="users")
-        clicks = lists.tile([P, S // 16], U16, name="clicks")
+        def sbuf(shape, dtype, tag):
+            return keep.tile(shape, dtype, name=tag, tag=tag, align_bytes=ALIGN)
 
-        tab_w = keep.tile([P, T], U32, name="tab_w", align_bytes=256)
-        tab_s = keep.tile([P, T], U8, name="tab_s", align_bytes=256)
-        v_w = keep.tile([P, S], U32, name="v_w", align_bytes=256)
-        v_s = keep.tile([P, S], U8, name="v_s", align_bytes=256)
-        wg_w_raw = keep.tile([P, 2 * H], U8, name="wg_w_raw", align_bytes=256)
-        wg_s_raw = keep.tile([P, H], U8, name="wg_s_raw", align_bytes=256)
-        wg_w = keep.tile([P, 2 * H], U8, name="wg_w", align_bytes=256)
-        wg_s = keep.tile([P, H], U8, name="wg_s", align_bytes=256)
-        wgt_sb = keep.tile([P, S], F32, name="wgt_sb", align_bytes=256)
-        wgt_raw = keep.tile([P, P], F32, name="wgt_raw", align_bytes=256)
-        ident = keep.tile([P, P], F32, name="ident", align_bytes=256)
-        bg_sb = keep.tile([P, 2, 8], F32, name="bg_sb", align_bytes=256)
-        picked = [keep.tile([P, PACK, S], F32, name="picked%d" % a, align_bytes=256) for a in range(2)]
-        gate = {(h, lo): keep.tile([P, PACK, BANK], F32, name="gate%d_%d" % (h, lo), align_bytes=256) for h in range(2) for lo in (0, BANK)}
-        xg_w = {}
-        xg_s = [keep.tile([P, S], U8, name="xg_s%d" % a, align_bytes=256) for a in range(2)]
-        wp_w = {}
-        wp_s = [keep.tile([P, H], U8, name="wp_s%d" % a, align_bytes=256) for a in range(2)]
-        h_w = {}
-        h_s = [keep.tile([P, S], U8, name="h_s%d" % h, align_bytes=256) for h in range(2)]
+        def bank_tile(shape, bank):
+            return psum.tile(shape, F32, name="bank", tag="bank%d" % bank)
 
-        def load_scale_rows(plane, rows, quadrants, queue):
-            for q in quadrants:
-                queue.dma_start(out=plane[32 * q : 32 * q + 4].bitcast(I32), in_=rows[4 * q : 4 * q + 4].bitcast(I32))
+        users = lists.tile([P, S // LIST_ROWS], U16, name="users")
+        clicks = lists.tile([P, S // LIST_ROWS], U16, name="clicks")
+
+        tab_w = sbuf([P, T], U32, "tab_w")
+        tab_s = sbuf([P, T], U8, "tab_s")
+        v_w = sbuf([P, S], U32, "v_w")
+        v_s = sbuf([P, S], U8, "v_s")
+        wg_w_raw = sbuf([P, 2 * H], U8, "wg_w_raw")
+        wg_s_raw = sbuf([P, H], U8, "wg_s_raw")
+        wg_w = sbuf([P, 2 * H], U8, "wg_w")
+        wg_s = sbuf([P, H], U8, "wg_s")
+        wgt_sb = sbuf([P, S], F32, "wgt_sb")
+        wgt_raw = sbuf([P, P], F32, "wgt_raw")
+        ident = sbuf([P, P], F32, "ident")
+        bg_sb = sbuf([P, 2, 2 * PACK], F32, "bg_sb")
+        picked = [sbuf([P, PACK, S], F32, "picked%d" % a) for a in range(2)]
+        gate = {(half, lo): sbuf([P, PACK, BANK], F32, "gate%d_%d" % (half, lo)) for half in range(2) for lo in (0, BANK)}
+        xg_s = [sbuf([P, S], U8, "xg_s%d" % a) for a in range(2)]
+        wp_s = [sbuf([P, H], U8, "wp_s%d" % a) for a in range(2)]
+        h_s = [sbuf([P, S], U8, "h_s%d" % half) for half in range(2)]
+
+        def load_scale_rows(dst, rows):
+            for q in range(4):
+                nc.sync.dma_start(out=dst[32 * q : 32 * q + 4].bitcast(I32), in_=rows[4 * q : 4 * q + 4].bitcast(I32))
 
         planes = {}
 
-        def load_plane(a, t, slot):
-            planes[a, t] = keep.tile([P, T], F32, name="plane", tag="slot%d" % slot, align_bytes=256)
+        def load_plane(a, i, slot):
+            planes[a, i] = sbuf([P, T], F32, "slot%d" % slot)
             rows = xT[KP * a : KP * (a + 1), :].rearrange("(p i) c -> p i c", i=PACK)
-            nc.sync.dma_start(out=planes[a, t][:], in_=rows[:, t, :])
+            nc.sync.dma_start(out=planes[a, i][:], in_=rows[:, i, :])
 
-        wp_raw = {}
+        def load_wp(half, a, lo, hi, slot):
+            raw = sbuf([P, PACK, hi - lo], F32, "slot%d" % slot)
+            rows = wp[KP * a : KP * (a + 1), KP * half + lo : KP * half + hi].rearrange("(p i) c -> p i c", i=PACK)
+            nc.sync.dma_start(out=raw[:], in_=rows)
+            return raw
 
-        def load_wp(h, a, slot, lo=0, hi=KP):
-            wp_raw[h, a, lo] = keep.tile([P, PACK, hi - lo], F32, name="wp_raw", tag="slot%d" % slot, align_bytes=256)[:]
-            rows = wp[KP * a : KP * (a + 1), KP * h + lo : KP * h + hi].rearrange("(p i) c -> p i c", i=PACK)
-            nc.sync.dma_start(out=wp_raw[h, a, lo], in_=rows)
+        def gather(a, i, lo, hi):
+            offsets = clicks[:, lo // LIST_ROWS : hi // LIST_ROWS]
+            nc.vector.tensor_tensor(picked[a][:, i, lo:hi], planes[a, i][:].indirect(offsets), wgt_sb[:, lo:hi], MULT)
 
-        def gather(a, t, lo, hi):
-            nc.vector.tensor_tensor(
-                picked[a][:, t, lo:hi], planes[a, t][:].indirect(clicks[:, lo // 16 : hi // 16]), wgt_sb[:, lo:hi], MULT
+        def round_xg(a, lo, hi, woven):
+            nc.scalar.copy(
+                out=woven.rearrange("p (c n i) -> p c i n", n=2, i=PACK),
+                in_=picked[a][:, :, lo:hi].rearrange("p i (c n) -> p c i n", n=2),
             )
 
-        xg_bf = {}
+        def round_xg_on_gpsimd(a, lo, hi, woven):
+            nc.gpsimd.tensor_scalar(
+                woven.rearrange("p (c n i) -> p c i n", n=1, i=PACK),
+                picked[a][:, :, lo:hi].rearrange("p i (c n) -> p c i n", n=1),
+                1.0,
+                0.0,
+                MULT,
+                ADD,
+            )
 
-        def round_xg(a, lo, hi, copy=nc.scalar.copy, tag=None, run=2, into=None, t0=0, t1=PACK):
-            if into is None:
-                into = keep.tile([P, PACK * (hi - lo)], BF16, name="xg_bf", tag=tag or "xg_bf%d_%d" % (a, lo), align_bytes=256)[:]
-            xg_bf[a, lo] = into
+        xg_w = {}
+
+        def quantize_xg(a, lo, hi, woven, tag):
+            codes = sbuf([P, hi - lo], U32, tag)[:]
+            for j0 in range(lo, hi, BLOCK):
+                xg_w[a, j0] = codes[:, j0 - lo : j0 - lo + BLOCK]
+            nc.vector.quantize_mx(out=codes.bitcast(FP8X4), scales=xg_s[a][:, lo:hi], in_=woven)
+
+        def round_wp(raw, lo, hi, woven, copy):
             copy(
-                out=xg_bf[a, lo].rearrange("p (c i t) -> p c t i", i=run, t=PACK)[:, :, t0:t1],
-                in_=picked[a][:, t0:t1, lo:hi].rearrange("p t (c i) -> p c t i", i=run),
+                out=woven[:].rearrange("p (t m i) -> p m i t", t=PACK, i=PACK)[:, lo // PACK : hi // PACK],
+                in_=raw.rearrange("p i (m t) -> p m i t", t=PACK),
             )
 
-        def on_gpsimd(out, in_):
-            nc.gpsimd.tensor_scalar(out, in_, 1.0, 0.0, MULT, ADD)
+        wp_w = {}
 
-        def quantize_xg(a, lo, hi, tag=None):
-            codes = keep.tile([P, hi - lo], U32, name="xg_w", tag=tag or "xg_w%d_%d" % (a, lo), align_bytes=256)[:]
-            for j0 in range(lo, hi, JC):
-                xg_w[a, j0] = codes[:, j0 - lo : j0 - lo + JC]
-            nc.vector.quantize_mx(out=codes.bitcast(FP8X4), scales=xg_s[a][:, lo:hi], in_=xg_bf[a, lo])
-
-        wp_bf = {}
-
-        def round_wp(h, a, tag, lo=0, hi=KP, copy=nc.scalar.copy):
-            if lo == 0:
-                wp_bf[h, a] = keep.tile([P, PACK * KP], BF16, name="wp_bf", tag=tag, align_bytes=256)
-            copy(
-                out=wp_bf[h, a][:].rearrange("p (t m i) -> p m i t", t=PACK, i=PACK)[:, lo // PACK : hi // PACK],
-                in_=wp_raw[h, a, lo].rearrange("p i (m t) -> p m i t", t=PACK),
+        def quantize_wp(half, a, woven):
+            wp_w[half, a] = sbuf([P, KP], U32, "wp_w%d%d" % (half, a))[:]
+            nc.vector.quantize_mx(
+                out=wp_w[half, a].bitcast(FP8X4), scales=wp_s[a][:, KP * half : KP * (half + 1)], in_=woven[:]
             )
 
-        def quantize_wp(h, a):
-            cols = slice(KP * h, KP * (h + 1))
-            codes = keep.tile([P, KP], U32, name="wp_w", tag="wp_w%d%d" % (h, a), align_bytes=256)
-            wp_w[h, a] = codes[:]
-            nc.vector.quantize_mx(out=wp_w[h, a].bitcast(FP8X4), scales=wp_s[a][:, cols], in_=wp_bf[h, a][:])
-
-        def order_wg_scales(h):
-            cols = slice(KP * h, KP * (h + 1))
-            nc.gpsimd.tensor_copy(
-                out=wg_s[:, cols].rearrange("p (t m) -> p t m", t=PACK),
-                in_=wg_s_raw[:, cols].rearrange("p (m t) -> p t m", t=PACK),
-            )
-
-        def make_gate(h, t, lo):
-            pre = psum.tile([P, BANK], F32, name="pre", tag="bank%d" % (t + PACK * h))
-            c0 = KP * h + P * t
+        def make_gate(half, t, lo):
+            pre = bank_tile([P, BANK], t + PACK * half)
+            c0 = KP * half + P * t
             nc.tensor.matmul_mx(
                 out=pre[:],
                 lhsT=wg_w[:, 2 * c0 : 2 * (c0 + P)].bitcast(FP4X4),
@@ -137,270 +142,283 @@ def tile_list_interest_user_gate_kernel(
                 start=True,
                 stop=True,
             )
-            nc.scalar.activation(
-                out=gate[h, lo][:, t, :], in_=pre[:], func=ACT.Sigmoid, bias=bg_sb[:, h, t : t + 1]
-            )
-
-        h_bf = {}
+            nc.scalar.activation(out=gate[half, lo][:, t, :], in_=pre[:], func=ACT.Sigmoid, bias=bg_sb[:, half, t : t + 1])
 
         acc = {}
 
-        def project(h, a, first, last, bank):
-            for j0 in range(first, last, JC):
-                if a == 0:
-                    acc[h, j0] = psum.tile([P, PACK, JC], F32, name="acc", tag="bank%d" % (bank + (j0 - first) // JC))
-                for t in range(PACK):
-                    c0 = KP * h + P * t
-                    nc.tensor.matmul_mx(
-                        out=acc[h, j0][:, t, :],
-                        lhsT=wp_w[h, a][:, P * t : P * (t + 1)].bitcast(FP8X4),
-                        lhsT_scale=wp_s[a][:, c0 : c0 + P],
-                        rhs=xg_w[a, j0].bitcast(FP8X4),
-                        rhs_scale=xg_s[a][:, j0 : j0 + JC],
-                        start=(a == 0 and t == 0),
-                        stop=(a == 1 and t == PACK - 1),
-                    )
+        def project(half, a, j0):
+            for t in range(PACK):
+                c0 = KP * half + P * t
+                nc.tensor.matmul_mx(
+                    out=acc[half, j0][:, t, :],
+                    lhsT=wp_w[half, a][:, P * t : P * (t + 1)].bitcast(FP8X4),
+                    lhsT_scale=wp_s[a][:, c0 : c0 + P],
+                    rhs=xg_w[a, j0].bitcast(FP8X4),
+                    rhs_scale=xg_s[a][:, j0 : j0 + BLOCK],
+                    start=(a == 0 and t == 0),
+                    stop=(a == 1 and t == PACK - 1),
+                )
 
-        def multiply(h, lo, hi, first, last, tag=None, made=False):
-            if made:
-                pass
-            elif tag is not None:
-                h_bf[h, lo] = keep.tile([P, PACK * (hi - lo)], BF16, name="h_held", tag=tag, align_bytes=256)
-            elif first == lo:
-                h_bf[h, lo] = stage.tile([P, PACK * (hi - lo)], BF16, name="h_bf", tag="h_bf", bufs=4, align_bytes=256)
-            for j0 in range(first, last, JC):
+        def open_sums(half, lo, hi, first_bank):
+            for j0 in range(lo, hi, BLOCK):
+                acc[half, j0] = bank_tile([P, PACK, BLOCK], first_bank + (j0 - lo) // BLOCK)
+                project(half, 0, j0)
+
+        def close_sums(half, lo, hi):
+            for j0 in range(lo, hi, BLOCK):
+                project(half, 1, j0)
+
+        def h_tile(requests):
+            return stage.tile([P, PACK * requests], BF16, name="h_bf", tag="h_bf", bufs=H_TILES, align_bytes=ALIGN)
+
+        def multiply(half, lo, hi, woven, at=0):
+            for j0 in range(lo, hi, BLOCK):
+                c0 = PACK * (at + j0 - lo)
                 nc.vector.tensor_tensor(
-                    h_bf[h, lo][:, PACK * (j0 - lo) : PACK * (j0 - lo + JC)].rearrange("p (c i t) -> p c t i", i=2, t=PACK),
-                    acc[h, j0][:].rearrange("p t (c i) -> p c t i", i=2),
-                    gate[h, j0 // BANK * BANK][:, :, j0 % BANK : j0 % BANK + JC].rearrange("p t (c i) -> p c t i", i=2),
+                    woven[:, c0 : c0 + PACK * BLOCK].rearrange("p (c n t) -> p c t n", n=2, t=PACK),
+                    acc[half, j0][:].rearrange("p t (c n) -> p c t n", n=2),
+                    gate[half, j0 // BANK * BANK][:, :, j0 % BANK : j0 % BANK + BLOCK].rearrange("p t (c n) -> p c t n", n=2),
                     MULT,
                 )
 
-        def copy_sums(h, j0, sums):
-            nc.scalar.copy(out=sums.rearrange("p (c t) -> p c t", t=PACK), in_=acc[h, j0][:].rearrange("p t c -> p c t"))
+        def copy_sums(half, j0, woven):
+            nc.scalar.copy(out=woven.rearrange("p (c t) -> p c t", t=PACK), in_=acc[half, j0][:].rearrange("p t c -> p c t"))
 
-        def multiply_on_gpsimd(h, lo, j0, sums, tag=None):
-            if tag is not None:
-                h_bf[h, lo] = keep.tile([P, PACK * JC], BF16, name="h_held", tag=tag, align_bytes=256)
+        def multiply_on_gpsimd(woven_sums, woven_gate, woven):
             nc.gpsimd.tensor_tensor(
-                h_bf[h, lo][:, PACK * (j0 - lo) : PACK * (j0 - lo + JC)].rearrange("p (c t) -> p c t", t=PACK),
-                sums.rearrange("p (c t) -> p c t", t=PACK),
-                woven_gate[j0].rearrange("p (c t) -> p c t", t=PACK),
+                woven[:].rearrange("p (c t) -> p c t", t=PACK),
+                woven_sums.rearrange("p (c t) -> p c t", t=PACK),
+                woven_gate.rearrange("p (c t) -> p c t", t=PACK),
                 MULT,
             )
 
-        woven_gate = {}
+        h_w = {}
 
-        def weave_gate(tag):
-            woven = keep.tile([P, 2 * BANK], F32, name="woven", tag=tag, align_bytes=256)
-            nc.scalar.copy(
-                out=woven[:].rearrange("p (c i t) -> p c t i", i=2, t=PACK),
-                in_=gate[0, BANK][:, :, 0 : 2 * JC].rearrange("p t (c i) -> p c t i", i=2),
-            )
-            woven_gate[512] = woven[:, 0:BANK]
-            woven_gate[640] = woven[:, BANK : 2 * BANK]
+        def h_codes(half, lo, hi, tag):
+            codes = sbuf([P, hi - lo], U32, tag)
+            for j0 in range(lo, hi, BLOCK):
+                h_w[half, j0] = codes[:, j0 - lo :]
 
-        def h_codes(h, lo, hi, tag=None):
-            codes = keep.tile([P, hi - lo], U32, name="h_w", tag=tag or "h_w%d_%d" % (h, lo), align_bytes=256)
-            for j0 in range(lo, hi, JC):
-                h_w[h, j0] = codes[:, j0 - lo :]
-
-        def quantize_h(h, lo, hi):
-            if (h, lo) not in h_w:
-                h_codes(h, lo, hi)
-            nc.vector.quantize_mx(out=h_w[h, lo][:, 0 : hi - lo].bitcast(FP8X4), scales=h_s[h][:, lo:hi], in_=h_bf[h, lo][:, 0 : PACK * (hi - lo)])
+        def quantize_h(half, lo, hi, woven):
+            if (half, lo) not in h_w:
+                h_codes(half, lo, hi, "h_w%d_%d" % (half, lo))
+            nc.vector.quantize_mx(out=h_w[half, lo][:, 0 : hi - lo].bitcast(FP8X4), scales=h_s[half][:, lo:hi], in_=woven[:])
 
         out_rows = out.rearrange("(m p) j -> p m j", p=P)
-
         tower = {}
 
-        def tower_pass(h, lo, hi, m0, m1, bank):
-            if h == 0:
-                tower[lo, m0] = psum.tile([P, m1 - m0, hi - lo], F32, name="tower", tag="bank%d" % bank)
+        def tower_pass(half, lo, hi, m0, m1):
             for m in range(m0, m1):
                 nc.tensor.matmul_mx(
                     out=tower[lo, m0][:, m - m0, :],
-                    lhsT=wt_w[:, h, P * m : P * (m + 1)].bitcast(FP8X4),
-                    lhsT_scale=wt_s[:, h, P * m : P * (m + 1)],
-                    rhs=h_w[h, lo][:, 0 : hi - lo].bitcast(FP8X4),
-                    rhs_scale=h_s[h][:, lo:hi],
-                    start=(h == 0 and m == m0),
-                    stop=(h == 1 and m == m1 - 1),
+                    lhsT=wt_w[:, half, P * m : P * (m + 1)].bitcast(FP8X4),
+                    lhsT_scale=wt_s[:, half, P * m : P * (m + 1)],
+                    rhs=h_w[half, lo][:, 0 : hi - lo].bitcast(FP8X4),
+                    rhs_scale=h_s[half][:, lo:hi],
+                    start=(half == 0 and m == m0),
+                    stop=(half == 1 and m == m1 - 1),
                 )
 
-        def store(lo, hi, m0, m1, on_vector):
-            res = stage.tile([P, m1 - m0, hi - lo], F32, name="res", tag="res", bufs=8, align_bytes=256)
-            for m in range(m0, m1):
-                if on_vector:
-                    nc.vector.tensor_scalar_add(res[:, m - m0, :], tower[lo, m0][:, m - m0, :], bt_sb[:, m : m + 1])
-                else:
-                    nc.scalar.activation(
-                        out=res[:, m - m0, :], in_=tower[lo, m0][:, m - m0, :], func=ACT.Identity, bias=bt_sb[:, m : m + 1]
-                    )
-            nc.sync.dma_start(out=out_rows[:, m0:m1, lo:hi], in_=res[:])
+        def open_tower(lo, hi, banks):
+            share = PACK // len(banks)
+            for n, bank in enumerate(banks):
+                tower[lo, share * n] = bank_tile([P, share, hi - lo], bank)
+                tower_pass(0, lo, hi, share * n, share * (n + 1))
 
-        def finish_last(lo, hi, banks):
-            for m in range(PACK):
-                tower_pass(0, lo, hi, m, m + 1, banks[m])
-            quantize_h(1, lo, hi)
+        def result_tile(lo, hi):
+            return stage.tile([P, 2, hi - lo], F32, name="res", tag="res", bufs=RESULT_TILES, align_bytes=ALIGN)
+
+        def add_bias_on_scalar(dst, src, m):
+            nc.scalar.activation(out=dst, in_=src, func=ACT.Identity, bias=bt_sb[:, m : m + 1])
+
+        def finish(lo, hi):
             for m0 in (0, 2):
-                res = stage.tile([P, 2, hi - lo], F32, name="res", tag="res", bufs=8, align_bytes=256)
-                tower_pass(1, lo, hi, m0, m0 + 1, None)
-                tower_pass(1, lo, hi, m0 + 1, m0 + 2, None)
-                nc.vector.tensor_scalar_add(res[:, 0, :], tower[lo, m0][:, 0, :], bt_sb[:, m0 : m0 + 1])
-                nc.scalar.activation(out=res[:, 1, :], in_=tower[lo, m0 + 1][:, 0, :], func=ACT.Identity, bias=bt_sb[:, m0 + 1 : m0 + 2])
+                tower_pass(1, lo, hi, m0, m0 + 2)
+                res = result_tile(lo, hi)
+                for m in (m0, m0 + 1):
+                    add_bias_on_scalar(res[:, m - m0, :], tower[lo, m0][:, m - m0, :], m)
                 nc.sync.dma_start(out=out_rows[:, m0 : m0 + 2, lo:hi], in_=res[:])
 
-        def finish(lo, hi, m0, m1, on_vector):
-            tower_pass(1, lo, hi, m0, m1, None)
-            store(lo, hi, m0, m1, on_vector)
+        def finish_last(lo, hi):
+            for m0 in (0, 2):
+                res = result_tile(lo, hi)
+                tower_pass(1, lo, hi, m0, m0 + 1)
+                tower_pass(1, lo, hi, m0 + 1, m0 + 2)
+                nc.vector.tensor_scalar_add(res[:, 0, :], tower[lo, m0][:, 0, :], bt_sb[:, m0 : m0 + 1])
+                add_bias_on_scalar(res[:, 1, :], tower[lo, m0 + 1][:, 0, :], m0 + 1)
+                nc.sync.dma_start(out=out_rows[:, m0 : m0 + 2, lo:hi], in_=res[:])
 
         nc.vector.memset(tab_s[:].bitcast(I32), 0)
         nc.gpsimd.memset(wg_s_raw[:].bitcast(I32), 0)
         make_identity(nc, ident[:])
-        wt_rows = wt_scales.rearrange("a r n -> r a n")
         nc.sync.dma_start(users[:], offs)
         nc.sync.dma_start(out=wg_w_raw[:].bitcast(I32), in_=wg_words[0].bitcast(I32))
         nc.sync.dma_start(out=wgt_raw[:], in_=wgt.rearrange("(g q) (b c) -> g (q b) c", q=16, c=P)[:, 0:16, :])
-        load_scale_rows(tab_s, tab_scales[0], range(4), nc.sync)
+        load_scale_rows(tab_s, tab_scales[0])
         nc.sync.dma_start(out=tab_w[:].bitcast(I32), in_=tab_words[0].rearrange("p n t -> p (n t)").bitcast(I32))
-        load_scale_rows(wg_s_raw, wg_scales[0], range(4), nc.sync)
+        load_scale_rows(wg_s_raw, wg_scales[0])
         nc.sync.dma_start(clicks[:], offs2)
         nc.sync.dma_start(out=bg_sb[:, :, 0:PACK], in_=bg.rearrange("(h p t) -> p h t", h=2, t=PACK))
-        load_plane(0, 0, 0)
-        load_plane(0, 1, 1)
-        load_plane(0, 2, 2)
-        load_plane(0, 3, 3)
-        load_plane(1, 0, 4)
-        load_plane(1, 1, 5)
-        load_plane(1, 2, 6)
-        load_wp(0, 0, 0)
-        load_wp(0, 1, 1, 0, 256)
+        for slot in range(2 * PACK - 1):
+            load_plane(slot // PACK, slot % PACK, slot)
+        wp00_raw = load_wp(0, 0, 0, KP, 0)
+        wp01_ahead_raw = load_wp(0, 1, 0, WP_AHEAD, 1)
         load_plane(1, 3, 2)
-        load_wp(0, 1, 3, 256, 512)
-        load_wp(1, 0, 4)
-        load_wp(1, 1, 5)
-        wt_s = keep.tile([P, 2, N], U8, name="wt_s", tag="slot6", align_bytes=256)
+        wp01_rest_raw = load_wp(0, 1, WP_AHEAD, KP, 3)
+        wp10_raw = load_wp(1, 0, 0, KP, 4)
+        wp11_raw = load_wp(1, 1, 0, KP, 5)
+        wt_s = sbuf([P, 2, N], U8, "slot6")
         nc.gpsimd.memset(wt_s[:].bitcast(I32), 0)
-        load_scale_rows(wt_s, wt_rows, range(4), nc.sync)
-        wt_w = keep.tile([P, 2, N], U32, name="wt_w", tag="slot0", align_bytes=256)
+        load_scale_rows(wt_s, wt_scales.rearrange("a r n -> r a n"))
+        wt_w = sbuf([P, 2, N], U32, "slot0")
         nc.sync.dma_start(out=wt_w[:].bitcast(I32), in_=wt_words.rearrange("a p n t -> p a (n t)").bitcast(I32))
-        bt_sb = keep.tile([P, N // P], F32, name="bt_sb", tag="slot1", align_bytes=256)
+        bt_sb = sbuf([P, N // P], F32, "slot1")
         with nc.allow_non_contiguous_dma(reason="one bias value for each partition"):
             nc.sync.dma_start(out=bt_sb[:], in_=bt.rearrange("(m p) -> p m", p=P))
-        turned = psum.tile([P, P], F32, name="turned", tag="bank0")
+
+        turned = bank_tile([P, P], 0)
         nc.tensor.transpose(turned[:], wgt_raw[:], ident[:])
-        for half in range(2):
-            spread = stage.tile([P, PACK, P], F32, name="spread", tag="res", bufs=8, align_bytes=256)
+        for part in range(S // BANK):
+            spread = stage.tile([P, PACK, P], F32, name="spread", tag="res", bufs=RESULT_TILES, align_bytes=ALIGN)
             nc.scalar.copy(
-                out=spread[:].rearrange("p b (g u r) -> p b g u r", g=8, r=2),
+                out=spread[:].rearrange("p b (g u r) -> p b g u r", g=HEADS, r=2),
                 in_=turned[:]
-                .rearrange("p (g r b) -> p b g r", g=8, r=2)[:, PACK * half : PACK * (half + 1)]
+                .rearrange("p (g r b) -> p b g r", g=HEADS, r=2)[:, PACK * part : PACK * (part + 1)]
                 .unsqueeze(3)
-                .broadcast_to([P, PACK, 8, 8, 2]),
+                .broadcast_to([P, PACK, HEADS, 8, 2]),
             )
-            back = psum.tile([P, PACK, P], F32, name="back", tag="bank%d" % (1 + half))
+            back = bank_tile([P, PACK, P], 1 + part)
             for b in range(PACK):
                 nc.tensor.transpose(back[:, b, :], spread[:, b, :], ident[:])
-            nc.scalar.copy(out=wgt_sb[:, BANK * half : BANK * (half + 1)], in_=back[:].rearrange("p b c -> p (b c)"))
+            nc.scalar.copy(out=wgt_sb[:, BANK * part : BANK * (part + 1)], in_=back[:].rearrange("p b c -> p (b c)"))
+
         nc.vector.tensor_copy(
             out=wg_w[:].bitcast(U16).rearrange("p (h t m) -> p h t m", h=2, t=PACK),
             in_=wg_w_raw[:].bitcast(U16).rearrange("p (h m t) -> p h t m", h=2, t=PACK),
         )
         nc.vector.tensor_copy(v_s[:], tab_s[:].indirect(users[:]))
-        nc.vector.tensor_copy(v_w[:, 0:512], tab_w[:].indirect(users[:, 0:32]))
-        nc.vector.tensor_copy(v_w[:, 512:1024], tab_w[:].indirect(users[:, 32:64]))
-        order_wg_scales(0)
-        order_wg_scales(1)
         for lo in range(0, S, BANK):
-            for h in range(2):
+            nc.vector.tensor_copy(v_w[:, lo : lo + BANK], tab_w[:].indirect(users[:, lo // LIST_ROWS : (lo + BANK) // LIST_ROWS]))
+        for half in range(2):
+            nc.gpsimd.tensor_copy(
+                out=wg_s[:, KP * half : KP * (half + 1)].rearrange("p (t m) -> p t m", t=PACK),
+                in_=wg_s_raw[:, KP * half : KP * (half + 1)].rearrange("p (m t) -> p t m", t=PACK),
+            )
+        for lo in range(0, S, BANK):
+            for half in range(2):
                 for t in range(PACK):
-                    make_gate(h, t, lo)
-        for t in range(PACK - 1):
-            gather(0, t, 0, S)
+                    make_gate(half, t, lo)
+
+        for i in range(PACK - 1):
+            gather(0, i, 0, S)
         gather(0, 3, 0, 512)
         gather(0, 3, 512, 1024)
-        round_xg(0, 0, 512)
-        round_xg(0, 512, 1024)
+        xg0_front = sbuf([P, PACK * 512], BF16, "xg0_front")[:]
+        round_xg(0, 0, 512, xg0_front)
+        xg0_back = sbuf([P, PACK * 512], BF16, "xg0_back")[:]
+        round_xg(0, 512, 1024, xg0_back)
         gather(1, 0, 0, S)
         gather(1, 1, 0, S)
-        quantize_xg(0, 0, 512)
-        weave_gate("xg_bf0_0")
-        round_wp(0, 0, "wp_a")
-        round_wp(0, 1, "picked0", 0, 256)
+        quantize_xg(0, 0, 512, xg0_front, "xg_w0_front")
+        woven_gate = sbuf([P, 2 * BANK], F32, "xg0_front")
+        nc.scalar.copy(
+            out=woven_gate[:].rearrange("p (c n t) -> p c t n", n=2, t=PACK),
+            in_=gate[0, BANK][:, :, 0 : 2 * BLOCK].rearrange("p t (c n) -> p c t n", n=2),
+        )
+        wp00 = sbuf([P, PACK * KP], BF16, "wp_bf")
+        round_wp(wp00_raw[:], 0, KP, wp00, nc.scalar.copy)
+        wp01 = sbuf([P, PACK * KP], BF16, "picked0")
+        round_wp(wp01_ahead_raw[:], 0, WP_AHEAD, wp01, nc.scalar.copy)
+        quantize_xg(0, 512, 1024, xg0_back, "xg_w0_back")
         gather(1, 2, 0, S)
-        quantize_wp(0, 0)
-        project(0, 0, 0, 512, 0)
+        quantize_wp(0, 0, wp00)
+        open_sums(0, 0, 512, 0)
+
         gather(1, 3, 0, 256)
         gather(1, 3, 256, 512)
         gather(1, 3, 512, 1024)
-        round_xg(1, 0, 256)
-        round_wp(0, 1, None, 256, 512)
-        round_xg(1, 256, 512)
-        round_wp(1, 0, "tab_w")
-        round_wp(1, 1, "wp_a")
-        quantize_xg(1, 0, 256)
-        quantize_wp(0, 1)
-        project(0, 1, 0, 256, None)
-        quantize_xg(0, 512, 1024, "picked0")
-        quantize_xg(1, 256, 512)
-        project(0, 1, 256, 512, None)
-        round_xg(1, 512, 768, on_gpsimd, tag="xg_bf1_256", run=1)
-        multiply(0, 0, 512, 0, 512, "slot3")
-        project(0, 0, 512, 1024, 0)
-        quantize_wp(1, 0)
-        quantize_xg(1, 512, 768)
-        project(0, 1, 512, 768, None)
-        project(1, 0, 0, 512, 4)
-        quantize_wp(1, 1)
-        h_codes(0, 0, 512, "wp_a")
-        quantize_h(0, 0, 512)
-        late = keep.tile([P, 3 * BANK], F32, name="late", tag="slot5", align_bytes=256)
-        copy_sums(0, 512, late[:, 0:BANK])
-        multiply_on_gpsimd(0, 512, 512, late[:, 0:BANK], "slot3")
-        project(1, 1, 0, 512, None)
-        multiply(1, 0, 256, 0, 256, "slot4")
-        multiply(1, 256, 512, 256, 384)
-        project(1, 0, 512, 640, 0)
-        project(1, 1, 512, 640, None)
-        copy_sums(0, 640, late[:, BANK : 2 * BANK])
-        round_xg(1, 768, 1024, into=late[:, 2 * BANK : 3 * BANK].bitcast(BF16))
-        project(1, 0, 640, 768, 1)
-        project(1, 1, 640, 768, None)
-        tower_pass(0, 0, 256, 0, 2, 4)
-        tower_pass(0, 0, 256, 2, 4, 5)
-        quantize_xg(1, 768, 1024)
-        quantize_h(1, 0, 256)
-        finish(0, 256, 0, 2, False)
-        finish(0, 256, 2, 4, False)
-        multiply_on_gpsimd(0, 640, 640, late[:, BANK : 2 * BANK], "slot4")
-        multiply(1, 256, 512, 384, 512)
-        multiply(1, 512, 768, 512, 768)
-        project(0, 1, 768, 1024, None)
-        tower_pass(0, 256, 512, 0, 2, 6)
-        tower_pass(0, 256, 512, 2, 4, 7)
-        project(1, 0, 768, 896, 0)
-        project(1, 1, 768, 896, None)
-        quantize_h(1, 256, 512)
-        finish(256, 512, 0, 2, False)
-        finish(256, 512, 2, 4, False)
-        h_codes(0, 512, 768)
-        quantize_h(0, 512, 640)
-        quantize_h(0, 640, 768)
-        quantize_h(1, 512, 768)
-        tower_pass(0, 512, 768, 0, 2, 4)
-        tower_pass(0, 512, 768, 2, 4, 5)
-        finish(512, 768, 0, 2, False)
-        finish(512, 768, 2, 4, False)
-        multiply(0, 768, 1024, 768, 1024)
-        project(1, 0, 896, 1024, 2)
-        project(1, 1, 896, 1024, None)
-        multiply(1, 768, 896, 768, 896)
-        quantize_h(0, 768, 1024)
-        tower_pass(0, 768, 896, 0, 2, 1)
-        tower_pass(0, 768, 896, 2, 4, 7)
-        multiply(1, 896, 1024, 896, 1024)
-        quantize_h(1, 768, 896)
-        finish(768, 896, 0, 2, False)
-        finish(768, 896, 2, 4, False)
-        finish_last(896, 1024, (3, 6, 4, 5))
+        xg1_blocks01 = sbuf([P, PACK * 256], BF16, "xg1_blocks01")[:]
+        round_xg(1, 0, 256, xg1_blocks01)
+        round_wp(wp01_rest_raw[:], WP_AHEAD, KP, wp01, nc.scalar.copy)
+        xg1_blocks23 = sbuf([P, PACK * 256], BF16, "xg1_blocks23")[:]
+        round_xg(1, 256, 512, xg1_blocks23)
+        wp10 = sbuf([P, PACK * KP], BF16, "tab_w")
+        round_wp(wp10_raw[:], 0, KP, wp10, nc.scalar.copy)
+        quantize_xg(1, 0, 256, xg1_blocks01, "xg_w1_blocks01")
+        quantize_wp(0, 1, wp01)
+        close_sums(0, 0, 256)
+        quantize_xg(1, 256, 512, xg1_blocks23, "xg_w1_blocks23")
+        close_sums(0, 256, 512)
+        xg1_blocks45 = sbuf([P, PACK * 256], BF16, "xg1_blocks23")
+        round_xg(1, 512 + XG_ON_GPSIMD, 768, xg1_blocks45[:, PACK * XG_ON_GPSIMD :])
+        round_xg_on_gpsimd(1, 512, 512 + XG_ON_GPSIMD, xg1_blocks45[:, 0 : PACK * XG_ON_GPSIMD])
+        wp11 = sbuf([P, PACK * KP], BF16, "wp_bf")
+        round_wp(wp11_raw[:, :, 0:WP_LAST_ON_SCALAR], 0, WP_LAST_ON_SCALAR, wp11, nc.scalar.copy)
+        h0_blocks03 = sbuf([P, PACK * 512], BF16, "slot3")
+        multiply(0, 0, 512, h0_blocks03)
+        open_sums(0, 512, 1024, 0)
+        quantize_wp(1, 0, wp10)
+        quantize_xg(1, 512, 768, xg1_blocks45[:], "xg_w1_blocks45")
+        round_wp(wp11_raw[:, :, WP_LAST_ON_SCALAR:KP], WP_LAST_ON_SCALAR, KP, wp11, nc.vector.tensor_copy)
+        close_sums(0, 512, 768)
+        open_sums(1, 0, 512, 4)
+        quantize_wp(1, 1, wp11)
+        h_codes(0, 0, 512, "wp_bf")
+        quantize_h(0, 0, 512, h0_blocks03)
+
+        late = sbuf([P, 3 * BANK], F32, "slot5")
+        sums4, sums5 = late[:, 0:BANK], late[:, BANK : 2 * BANK]
+        xg1_blocks67 = late[:, 2 * BANK : 3 * BANK].bitcast(BF16)
+        copy_sums(0, 512, sums4)
+        h0_block4 = sbuf([P, PACK * BLOCK], BF16, "slot3")
+        multiply_on_gpsimd(sums4, woven_gate[:, 0:BANK], h0_block4)
+        close_sums(1, 0, 512)
+        h1_blocks01 = sbuf([P, PACK * 256], BF16, "slot4")
+        multiply(1, 0, 256, h1_blocks01)
+        h1_blocks23 = h_tile(256)
+        multiply(1, 256, 384, h1_blocks23)
+        open_sums(1, 512, 640, 0)
+        close_sums(1, 512, 640)
+        copy_sums(0, 640, sums5)
+        round_xg(1, 768, 1024, xg1_blocks67)
+        open_sums(1, 640, 768, 1)
+        close_sums(1, 640, 768)
+        open_tower(0, 256, (4, 5))
+        quantize_xg(1, 768, 1024, xg1_blocks67, "xg_w1_blocks67")
+        quantize_h(1, 0, 256, h1_blocks01)
+        finish(0, 256)
+
+        h0_block5 = sbuf([P, PACK * BLOCK], BF16, "slot4")
+        multiply_on_gpsimd(sums5, woven_gate[:, BANK : 2 * BANK], h0_block5)
+        multiply(1, 384, 512, h1_blocks23, at=BLOCK)
+        h1_blocks45 = h_tile(256)
+        multiply(1, 512, 768, h1_blocks45)
+        close_sums(0, 768, 1024)
+        open_tower(256, 512, (6, 7))
+        open_sums(1, 768, 896, 0)
+        close_sums(1, 768, 896)
+        quantize_h(1, 256, 512, h1_blocks23)
+        finish(256, 512)
+
+        h_codes(0, 512, 768, "h_w0_512")
+        quantize_h(0, 512, 640, h0_block4)
+        quantize_h(0, 640, 768, h0_block5)
+        quantize_h(1, 512, 768, h1_blocks45)
+        open_tower(512, 768, (4, 5))
+        finish(512, 768)
+
+        h0_blocks67 = h_tile(256)
+        multiply(0, 768, 1024, h0_blocks67)
+        open_sums(1, 896, 1024, 2)
+        close_sums(1, 896, 1024)
+        h1_block6 = h_tile(BLOCK)
+        multiply(1, 768, 896, h1_block6)
+        quantize_h(0, 768, 1024, h0_blocks67)
+        open_tower(768, 896, (1, 7))
+        h1_block7 = h_tile(BLOCK)
+        multiply(1, 896, 1024, h1_block7)
+        quantize_h(1, 768, 896, h1_block6)
+        finish(768, 896)
+        open_tower(896, 1024, (3, 6, 4, 5))
+        quantize_h(1, 896, 1024, h1_block7)
+        finish_last(896, 1024)

@@ -30,8 +30,8 @@ H_TILES = 4
 RESULT_TILES = 8
 
 WP_AHEAD = 256
+XG_FIRST = 224
 WP_LAST_ON_SCALAR = 384
-XG_ON_GPSIMD = 192
 
 
 def tile_list_interest_user_gate_kernel(
@@ -186,7 +186,7 @@ def tile_list_interest_user_gate_kernel(
 
         def multiply_on_gpsimd(woven_sums, woven_gate, woven):
             nc.gpsimd.tensor_tensor(
-                woven[:].rearrange("p (c t) -> p c t", t=PACK),
+                woven.rearrange("p (c t) -> p c t", t=PACK),
                 woven_sums.rearrange("p (c t) -> p c t", t=PACK),
                 woven_gate.rearrange("p (c t) -> p c t", t=PACK),
                 MULT,
@@ -253,7 +253,7 @@ def tile_list_interest_user_gate_kernel(
         make_identity(nc, ident[:])
         nc.sync.dma_start(users[:], offs)
         nc.sync.dma_start(out=wg_w_raw[:].bitcast(I32), in_=wg_words[0].bitcast(I32))
-        nc.sync.dma_start(out=wgt_raw[:], in_=wgt.rearrange("(g q) (b c) -> g (q b) c", q=16, c=P)[:, 0:16, :])
+        nc.sync.dma_start(out=wgt_raw[:], in_=wgt.rearrange("(u q) (b c) -> u (q b) c", q=8, c=P)[:, 0:64:9, :])
         load_scale_rows(tab_s, tab_scales[0])
         nc.sync.dma_start(out=tab_w[:].bitcast(I32), in_=tab_words[0].rearrange("p n t -> p (n t)").bitcast(I32))
         load_scale_rows(wg_s_raw, wg_scales[0])
@@ -321,10 +321,11 @@ def tile_list_interest_user_gate_kernel(
         gather(1, 1, 0, S)
         quantize_xg(0, 0, 512, xg0_front, "xg_w0_front")
         woven_gate = sbuf([P, 2 * BANK], F32, "xg0_front")
-        nc.scalar.copy(
-            out=woven_gate[:].rearrange("p (c n t) -> p c t n", n=2, t=PACK),
-            in_=gate[0, BANK][:, :, 0 : 2 * BLOCK].rearrange("p t (c n) -> p c t n", n=2),
-        )
+        for n, j0 in enumerate((384, 512)):
+            nc.scalar.copy(
+                out=woven_gate[:, BANK * n : BANK * (n + 1)].rearrange("p (c n t) -> p c t n", n=2, t=PACK),
+                in_=gate[0, j0 // BANK * BANK][:, :, j0 % BANK : j0 % BANK + BLOCK].rearrange("p t (c n) -> p c t n", n=2),
+            )
         wp00 = sbuf([P, PACK * KP], BF16, "wp_bf")
         round_wp(wp00_raw[:], 0, KP, wp00, nc.scalar.copy)
         wp01 = sbuf([P, PACK * KP], BF16, "picked0")
@@ -334,91 +335,91 @@ def tile_list_interest_user_gate_kernel(
         quantize_wp(0, 0, wp00)
         open_sums(0, 0, 512, 0)
 
-        gather(1, 3, 0, 256)
-        gather(1, 3, 256, 512)
-        gather(1, 3, 512, 1024)
-        xg1_blocks01 = sbuf([P, PACK * 256], BF16, "xg1_blocks01")[:]
-        round_xg(1, 0, 256, xg1_blocks01)
+        gather(1, 3, 0, XG_FIRST)
+        gather(1, 3, XG_FIRST, 384)
+        gather(1, 3, 384, 1024)
+        xg1_blocks02 = sbuf([P, PACK * 384], BF16, "xg1_middle")[:]
+        round_xg(1, 0, XG_FIRST, xg1_blocks02[:, 0 : PACK * XG_FIRST])
         round_wp(wp01_rest_raw[:], WP_AHEAD, KP, wp01, nc.scalar.copy)
-        xg1_blocks23 = sbuf([P, PACK * 256], BF16, "xg1_blocks23")[:]
-        round_xg(1, 256, 512, xg1_blocks23)
+        round_xg(1, XG_FIRST, 384, xg1_blocks02[:, PACK * XG_FIRST :])
         wp10 = sbuf([P, PACK * KP], BF16, "tab_w")
         round_wp(wp10_raw[:], 0, KP, wp10, nc.scalar.copy)
-        quantize_xg(1, 0, 256, xg1_blocks01, "xg_w1_blocks01")
+        quantize_xg(1, 0, 128, xg1_blocks02[:, 0 : PACK * BLOCK], "xg_w1_block0")
         quantize_wp(0, 1, wp01)
-        close_sums(0, 0, 256)
-        quantize_xg(1, 256, 512, xg1_blocks23, "xg_w1_blocks23")
-        close_sums(0, 256, 512)
-        xg1_blocks45 = sbuf([P, PACK * 256], BF16, "xg1_blocks23")
-        round_xg(1, 512 + XG_ON_GPSIMD, 768, xg1_blocks45[:, PACK * XG_ON_GPSIMD :])
-        round_xg_on_gpsimd(1, 512, 512 + XG_ON_GPSIMD, xg1_blocks45[:, 0 : PACK * XG_ON_GPSIMD])
+        close_sums(0, 0, 128)
+        quantize_xg(1, 128, 384, xg1_blocks02[:, PACK * BLOCK :], "xg_w1_blocks12")
+        close_sums(0, 128, 384)
+        xg1_blocks34 = sbuf([P, PACK * 256], BF16, "xg1_middle")
+        round_xg_on_gpsimd(1, 384, 640, xg1_blocks34[:])
         wp11 = sbuf([P, PACK * KP], BF16, "wp_bf")
         round_wp(wp11_raw[:, :, 0:WP_LAST_ON_SCALAR], 0, WP_LAST_ON_SCALAR, wp11, nc.scalar.copy)
-        h0_blocks03 = sbuf([P, PACK * 512], BF16, "slot3")
-        multiply(0, 0, 512, h0_blocks03)
-        open_sums(0, 512, 1024, 0)
+        h0_blocks02 = sbuf([P, PACK * 384], BF16, "slot3")
+        multiply(0, 0, 384, h0_blocks02)
+        open_sums(0, 512, 896, 0)
+        quantize_xg(1, 384, 640, xg1_blocks34[:], "xg_w1_blocks34")
+        close_sums(0, 384, 640)
         quantize_wp(1, 0, wp10)
-        quantize_xg(1, 512, 768, xg1_blocks45[:], "xg_w1_blocks45")
-        round_wp(wp11_raw[:, :, WP_LAST_ON_SCALAR:KP], WP_LAST_ON_SCALAR, KP, wp11, nc.vector.tensor_copy)
-        close_sums(0, 512, 768)
         open_sums(1, 0, 512, 4)
+        round_wp(wp11_raw[:, :, WP_LAST_ON_SCALAR:KP], WP_LAST_ON_SCALAR, KP, wp11, nc.vector.tensor_copy)
         quantize_wp(1, 1, wp11)
         h_codes(0, 0, 512, "wp_bf")
-        quantize_h(0, 0, 512, h0_blocks03)
+        quantize_h(0, 0, 384, h0_blocks02)
 
-        late = sbuf([P, 3 * BANK], F32, "slot5")
-        sums4, sums5 = late[:, 0:BANK], late[:, BANK : 2 * BANK]
-        xg1_blocks67 = late[:, 2 * BANK : 3 * BANK].bitcast(BF16)
+        late = sbuf([P, 3 * BANK + BANK // 2], F32, "slot5")
+        sums3, sums4 = late[:, 0:BANK], late[:, BANK : 2 * BANK]
+        xg1_blocks57 = late[:, 2 * BANK :].bitcast(BF16)
+        copy_sums(0, 384, sums3)
+        open_sums(0, 896, 1024, 3)
         copy_sums(0, 512, sums4)
-        h0_block4 = sbuf([P, PACK * BLOCK], BF16, "slot3")
-        multiply_on_gpsimd(sums4, woven_gate[:, 0:BANK], h0_block4)
+        h0_block3 = sbuf([P, PACK * BLOCK], BF16, "slot3")
+        multiply_on_gpsimd(sums3, woven_gate[:, 0:BANK], h0_block3[:])
         close_sums(1, 0, 512)
-        h1_blocks01 = sbuf([P, PACK * 256], BF16, "slot4")
+        h1_blocks01 = h_tile(256)
         multiply(1, 0, 256, h1_blocks01)
         h1_blocks23 = h_tile(256)
         multiply(1, 256, 384, h1_blocks23)
         open_sums(1, 512, 640, 0)
         close_sums(1, 512, 640)
-        copy_sums(0, 640, sums5)
-        round_xg(1, 768, 1024, xg1_blocks67)
-        open_sums(1, 640, 768, 1)
-        close_sums(1, 640, 768)
+        round_xg(1, 640, 1024, xg1_blocks57)
         open_tower(0, 256, (4, 5))
-        quantize_xg(1, 768, 1024, xg1_blocks67, "xg_w1_blocks67")
+        open_sums(1, 640, 768, 6)
         quantize_h(1, 0, 256, h1_blocks01)
+        quantize_xg(1, 640, 1024, xg1_blocks57, "xg_w1_blocks57")
+        quantize_h(0, 384, 512, h0_block3)
+        close_sums(0, 640, 768)
+        close_sums(1, 640, 768)
         finish(0, 256)
 
-        h0_block5 = sbuf([P, PACK * BLOCK], BF16, "slot4")
-        multiply_on_gpsimd(sums5, woven_gate[:, BANK : 2 * BANK], h0_block5)
+        h0_blocks45 = sbuf([P, PACK * 256], BF16, "slot3")
+        multiply_on_gpsimd(sums4, woven_gate[:, BANK : 2 * BANK], h0_blocks45[:, 0 : PACK * BLOCK])
         multiply(1, 384, 512, h1_blocks23, at=BLOCK)
         h1_blocks45 = h_tile(256)
-        multiply(1, 512, 768, h1_blocks45)
+        multiply(1, 512, 640, h1_blocks45)
+        multiply(0, 640, 768, h0_blocks45, at=BLOCK)
+        multiply(1, 640, 768, h1_blocks45, at=BLOCK)
         close_sums(0, 768, 1024)
-        open_tower(256, 512, (6, 7))
-        open_sums(1, 768, 896, 0)
+        open_tower(256, 512, (7, 0))
+        open_sums(1, 768, 896, 1)
         close_sums(1, 768, 896)
         quantize_h(1, 256, 512, h1_blocks23)
         finish(256, 512)
-
-        h_codes(0, 512, 768, "h_w0_512")
-        quantize_h(0, 512, 640, h0_block4)
-        quantize_h(0, 640, 768, h0_block5)
+        quantize_h(0, 512, 768, h0_blocks45)
         quantize_h(1, 512, 768, h1_blocks45)
         open_tower(512, 768, (4, 5))
         finish(512, 768)
 
         h0_blocks67 = h_tile(256)
         multiply(0, 768, 1024, h0_blocks67)
-        open_sums(1, 896, 1024, 2)
+        open_sums(1, 896, 1024, 6)
         close_sums(1, 896, 1024)
         h1_block6 = h_tile(BLOCK)
         multiply(1, 768, 896, h1_block6)
         quantize_h(0, 768, 1024, h0_blocks67)
-        open_tower(768, 896, (1, 7))
+        open_tower(768, 896, (2, 3))
         h1_block7 = h_tile(BLOCK)
         multiply(1, 896, 1024, h1_block7)
         quantize_h(1, 768, 896, h1_block6)
         finish(768, 896)
-        open_tower(896, 1024, (3, 6, 4, 5))
+        open_tower(896, 1024, (7, 0, 1, 4))
         quantize_h(1, 896, 1024, h1_block7)
         finish_last(896, 1024)

@@ -349,15 +349,15 @@ def tile_list_interest_user_gate_kernel(
         close_sums(0, 0, 128)
         quantize_xg(1, 128, 384, xg1_blocks02[:, PACK * BLOCK :], "xg_w1_blocks12")
         close_sums(0, 128, 384)
-        xg1_blocks34 = sbuf([P, PACK * 256], BF16, "xg1_middle")
-        round_xg_on_gpsimd(1, 384, 640, xg1_blocks34[:])
+        xg1_block3 = sbuf([P, PACK * BLOCK], BF16, "xg1_middle")
+        round_xg_on_gpsimd(1, 384, 512, xg1_block3[:])
         wp11 = sbuf([P, PACK * KP], BF16, "wp_bf")
         round_wp(wp11_raw[:, :, 0:WP_LAST_ON_SCALAR], 0, WP_LAST_ON_SCALAR, wp11, nc.scalar.copy)
         h0_blocks02 = sbuf([P, PACK * 384], BF16, "slot3")
         multiply(0, 0, 384, h0_blocks02)
         open_sums(0, 512, 896, 0)
-        quantize_xg(1, 384, 640, xg1_blocks34[:], "xg_w1_blocks34")
-        close_sums(0, 384, 640)
+        quantize_xg(1, 384, 512, xg1_block3[:], "xg_w1_block3")
+        close_sums(0, 384, 512)
         quantize_wp(1, 0, wp10)
         open_sums(1, 0, 512, 4)
         round_wp(wp11_raw[:, :, WP_LAST_ON_SCALAR:KP], WP_LAST_ON_SCALAR, KP, wp11, nc.vector.tensor_copy)
@@ -365,22 +365,27 @@ def tile_list_interest_user_gate_kernel(
         h_codes(0, 0, 512, "wp_bf")
         quantize_h(0, 0, 384, h0_blocks02)
 
-        late = sbuf([P, 3 * BANK + BANK // 2], F32, "slot5")
+        late = sbuf([P, 4 * BANK + BANK // 2], F32, "slot5")
         sums3, sums4 = late[:, 0:BANK], late[:, BANK : 2 * BANK]
-        xg1_blocks57 = late[:, 2 * BANK :].bitcast(BF16)
+        h0_blocks45 = late[:, 2 * BANK : 3 * BANK].bitcast(BF16)
+        xg1_block4 = h0_block3 = h0_blocks45[:, 0 : PACK * BLOCK]
+        xg1_blocks57 = late[:, 3 * BANK :].bitcast(BF16)
+        round_xg(1, 512, 640, xg1_block4)
         copy_sums(0, 384, sums3)
-        open_sums(0, 896, 1024, 3)
-        copy_sums(0, 512, sums4)
-        h0_block3 = sbuf([P, PACK * BLOCK], BF16, "slot3")
-        multiply_on_gpsimd(sums3, woven_gate[:, 0:BANK], h0_block3[:])
-        close_sums(1, 0, 512)
+        quantize_xg(1, 512, 640, xg1_block4, "xg_w1_block4")
+        multiply_on_gpsimd(sums3, woven_gate[:, 0:BANK], h0_block3)
+        close_sums(1, 0, 256)
+        close_sums(0, 512, 640)
+        close_sums(1, 256, 512)
         h1_blocks01 = h_tile(256)
         multiply(1, 0, 256, h1_blocks01)
         h1_blocks23 = h_tile(256)
         multiply(1, 256, 384, h1_blocks23)
-        open_sums(1, 512, 640, 0)
-        close_sums(1, 512, 640)
         round_xg(1, 640, 1024, xg1_blocks57)
+        open_sums(1, 512, 640, 3)
+        close_sums(1, 512, 640)
+        copy_sums(0, 512, sums4)
+        open_sums(0, 896, 1024, 0)
         open_tower(0, 256, (4, 5))
         open_sums(1, 640, 768, 6)
         quantize_h(1, 0, 256, h1_blocks01)
@@ -390,7 +395,6 @@ def tile_list_interest_user_gate_kernel(
         close_sums(1, 640, 768)
         finish(0, 256)
 
-        h0_blocks45 = sbuf([P, PACK * 256], BF16, "slot3")
         multiply_on_gpsimd(sums4, woven_gate[:, BANK : 2 * BANK], h0_blocks45[:, 0 : PACK * BLOCK])
         multiply(1, 384, 512, h1_blocks23, at=BLOCK)
         h1_blocks45 = h_tile(256)
@@ -398,7 +402,7 @@ def tile_list_interest_user_gate_kernel(
         multiply(0, 640, 768, h0_blocks45, at=BLOCK)
         multiply(1, 640, 768, h1_blocks45, at=BLOCK)
         close_sums(0, 768, 1024)
-        open_tower(256, 512, (7, 0))
+        open_tower(256, 512, (7, 3))
         open_sums(1, 768, 896, 1)
         close_sums(1, 768, 896)
         quantize_h(1, 256, 512, h1_blocks23)
@@ -415,11 +419,11 @@ def tile_list_interest_user_gate_kernel(
         h1_block6 = h_tile(BLOCK)
         multiply(1, 768, 896, h1_block6)
         quantize_h(0, 768, 1024, h0_blocks67)
-        open_tower(768, 896, (2, 3))
+        open_tower(768, 896, (2, 0))
         h1_block7 = h_tile(BLOCK)
         multiply(1, 896, 1024, h1_block7)
         quantize_h(1, 768, 896, h1_block6)
         finish(768, 896)
-        open_tower(896, 1024, (7, 0, 1, 4))
+        open_tower(896, 1024, (7, 3, 1, 4))
         quantize_h(1, 896, 1024, h1_block7)
         finish_last(896, 1024)

@@ -367,8 +367,7 @@ def tile_list_interest_user_gate_kernel(
 
         late = sbuf([P, 4 * BANK + BANK // 2], F32, "slot5")
         sums3, sums4 = late[:, 0:BANK], late[:, BANK : 2 * BANK]
-        h0_blocks45 = late[:, 2 * BANK : 3 * BANK].bitcast(BF16)
-        xg1_block4 = h0_block3 = h0_blocks45[:, 0 : PACK * BLOCK]
+        xg1_block4 = h0_block3 = late[:, 2 * BANK : 2 * BANK + BANK // 2].bitcast(BF16)
         xg1_blocks57 = late[:, 3 * BANK :].bitcast(BF16)
         round_xg(1, 512, 640, xg1_block4)
         copy_sums(0, 384, sums3)
@@ -379,42 +378,43 @@ def tile_list_interest_user_gate_kernel(
         close_sums(1, 256, 512)
         h1_blocks01 = h_tile(256)
         multiply(1, 0, 256, h1_blocks01)
-        h1_blocks23 = h_tile(256)
-        multiply(1, 256, 384, h1_blocks23)
+        h1_blocks23 = sbuf([P, PACK * 256], BF16, "h_middle")
+        multiply(1, 256, 512, h1_blocks23)
         round_xg(1, 640, 1024, xg1_blocks57)
         open_sums(1, 512, 640, 3)
         close_sums(1, 512, 640)
         copy_sums(0, 512, sums4)
         open_sums(0, 896, 1024, 0)
         open_tower(0, 256, (4, 5))
-        open_sums(1, 640, 768, 6)
         quantize_h(1, 0, 256, h1_blocks01)
         quantize_xg(1, 640, 1024, xg1_blocks57, "xg_w1_blocks57")
         quantize_h(0, 384, 512, h0_block3)
-        close_sums(0, 640, 768)
-        close_sums(1, 640, 768)
         finish(0, 256)
+        close_sums(0, 640, 896)
+        open_tower(256, 512, (6, 7))
+        quantize_h(1, 256, 512, h1_blocks23)
+        finish(256, 512)
+        open_sums(1, 640, 768, 4)
+        close_sums(1, 640, 768)
 
+        h0_blocks45 = sbuf([P, PACK * 256], BF16, "h_middle")
         multiply_on_gpsimd(sums4, woven_gate[:, BANK : 2 * BANK], h0_blocks45[:, 0 : PACK * BLOCK])
-        multiply(1, 384, 512, h1_blocks23, at=BLOCK)
         h1_blocks45 = h_tile(256)
         multiply(1, 512, 640, h1_blocks45)
         multiply(0, 640, 768, h0_blocks45, at=BLOCK)
+        h0_blocks67 = h_tile(256)
+        multiply(0, 768, 896, h0_blocks67)
         multiply(1, 640, 768, h1_blocks45, at=BLOCK)
-        close_sums(0, 768, 1024)
-        open_tower(256, 512, (7, 3))
+        close_sums(0, 896, 1024)
         open_sums(1, 768, 896, 1)
         close_sums(1, 768, 896)
-        quantize_h(1, 256, 512, h1_blocks23)
-        finish(256, 512)
         quantize_h(0, 512, 768, h0_blocks45)
         quantize_h(1, 512, 768, h1_blocks45)
-        open_tower(512, 768, (4, 5))
+        open_tower(512, 768, (6, 7))
         finish(512, 768)
 
-        h0_blocks67 = h_tile(256)
-        multiply(0, 768, 1024, h0_blocks67)
-        open_sums(1, 896, 1024, 6)
+        multiply(0, 896, 1024, h0_blocks67, at=BLOCK)
+        open_sums(1, 896, 1024, 5)
         close_sums(1, 896, 1024)
         h1_block6 = h_tile(BLOCK)
         multiply(1, 768, 896, h1_block6)
@@ -424,6 +424,6 @@ def tile_list_interest_user_gate_kernel(
         multiply(1, 896, 1024, h1_block7)
         quantize_h(1, 768, 896, h1_block6)
         finish(768, 896)
-        open_tower(896, 1024, (7, 3, 1, 4))
+        open_tower(896, 1024, (3, 1, 4, 6))
         quantize_h(1, 896, 1024, h1_block7)
         finish_last(896, 1024)

@@ -118,8 +118,8 @@ def tile_list_interest_user_gate_kernel(
 
         def round_wp(raw, lo, hi, woven, copy):
             copy(
-                out=woven[:].rearrange("p (t m i) -> p m i t", t=PACK, i=PACK)[:, lo // PACK : hi // PACK],
-                in_=raw.rearrange("p i (m t) -> p m i t", t=PACK),
+                out=woven[:].rearrange("p (u t m i) -> p u m i t", u=2, t=2, i=PACK)[:, :, lo // PACK : hi // PACK],
+                in_=raw.rearrange("p i (m u t) -> p u m i t", u=2, t=2),
             )
 
         wp_w = {}
@@ -246,7 +246,10 @@ def tile_list_interest_user_gate_kernel(
                 tower_pass(1, lo, hi, m0 + 1, m0 + 2)
                 nc.vector.tensor_scalar_add(res[:, 0, :], tower[lo, m0][:, 0, :], bt_sb[:, m0 : m0 + 1])
                 add_bias_on_scalar(res[:, 1, :], tower[lo, m0 + 1][:, 0, :], m0 + 1)
-                nc.sync.dma_start(out=out_rows[:, m0 : m0 + 2, lo:hi], in_=res[:])
+                if m0 == 0:
+                    nc.sync.dma_start(out=out_rows[:, 0:2, lo:hi], in_=res[:])
+            nc.sync.dma_start(out=out_rows[:, 2, lo:hi], in_=res[:, 0, :])
+            nc.scalar.dma_start(out=out_rows[:, 3, lo:hi], in_=res[:, 1, :])
 
         nc.vector.memset(tab_s[:].bitcast(I32), 0)
         nc.gpsimd.memset(wg_s_raw[:].bitcast(I32), 0)
@@ -336,8 +339,7 @@ def tile_list_interest_user_gate_kernel(
         open_sums(0, 0, 512, 0)
 
         gather(1, 3, 0, XG_FIRST)
-        gather(1, 3, XG_FIRST, 384)
-        gather(1, 3, 384, 1024)
+        gather(1, 3, XG_FIRST, 1024)
         xg1_blocks02 = sbuf([P, PACK * 384], BF16, "xg1_middle")[:]
         round_xg(1, 0, XG_FIRST, xg1_blocks02[:, 0 : PACK * XG_FIRST])
         round_wp(wp01_rest_raw[:], WP_AHEAD, KP, wp01, nc.scalar.copy)
@@ -386,35 +388,35 @@ def tile_list_interest_user_gate_kernel(
         copy_sums(0, 512, sums4)
         open_sums(0, 896, 1024, 0)
         open_tower(0, 256, (4, 5))
+        open_sums(1, 640, 768, 6)
         quantize_h(1, 0, 256, h1_blocks01)
         quantize_xg(1, 640, 1024, xg1_blocks57, "xg_w1_blocks57")
         quantize_h(0, 384, 512, h0_block3)
         finish(0, 256)
-        close_sums(0, 640, 896)
-        open_tower(256, 512, (6, 7))
+        close_sums(0, 640, 768)
+        close_sums(1, 640, 768)
+        close_sums(0, 768, 896)
+        open_tower(256, 512, (7, 4))
         quantize_h(1, 256, 512, h1_blocks23)
         finish(256, 512)
-        open_sums(1, 640, 768, 4)
-        close_sums(1, 640, 768)
 
         h0_blocks45 = sbuf([P, PACK * 256], BF16, "h_middle")
         multiply_on_gpsimd(sums4, woven_gate[:, BANK : 2 * BANK], h0_blocks45[:, 0 : PACK * BLOCK])
         h1_blocks45 = h_tile(256)
         multiply(1, 512, 640, h1_blocks45)
         multiply(0, 640, 768, h0_blocks45, at=BLOCK)
-        h0_blocks67 = h_tile(256)
-        multiply(0, 768, 896, h0_blocks67)
         multiply(1, 640, 768, h1_blocks45, at=BLOCK)
         close_sums(0, 896, 1024)
         open_sums(1, 768, 896, 1)
         close_sums(1, 768, 896)
         quantize_h(0, 512, 768, h0_blocks45)
         quantize_h(1, 512, 768, h1_blocks45)
-        open_tower(512, 768, (6, 7))
+        open_tower(512, 768, (5, 7))
         finish(512, 768)
 
-        multiply(0, 896, 1024, h0_blocks67, at=BLOCK)
-        open_sums(1, 896, 1024, 5)
+        h0_blocks67 = h_tile(256)
+        multiply(0, 768, 1024, h0_blocks67)
+        open_sums(1, 896, 1024, 6)
         close_sums(1, 896, 1024)
         h1_block6 = h_tile(BLOCK)
         multiply(1, 768, 896, h1_block6)
@@ -424,6 +426,6 @@ def tile_list_interest_user_gate_kernel(
         multiply(1, 896, 1024, h1_block7)
         quantize_h(1, 768, 896, h1_block6)
         finish(768, 896)
-        open_tower(896, 1024, (3, 1, 4, 6))
+        open_tower(896, 1024, (3, 1, 4, 5))
         quantize_h(1, 896, 1024, h1_block7)
         finish_last(896, 1024)

@@ -31,7 +31,7 @@ RESULT_TILES = 8
 
 WP_AHEAD = 256
 XG_FIRST = 224
-WP_LAST_ON_SCALAR = 384
+WP_LAST_ON_SCALAR = 352
 
 
 def tile_list_interest_user_gate_kernel(
@@ -100,8 +100,8 @@ def tile_list_interest_user_gate_kernel(
 
         def round_xg_on_gpsimd(a, lo, hi, woven):
             nc.gpsimd.tensor_scalar(
-                woven.rearrange("p (c n i) -> p c i n", n=1, i=PACK),
-                picked[a][:, :, lo:hi].rearrange("p i (c n) -> p c i n", n=1),
+                woven.rearrange("p (c n i) -> p c i n", n=8, i=PACK),
+                picked[a][:, :, lo:hi].rearrange("p i (c n) -> p c i n", n=8),
                 1.0,
                 0.0,
                 MULT,
@@ -338,10 +338,12 @@ def tile_list_interest_user_gate_kernel(
         quantize_wp(0, 0, wp00)
         open_sums(0, 0, 512, 0)
 
-        gather(1, 3, 0, XG_FIRST)
-        gather(1, 3, XG_FIRST, 1024)
+        gather(1, 3, 0, BLOCK)
+        gather(1, 3, BLOCK, 2 * BLOCK)
+        gather(1, 3, 2 * BLOCK, 1024)
         xg1_blocks02 = sbuf([P, PACK * 384], BF16, "xg1_middle")[:]
-        round_xg(1, 0, XG_FIRST, xg1_blocks02[:, 0 : PACK * XG_FIRST])
+        round_xg(1, 0, BLOCK, xg1_blocks02[:, 0 : PACK * BLOCK])
+        round_xg(1, BLOCK, XG_FIRST, xg1_blocks02[:, PACK * BLOCK : PACK * XG_FIRST])
         round_wp(wp01_rest_raw[:], WP_AHEAD, KP, wp01, nc.scalar.copy)
         round_xg(1, XG_FIRST, 384, xg1_blocks02[:, PACK * XG_FIRST :])
         wp10 = sbuf([P, PACK * KP], BF16, "tab_w")
@@ -351,15 +353,15 @@ def tile_list_interest_user_gate_kernel(
         close_sums(0, 0, 128)
         quantize_xg(1, 128, 384, xg1_blocks02[:, PACK * BLOCK :], "xg_w1_blocks12")
         close_sums(0, 128, 384)
-        xg1_block3 = sbuf([P, PACK * BLOCK], BF16, "xg1_middle")
-        round_xg_on_gpsimd(1, 384, 512, xg1_block3[:])
+        xg1_blocks34 = sbuf([P, PACK * 256], BF16, "xg1_middle")
+        round_xg_on_gpsimd(1, 384, 640, xg1_blocks34[:])
         wp11 = sbuf([P, PACK * KP], BF16, "wp_bf")
         round_wp(wp11_raw[:, :, 0:WP_LAST_ON_SCALAR], 0, WP_LAST_ON_SCALAR, wp11, nc.scalar.copy)
         h0_blocks02 = sbuf([P, PACK * 384], BF16, "slot3")
         multiply(0, 0, 384, h0_blocks02)
         open_sums(0, 512, 896, 0)
-        quantize_xg(1, 384, 512, xg1_block3[:], "xg_w1_block3")
-        close_sums(0, 384, 512)
+        quantize_xg(1, 384, 640, xg1_blocks34[:], "xg_w1_blocks34")
+        close_sums(0, 384, 640)
         quantize_wp(1, 0, wp10)
         open_sums(1, 0, 512, 4)
         round_wp(wp11_raw[:, :, WP_LAST_ON_SCALAR:KP], WP_LAST_ON_SCALAR, KP, wp11, nc.vector.tensor_copy)
@@ -367,17 +369,15 @@ def tile_list_interest_user_gate_kernel(
         h_codes(0, 0, 512, "wp_bf")
         quantize_h(0, 0, 384, h0_blocks02)
 
-        late = sbuf([P, 4 * BANK + BANK // 2], F32, "slot5")
+        late = sbuf([P, 3 * BANK + BANK // 2], F32, "slot5")
         sums3, sums4 = late[:, 0:BANK], late[:, BANK : 2 * BANK]
-        xg1_block4 = h0_block3 = late[:, 2 * BANK : 2 * BANK + BANK // 2].bitcast(BF16)
-        xg1_blocks57 = late[:, 3 * BANK :].bitcast(BF16)
-        round_xg(1, 512, 640, xg1_block4)
+        xg1_blocks57 = late[:, 2 * BANK :].bitcast(BF16)
         copy_sums(0, 384, sums3)
-        quantize_xg(1, 512, 640, xg1_block4, "xg_w1_block4")
+        h0_block3 = sbuf([P, PACK * BLOCK], BF16, "slot3")[:]
         multiply_on_gpsimd(sums3, woven_gate[:, 0:BANK], h0_block3)
-        close_sums(1, 0, 256)
-        close_sums(0, 512, 640)
-        close_sums(1, 256, 512)
+        close_sums(1, 0, 512)
+        copy_sums(0, 512, sums4)
+        open_sums(0, 896, 1024, 0)
         h1_blocks01 = h_tile(256)
         multiply(1, 0, 256, h1_blocks01)
         h1_blocks23 = sbuf([P, PACK * 256], BF16, "h_middle")
@@ -385,8 +385,6 @@ def tile_list_interest_user_gate_kernel(
         round_xg(1, 640, 1024, xg1_blocks57)
         open_sums(1, 512, 640, 3)
         close_sums(1, 512, 640)
-        copy_sums(0, 512, sums4)
-        open_sums(0, 896, 1024, 0)
         open_tower(0, 256, (4, 5))
         open_sums(1, 640, 768, 6)
         quantize_h(1, 0, 256, h1_blocks01)
@@ -416,12 +414,12 @@ def tile_list_interest_user_gate_kernel(
 
         h0_blocks67 = h_tile(256)
         multiply(0, 768, 1024, h0_blocks67)
-        open_sums(1, 896, 1024, 6)
+        open_sums(1, 896, 1024, 2)
         close_sums(1, 896, 1024)
         h1_block6 = h_tile(BLOCK)
         multiply(1, 768, 896, h1_block6)
         quantize_h(0, 768, 1024, h0_blocks67)
-        open_tower(768, 896, (2, 0))
+        open_tower(768, 896, (6, 0))
         h1_block7 = h_tile(BLOCK)
         multiply(1, 896, 1024, h1_block7)
         quantize_h(1, 768, 896, h1_block6)

@@ -239,6 +239,18 @@ def tile_list_interest_user_gate_kernel(
                     add_bias_on_scalar(res[:, m - m0, :], tower[lo, m0][:, m - m0, :], m)
                 nc.sync.dma_start(out=out_rows[:, m0 : m0 + 2, lo:hi], in_=res[:])
 
+        def finish_early(lo, hi, banks):
+            for m0, bank in zip((0, 2), banks):
+                tower[lo, m0] = bank_tile([P, 2, hi - lo], bank)
+                tower_pass(0, lo, hi, m0, m0 + 2)
+                tower_pass(1, lo, hi, m0, m0 + 2)
+                res = result_tile(lo, hi)
+                for m in (m0, m0 + 1):
+                    add_bias_on_scalar(res[:, m - m0, :], tower[lo, m0][:, m - m0, :], m)
+                    if m0 == 0:
+                        nc.sync.dma_start(out=out_rows[:, m, lo:hi], in_=res[:, m, :])
+            nc.sync.dma_start(out=out_rows[:, 2:4, lo:hi], in_=res[:])
+
         def finish_last(lo, hi):
             for m0 in (0, 2):
                 res = result_tile(lo, hi)
@@ -409,21 +421,20 @@ def tile_list_interest_user_gate_kernel(
         close_sums(1, 768, 896)
         quantize_h(0, 512, 768, h0_blocks45)
         quantize_h(1, 512, 768, h1_blocks45)
-        open_tower(512, 768, (5, 7))
-        finish(512, 768)
+        finish_early(512, 768, (5, 7))
 
         h0_blocks67 = h_tile(256)
         multiply(0, 768, 1024, h0_blocks67)
         open_sums(1, 896, 1024, 2)
         close_sums(1, 896, 1024)
-        h1_block6 = h_tile(BLOCK)
+        h1_block6 = sbuf([P, PACK * BLOCK], BF16, "h_last")
         multiply(1, 768, 896, h1_block6)
         quantize_h(0, 768, 1024, h0_blocks67)
         open_tower(768, 896, (6, 0))
-        h1_block7 = h_tile(BLOCK)
-        multiply(1, 896, 1024, h1_block7)
         quantize_h(1, 768, 896, h1_block6)
-        finish(768, 896)
         open_tower(896, 1024, (3, 1, 4, 5))
+        h1_block7 = sbuf([P, PACK * BLOCK], BF16, "h_last")
+        multiply(1, 896, 1024, h1_block7)
+        finish(768, 896)
         quantize_h(1, 896, 1024, h1_block7)
         finish_last(896, 1024)

from contextlib import ExitStack

import concourse.mybir as mybir
from concourse.masks import make_identity

K, D, H, N, T, S = 1024, 512, 1024, 512, 2048, 1024
FLOPS = 2 * S * (K * H + D * H + H * N)

F32 = mybir.dt.float32
BF16 = mybir.dt.bfloat16
I32 = mybir.dt.int32
U32 = mybir.dt.uint32
U16 = mybir.dt.uint16
U8 = mybir.dt.uint8
FP8X4 = mybir.dt.float8_e4m3fn_x4
FP4X4 = mybir.dt.float4_e2m1fn_x4
MULT = mybir.AluOpType.mult
ADD = mybir.AluOpType.add
ACT = mybir.ActivationFunctionType

P = 128
PACK = 4
KP = P * PACK
BANK = 512
BLOCK = 128
LIST_ROWS = 16
HEADS = 8
ALIGN = 256
H_TILES = 4
RESULT_TILES = 8

WP_AHEAD = 256
XG_FIRST = 224
WP_LAST_ON_SCALAR = 352


def tile_list_interest_user_gate_kernel(
    tc, tab_words, tab_scales, offs, xT, wgt, offs2, wp, wg_words, wg_scales, bg, wt_words, wt_scales, bt, out
):
    nc = tc.nc
    with ExitStack() as ctx:
        lists = ctx.enter_context(tc.tile_pool(name="lists", bufs=1))
        keep = ctx.enter_context(tc.tile_pool(name="keep", bufs=1))
        stage = ctx.enter_context(tc.tile_pool(name="stage", bufs=1))
        psum = ctx.enter_context(tc.psum_pool(name="psum", bufs=1))

        def sbuf(shape, dtype, tag):
            return keep.tile(shape, dtype, name=tag, tag=tag, align_bytes=ALIGN)

        def bank_tile(shape, bank):
            return psum.tile(shape, F32, name="bank", tag="bank%d" % bank)

        users = lists.tile([P, S // LIST_ROWS], U16, name="users")
        clicks = lists.tile([P, S // LIST_ROWS], U16, name="clicks")

        tab_w = sbuf([P, T], U32, "tab_w")
        tab_s = sbuf([P, T], U8, "tab_s")
        v_w = sbuf([P, S], U32, "v_w")
        v_s = sbuf([P, S], U8, "v_s")
        wg_w_raw = sbuf([P, 2 * H], U8, "wg_w_raw")
        wg_s_raw = sbuf([P, H], U8, "wg_s_raw")
        wg_w = sbuf([P, 2 * H], U8, "wg_w")
        wg_s = sbuf([P, H], U8, "wg_s")
        wgt_sb = sbuf([P, S], F32, "wgt_sb")
        wgt_raw = sbuf([P, P], F32, "wgt_raw")
        ident = sbuf([P, P], F32, "ident")
        bg_sb = sbuf([P, 2, 2 * PACK], F32, "bg_sb")
        picked = [sbuf([P, PACK, S], F32, "picked%d" % a) for a in range(2)]
        gate = {(half, lo): sbuf([P, PACK, BANK], F32, "gate%d_%d" % (half, lo)) for half in range(2) for lo in (0, BANK)}
        xg_s = [sbuf([P, S], U8, "xg_s%d" % a) for a in range(2)]
        wp_s = [sbuf([P, H], U8, "wp_s%d" % a) for a in range(2)]
        h_s = [sbuf([P, S], U8, "h_s%d" % half) for half in range(2)]

        def load_scale_rows(dst, rows):
            for q in range(4):
                nc.sync.dma_start(out=dst[32 * q : 32 * q + 4].bitcast(I32), in_=rows[4 * q : 4 * q + 4].bitcast(I32))

        planes = {}

        def load_plane(a, i, slot):
            planes[a, i] = sbuf([P, T], F32, "slot%d" % slot)
            rows = xT[KP * a : KP * (a + 1), :].rearrange("(p i) c -> p i c", i=PACK)
            nc.sync.dma_start(out=planes[a, i][:], in_=rows[:, i, :])

        def load_wp(half, a, lo, hi, slot):
            raw = sbuf([P, PACK, hi - lo], F32, "slot%d" % slot)
            rows = wp[KP * a : KP * (a + 1), KP * half + lo : KP * half + hi].rearrange("(p i) c -> p i c", i=PACK)
            nc.sync.dma_start(out=raw[:], in_=rows)
            return raw

        def gather(a, i, lo, hi):
            offsets = clicks[:, lo // LIST_ROWS : hi // LIST_ROWS]
            nc.vector.tensor_tensor(picked[a][:, i, lo:hi], planes[a, i][:].indirect(offsets), wgt_sb[:, lo:hi], MULT)

        def round_xg(a, lo, hi, woven):
            nc.scalar.copy(
                out=woven.rearrange("p (c n i) -> p c i n", n=2, i=PACK),
                in_=picked[a][:, :, lo:hi].rearrange("p i (c n) -> p c i n", n=2),
            )

        def round_xg_on_gpsimd(a, lo, hi, woven):
            nc.gpsimd.tensor_scalar(
                woven.rearrange("p (c n i) -> p c i n", n=8, i=PACK),
                picked[a][:, :, lo:hi].rearrange("p i (c n) -> p c i n", n=8),
                1.0,
                0.0,
                MULT,
                ADD,
            )

        xg_w = {}

        def quantize_xg(a, lo, hi, woven, tag):
            codes = sbuf([P, hi - lo], U32, tag)[:]
            for j0 in range(lo, hi, BLOCK):
                xg_w[a, j0] = codes[:, j0 - lo : j0 - lo + BLOCK]
            nc.vector.quantize_mx(out=codes.bitcast(FP8X4), scales=xg_s[a][:, lo:hi], in_=woven)

        def round_wp(raw, lo, hi, woven, copy):
            copy(
                out=woven[:].rearrange("p (u t m i) -> p u m i t", u=2, t=2, i=PACK)[:, :, lo // PACK : hi // PACK],
                in_=raw.rearrange("p i (m u t) -> p u m i t", u=2, t=2),
            )

        wp_w = {}

        def quantize_wp(half, a, woven):
            wp_w[half, a] = sbuf([P, KP], U32, "wp_w%d%d" % (half, a))[:]
            nc.vector.quantize_mx(
                out=wp_w[half, a].bitcast(FP8X4), scales=wp_s[a][:, KP * half : KP * (half + 1)], in_=woven[:]
            )

        def make_gate(half, t, lo):
            pre = bank_tile([P, BANK], t + PACK * half)
            c0 = KP * half + P * t
            nc.tensor.matmul_mx(
                out=pre[:],
                lhsT=wg_w[:, 2 * c0 : 2 * (c0 + P)].bitcast(FP4X4),
                lhsT_scale=wg_s[:, c0 : c0 + P],
                rhs=v_w[:, lo : lo + BANK].bitcast(FP8X4),
                rhs_scale=v_s[:, lo : lo + BANK],
                start=True,
                stop=True,
            )
            nc.scalar.activation(out=gate[half, lo][:, t, :], in_=pre[:], func=ACT.Sigmoid, bias=bg_sb[:, half, t : t + 1])

        acc = {}

        def project(half, a, j0):
            for t in range(PACK):
                c0 = KP * half + P * t
                nc.tensor.matmul_mx(
                    out=acc[half, j0][:, t, :],
                    lhsT=wp_w[half, a][:, P * t : P * (t + 1)].bitcast(FP8X4),
                    lhsT_scale=wp_s[a][:, c0 : c0 + P],
                    rhs=xg_w[a, j0].bitcast(FP8X4),
                    rhs_scale=xg_s[a][:, j0 : j0 + BLOCK],
                    start=(a == 0 and t == 0),
                    stop=(a == 1 and t == PACK - 1),
                )

        def open_sums(half, lo, hi, first_bank):
            for j0 in range(lo, hi, BLOCK):
                acc[half, j0] = bank_tile([P, PACK, BLOCK], first_bank + (j0 - lo) // BLOCK)
                project(half, 0, j0)

        def close_sums(half, lo, hi):
            for j0 in range(lo, hi, BLOCK):
                project(half, 1, j0)

        def h_tile(requests):
            return stage.tile([P, PACK * requests], BF16, name="h_bf", tag="h_bf", bufs=H_TILES, align_bytes=ALIGN)

        def multiply(half, lo, hi, woven, at=0):
            for j0 in range(lo, hi, BLOCK):
                c0 = PACK * (at + j0 - lo)
                nc.vector.tensor_tensor(
                    woven[:, c0 : c0 + PACK * BLOCK].rearrange("p (c n t) -> p c t n", n=2, t=PACK),
                    acc[half, j0][:].rearrange("p t (c n) -> p c t n", n=2),
                    gate[half, j0 // BANK * BANK][:, :, j0 % BANK : j0 % BANK + BLOCK].rearrange("p t (c n) -> p c t n", n=2),
                    MULT,
                )

        def copy_sums(half, j0, woven):
            nc.scalar.copy(out=woven.rearrange("p (c t) -> p c t", t=PACK), in_=acc[half, j0][:].rearrange("p t c -> p c t"))

        def multiply_on_gpsimd(woven_sums, woven_gate, woven):
            nc.gpsimd.tensor_tensor(
                woven.rearrange("p (c t) -> p c t", t=PACK),
                woven_sums.rearrange("p (c t) -> p c t", t=PACK),
                woven_gate.rearrange("p (c t) -> p c t", t=PACK),
                MULT,
            )

        h_w = {}

        def h_codes(half, lo, hi, tag):
            codes = sbuf([P, hi - lo], U32, tag)
            for j0 in range(lo, hi, BLOCK):
                h_w[half, j0] = codes[:, j0 - lo :]

        def quantize_h(half, lo, hi, woven):
            if (half, lo) not in h_w:
                h_codes(half, lo, hi, "h_w%d_%d" % (half, lo))
            nc.vector.quantize_mx(out=h_w[half, lo][:, 0 : hi - lo].bitcast(FP8X4), scales=h_s[half][:, lo:hi], in_=woven[:])

        out_rows = out.rearrange("(m p) j -> p m j", p=P)
        tower = {}

        def tower_pass(half, lo, hi, m0, m1):
            for m in range(m0, m1):
                nc.tensor.matmul_mx(
                    out=tower[lo, m0][:, m - m0, :],
                    lhsT=wt_w[:, half, P * m : P * (m + 1)].bitcast(FP8X4),
                    lhsT_scale=wt_s[:, half, P * m : P * (m + 1)],
                    rhs=h_w[half, lo][:, 0 : hi - lo].bitcast(FP8X4),
                    rhs_scale=h_s[half][:, lo:hi],
                    start=(half == 0 and m == m0),
                    stop=(half == 1 and m == m1 - 1),
                )

        def open_tower(lo, hi, banks):
            share = PACK // len(banks)
            for n, bank in enumerate(banks):
                tower[lo, share * n] = bank_tile([P, share, hi - lo], bank)
                tower_pass(0, lo, hi, share * n, share * (n + 1))

        def result_tile(lo, hi):
            return stage.tile([P, 2, hi - lo], F32, name="res", tag="res", bufs=RESULT_TILES, align_bytes=ALIGN)

        def add_bias_on_scalar(dst, src, m):
            nc.scalar.activation(out=dst, in_=src, func=ACT.Identity, bias=bt_sb[:, m : m + 1])

        def finish(lo, hi):
            for m0 in (0, 2):
                tower_pass(1, lo, hi, m0, m0 + 2)
                res = result_tile(lo, hi)
                for m in (m0, m0 + 1):
                    add_bias_on_scalar(res[:, m - m0, :], tower[lo, m0][:, m - m0, :], m)
                nc.sync.dma_start(out=out_rows[:, m0 : m0 + 2, lo:hi], in_=res[:])

        def finish_early(lo, hi, banks):
            for m0, bank in zip((0, 2), banks):
                tower[lo, m0] = bank_tile([P, 2, hi - lo], bank)
                tower_pass(0, lo, hi, m0, m0 + 2)
                tower_pass(1, lo, hi, m0, m0 + 2)
                res = result_tile(lo, hi)
                for m in (m0, m0 + 1):
                    add_bias_on_scalar(res[:, m - m0, :], tower[lo, m0][:, m - m0, :], m)
                    if m0 == 0:
                        nc.sync.dma_start(out=out_rows[:, m, lo:hi], in_=res[:, m, :])
            nc.sync.dma_start(out=out_rows[:, 2:4, lo:hi], in_=res[:])

        def finish_last(lo, hi):
            for m0 in (0, 2):
                res = result_tile(lo, hi)
                tower_pass(1, lo, hi, m0, m0 + 1)
                tower_pass(1, lo, hi, m0 + 1, m0 + 2)
                nc.vector.tensor_scalar_add(res[:, 0, :], tower[lo, m0][:, 0, :], bt_sb[:, m0 : m0 + 1])
                add_bias_on_scalar(res[:, 1, :], tower[lo, m0 + 1][:, 0, :], m0 + 1)
                if m0 == 0:
                    nc.sync.dma_start(out=out_rows[:, 0:2, lo:hi], in_=res[:])
            nc.sync.dma_start(out=out_rows[:, 2, lo:hi], in_=res[:, 0, :])
            nc.scalar.dma_start(out=out_rows[:, 3, lo:hi], in_=res[:, 1, :])

        nc.vector.memset(tab_s[:].bitcast(I32), 0)
        nc.gpsimd.memset(wg_s_raw[:].bitcast(I32), 0)
        make_identity(nc, ident[:])
        nc.sync.dma_start(users[:], offs)
        nc.sync.dma_start(out=wg_w_raw[:].bitcast(I32), in_=wg_words[0].bitcast(I32))
        nc.sync.dma_start(out=wgt_raw[:], in_=wgt.rearrange("(u q) (b c) -> u (q b) c", q=8, c=P)[:, 0:64:9, :])
        load_scale_rows(tab_s, tab_scales[0])
        nc.sync.dma_start(out=tab_w[:].bitcast(I32), in_=tab_words[0].rearrange("p n t -> p (n t)").bitcast(I32))
        load_scale_rows(wg_s_raw, wg_scales[0])
        nc.sync.dma_start(clicks[:], offs2)
        nc.sync.dma_start(out=bg_sb[:, :, 0:PACK], in_=bg.rearrange("(h p t) -> p h t", h=2, t=PACK))
        for slot in range(2 * PACK - 1):
            load_plane(slot // PACK, slot % PACK, slot)
        wp00_raw = load_wp(0, 0, 0, KP, 0)
        wp01_ahead_raw = load_wp(0, 1, 0, WP_AHEAD, 1)
        load_plane(1, 3, 2)
        wp01_rest_raw = load_wp(0, 1, WP_AHEAD, KP, 3)
        wp10_raw = load_wp(1, 0, 0, KP, 4)
        wp11_raw = load_wp(1, 1, 0, KP, 5)
        wt_s = sbuf([P, 2, N], U8, "slot6")
        nc.gpsimd.memset(wt_s[:].bitcast(I32), 0)
        load_scale_rows(wt_s, wt_scales.rearrange("a r n -> r a n"))
        wt_w = sbuf([P, 2, N], U32, "slot0")
        nc.sync.dma_start(out=wt_w[:].bitcast(I32), in_=wt_words.rearrange("a p n t -> p a (n t)").bitcast(I32))
        bt_sb = sbuf([P, N // P], F32, "slot1")
        with nc.allow_non_contiguous_dma(reason="one bias value for each partition"):
            nc.sync.dma_start(out=bt_sb[:], in_=bt.rearrange("(m p) -> p m", p=P))

        turned = bank_tile([P, P], 0)
        nc.tensor.transpose(turned[:], wgt_raw[:], ident[:])
        for part in range(S // BANK):
            spread = stage.tile([P, PACK, P], F32, name="spread", tag="res", bufs=RESULT_TILES, align_bytes=ALIGN)
            nc.scalar.copy(
                out=spread[:].rearrange("p b (g u r) -> p b g u r", g=HEADS, r=2),
                in_=turned[:]
                .rearrange("p (g r b) -> p b g r", g=HEADS, r=2)[:, PACK * part : PACK * (part + 1)]
                .unsqueeze(3)
                .broadcast_to([P, PACK, HEADS, 8, 2]),
            )
            back = bank_tile([P, PACK, P], 1 + part)
            for b in range(PACK):
                nc.tensor.transpose(back[:, b, :], spread[:, b, :], ident[:])
            nc.scalar.copy(out=wgt_sb[:, BANK * part : BANK * (part + 1)], in_=back[:].rearrange("p b c -> p (b c)"))

        nc.vector.tensor_copy(
            out=wg_w[:].bitcast(U16).rearrange("p (h t m) -> p h t m", h=2, t=PACK),
            in_=wg_w_raw[:].bitcast(U16).rearrange("p (h m t) -> p h t m", h=2, t=PACK),
        )
        nc.vector.tensor_copy(v_s[:], tab_s[:].indirect(users[:]))
        for lo in range(0, S, BANK):
            nc.vector.tensor_copy(v_w[:, lo : lo + BANK], tab_w[:].indirect(users[:, lo // LIST_ROWS : (lo + BANK) // LIST_ROWS]))
        for half in range(2):
            nc.gpsimd.tensor_copy(
                out=wg_s[:, KP * half : KP * (half + 1)].rearrange("p (t m) -> p t m", t=PACK),
                in_=wg_s_raw[:, KP * half : KP * (half + 1)].rearrange("p (m t) -> p t m", t=PACK),
            )
        for lo in range(0, S, BANK):
            for half in range(2):
                for t in range(PACK):
                    make_gate(half, t, lo)

        for i in range(PACK - 1):
            gather(0, i, 0, S)
        gather(0, 3, 0, 512)
        gather(0, 3, 512, 1024)
        xg0_front = sbuf([P, PACK * 512], BF16, "xg0_front")[:]
        round_xg(0, 0, 512, xg0_front)
        xg0_back = sbuf([P, PACK * 512], BF16, "xg0_back")[:]
        round_xg(0, 512, 1024, xg0_back)
        gather(1, 0, 0, S)
        gather(1, 1, 0, S)
        quantize_xg(0, 0, 512, xg0_front, "xg_w0_front")
        woven_gate = sbuf([P, 2 * BANK], F32, "xg0_front")
        for n, j0 in enumerate((384, 512)):
            nc.scalar.copy(
                out=woven_gate[:, BANK * n : BANK * (n + 1)].rearrange("p (c n t) -> p c t n", n=2, t=PACK),
                in_=gate[0, j0 // BANK * BANK][:, :, j0 % BANK : j0 % BANK + BLOCK].rearrange("p t (c n) -> p c t n", n=2),
            )
        wp00 = sbuf([P, PACK * KP], BF16, "wp_bf")
        round_wp(wp00_raw[:], 0, KP, wp00, nc.scalar.copy)
        wp01 = sbuf([P, PACK * KP], BF16, "picked0")
        round_wp(wp01_ahead_raw[:], 0, WP_AHEAD, wp01, nc.scalar.copy)
        quantize_xg(0, 512, 1024, xg0_back, "xg_w0_back")
        gather(1, 2, 0, S)
        quantize_wp(0, 0, wp00)
        open_sums(0, 0, 512, 0)

        gather(1, 3, 0, BLOCK)
        gather(1, 3, BLOCK, 2 * BLOCK)
        gather(1, 3, 2 * BLOCK, 1024)
        xg1_blocks02 = sbuf([P, PACK * 384], BF16, "xg1_middle")[:]
        round_xg(1, 0, BLOCK, xg1_blocks02[:, 0 : PACK * BLOCK])
        round_xg(1, BLOCK, XG_FIRST, xg1_blocks02[:, PACK * BLOCK : PACK * XG_FIRST])
        round_wp(wp01_rest_raw[:], WP_AHEAD, KP, wp01, nc.scalar.copy)
        round_xg(1, XG_FIRST, 384, xg1_blocks02[:, PACK * XG_FIRST :])
        wp10 = sbuf([P, PACK * KP], BF16, "tab_w")
        round_wp(wp10_raw[:], 0, KP, wp10, nc.scalar.copy)
        quantize_xg(1, 0, 128, xg1_blocks02[:, 0 : PACK * BLOCK], "xg_w1_block0")
        quantize_wp(0, 1, wp01)
        close_sums(0, 0, 128)
        quantize_xg(1, 128, 384, xg1_blocks02[:, PACK * BLOCK :], "xg_w1_blocks12")
        close_sums(0, 128, 384)
        xg1_blocks34 = sbuf([P, PACK * 256], BF16, "xg1_middle")
        round_xg_on_gpsimd(1, 384, 640, xg1_blocks34[:])
        wp11 = sbuf([P, PACK * KP], BF16, "wp_bf")
        round_wp(wp11_raw[:, :, 0:WP_LAST_ON_SCALAR], 0, WP_LAST_ON_SCALAR, wp11, nc.scalar.copy)
        h0_blocks02 = sbuf([P, PACK * 384], BF16, "slot3")
        multiply(0, 0, 384, h0_blocks02)
        open_sums(0, 512, 896, 0)
        quantize_xg(1, 384, 640, xg1_blocks34[:], "xg_w1_blocks34")
        close_sums(0, 384, 640)
        quantize_wp(1, 0, wp10)
        open_sums(1, 0, 512, 4)
        round_wp(wp11_raw[:, :, WP_LAST_ON_SCALAR:KP], WP_LAST_ON_SCALAR, KP, wp11, nc.vector.tensor_copy)
        quantize_wp(1, 1, wp11)
        h_codes(0, 0, 512, "wp_bf")
        quantize_h(0, 0, 384, h0_blocks02)

        late = sbuf([P, 3 * BANK + BANK // 2], F32, "slot5")
        sums3, sums4 = late[:, 0:BANK], late[:, BANK : 2 * BANK]
        xg1_blocks57 = late[:, 2 * BANK :].bitcast(BF16)
        copy_sums(0, 384, sums3)
        h0_block3 = sbuf([P, PACK * BLOCK], BF16, "slot3")[:]
        multiply_on_gpsimd(sums3, woven_gate[:, 0:BANK], h0_block3)
        close_sums(1, 0, 512)
        copy_sums(0, 512, sums4)
        open_sums(0, 896, 1024, 0)
        h1_blocks01 = h_tile(256)
        multiply(1, 0, 256, h1_blocks01)
        h1_blocks23 = sbuf([P, PACK * 256], BF16, "h_middle")
        multiply(1, 256, 512, h1_blocks23)
        round_xg(1, 640, 1024, xg1_blocks57)
        open_sums(1, 512, 640, 3)
        close_sums(1, 512, 640)
        open_tower(0, 256, (4, 5))
        open_sums(1, 640, 768, 6)
        quantize_h(1, 0, 256, h1_blocks01)
        quantize_xg(1, 640, 1024, xg1_blocks57, "xg_w1_blocks57")
        quantize_h(0, 384, 512, h0_block3)
        finish(0, 256)
        close_sums(0, 640, 768)
        close_sums(1, 640, 768)
        close_sums(0, 768, 896)
        open_tower(256, 512, (7, 4))
        quantize_h(1, 256, 512, h1_blocks23)
        finish(256, 512)

        h0_blocks45 = sbuf([P, PACK * 256], BF16, "h_middle")
        multiply_on_gpsimd(sums4, woven_gate[:, BANK : 2 * BANK], h0_blocks45[:, 0 : PACK * BLOCK])
        h1_blocks45 = h_tile(256)
        multiply(1, 512, 640, h1_blocks45)
        multiply(0, 640, 768, h0_blocks45, at=BLOCK)
        multiply(1, 640, 768, h1_blocks45, at=BLOCK)
        close_sums(0, 896, 1024)
        open_sums(1, 768, 896, 1)
        close_sums(1, 768, 896)
        quantize_h(0, 512, 768, h0_blocks45)
        quantize_h(1, 512, 768, h1_blocks45)
        finish_early(512, 768, (5, 7))

        h0_blocks67 = h_tile(256)
        multiply(0, 768, 1024, h0_blocks67)
        open_sums(1, 896, 1024, 2)
        close_sums(1, 896, 1024)
        h1_block6 = sbuf([P, PACK * BLOCK], BF16, "h_last")
        multiply(1, 768, 896, h1_block6)
        quantize_h(0, 768, 1024, h0_blocks67)
        open_tower(768, 896, (6, 0))
        quantize_h(1, 768, 896, h1_block6)
        open_tower(896, 1024, (3, 1, 4, 5))
        h1_block7 = sbuf([P, PACK * BLOCK], BF16, "h_last")
        multiply(1, 896, 1024, h1_block7)
        finish(768, 896)
        quantize_h(1, 896, 1024, h1_block7)
        finish_last(896, 1024)
